import numpy as np
import ml_dtypes


def mxq(x, axis, fmt="e4m3"):
    dtype, down = {"e4m3": (ml_dtypes.float8_e4m3fn, 7), "e5m2": (ml_dtypes.float8_e5m2, 14)}[fmt]
    v = np.moveaxis(np.asarray(x, np.float32).astype(ml_dtypes.bfloat16).astype(np.float64), axis, -1)
    blocks = v.reshape(v.shape[:-1] + (-1, 32))
    amax = np.abs(blocks).max(-1, keepdims=True)
    byte = np.maximum(np.where(amax > 0, np.frexp(amax)[1] - 1 + 127, 0) - down, 1)
    scale = np.exp2(byte - 127.0)
    codes = (blocks / scale).astype(np.float32).astype(dtype).astype(np.float64)
    return np.moveaxis((codes * scale).reshape(v.shape), -1, axis)


WIDE = False


def mx_kscale(k):
    if not WIDE:
        return np.ones(k)
    levels = np.array([10, -10, 5, -5, 0])
    if k % 512:
        return np.exp2(np.random.permutation(np.resize(levels, k // 32))).repeat(32)
    a = np.empty((k // 512, 16))
    for p in range(k // 512):
        a[p, :8] = np.random.permutation(np.resize(levels, 8))
        for g in range(8):
            far = levels[np.abs(levels - a[p, g]) >= 10]
            a[p, g + 8] = far[np.random.randint(len(far))]
    return np.exp2(a.ravel()).repeat(32)


def f64(x):
    return np.asarray(x).astype(np.float64)


def striped(idx):
    return np.tile(idx.reshape(-1, 16).T, (8, 1)).astype(np.uint16)


def unstriped(offs):
    return offs[:16].T.reshape(-1).astype(np.int64)


E2M1 = np.array([0.0, 0.5, 1.0, 1.5, 2.0, 3.0, 4.0, 6.0, -0.0, -0.5, -1.0, -1.5, -2.0, -3.0, -4.0, -6.0])


def pack_weight(w, fmt):
    k, n = w.shape
    w = f64(np.asarray(w, np.float32).astype(ml_dtypes.bfloat16)).reshape(k // 32, 32, n)
    amax = np.abs(w).max(1)
    if fmt == "e4m3":
        byte = np.frexp(amax)[1] - 1 + 127 - 7
    else:
        mant, ex = np.frexp(amax / 6.0)
        byte = np.where(mant > 0.5, ex, ex - 1) + 127
    byte = np.clip(np.where(amax > 0, byte, 1), 1, 254)
    scaled = (w * np.exp2(127.0 - byte)[:, None, :]).reshape(k, n).astype(np.float32)
    by_word = np.ascontiguousarray(scaled.reshape(k // 512, 128, 4, n).transpose(0, 1, 3, 2))
    if fmt == "e4m3":
        words = by_word.astype(ml_dtypes.float8_e4m3fn).view(np.uint8)
    else:
        c = by_word.astype(ml_dtypes.float4_e2m1fn).view(np.uint8) & 0xF
        words = (c[..., 0::2] | (c[..., 1::2] << 4)).reshape(k // 512, 128, 2 * n)
    return np.ascontiguousarray(words), np.ascontiguousarray(byte.astype(np.uint8).reshape(k // 512, 16, n))


def unpack_weight(words, scales, fmt):
    g, _, n = scales.shape
    words = np.ascontiguousarray(words).reshape(g, 128, n, -1)
    if fmt == "e4m3":
        vals = words.view(ml_dtypes.float8_e4m3fn).astype(np.float64)
    else:
        nib = np.empty((g, 128, n, 4), np.uint8)
        nib[..., 0::2] = words & 0xF
        nib[..., 1::2] = words >> 4
        vals = E2M1[nib]
    vals = vals * np.repeat(np.exp2(scales.astype(np.float64) - 127.0), 8, axis=1)[..., None]
    return vals.transpose(0, 1, 3, 2).reshape(g * 512, n)


def gelu(v):
    return 0.5 * v * (1.0 + np.tanh(np.sqrt(2.0 / np.pi) * (v + 0.044715 * v**3)))


def striped8(idx):
    return np.concatenate([v.reshape(-1, 16).T for v in idx]).astype(np.uint16)


def unstriped8(offs):
    return np.stack([offs[16 * g:16 * g + 16].T.reshape(-1) for g in range(8)]).astype(np.int64)


def heads(h, wgt, idx8):
    r = np.arange(h.shape[0])
    return wgt[r // 4 % 128] * h[r[:, None], idx8[r % 512 // 64]]


T, S, P, K, H, N = 4096, 2048, 1024, 512, 1024, 512

def setup_inputs():
    n = np.random.standard_normal
    s = mx_kscale(K)[:, None]
    u = mx_kscale(H)[:, None]
    tab_words, tab_scales = pack_weight(n((K, T)) * s, "e4m3")
    w2_words, w2_scales = pack_weight(2.0 * n((H, N)) / np.sqrt(H) / u, "e2m1")
    return {
        "tab_words": tab_words, "tab_scales": tab_scales,
        "offs": striped(np.random.permutation(T)[:S]),
        "w1": (1.5 * n((K, H)) / np.sqrt(K) / s).astype(np.float32),
        "offs2": striped8(np.stack([np.random.permutation(S)[:P] for _ in range(8)])),
        "wgt": np.repeat(np.random.uniform(0.5, 2.0, (8, P)), 16, axis=0).astype(np.float32),
        "gain": (n(H) * u[:, 0]).astype(np.float32),
        "w2_words": w2_words, "w2_scales": w2_scales,
        "sil": np.random.uniform(0.0, 1.0, (N, P)).astype(np.float32),
        "w3": (2.0 * n((H, N)) / np.sqrt(H) / u).astype(np.float32),
    }

def reference(tab_words, tab_scales, offs, w1, offs2, wgt, gain, w2_words, w2_scales, sil, w3):
    v = unpack_weight(tab_words, tab_scales, "e4m3")[:, unstriped(offs)]
    h = mxq(f64(w1), 0, "e4m3").T @ v
    x = heads(h, f64(wgt), unstriped8(offs2))
    z = f64(gain)[:, None] / (1.0 + np.exp(-x))
    zq = mxq(z, 0, "e4m3")
    w2 = unpack_weight(w2_words, w2_scales, "e2m1")
    speech = w2.T @ zq
    carry = mxq(f64(w3), 0, "e4m3").T @ zq
    return speech * (1.0 - f64(sil)) + carry

@@ -1,0 +1,214 @@
+from contextlib import ExitStack
+
+import concourse.mybir as mybir
+
+T, S, E, K, H, N = 4096, 2048, 1024, 512, 1024, 512
+FLOPS = 2 * K * H * S + 2 * 2 * H * N * E
+
+F32 = mybir.dt.float32
+BF16 = mybir.dt.bfloat16
+I32 = mybir.dt.int32
+U32 = mybir.dt.uint32
+U16 = mybir.dt.uint16
+U8 = mybir.dt.uint8
+FP8X4 = mybir.dt.float8_e4m3fn_x4
+FP4X4 = mybir.dt.float4_e2m1fn_x4
+ALU = mybir.AluOpType
+ACT = mybir.ActivationFunctionType
+
+P = 128
+PACK = 4
+BANK = 512
+PASSES = H // (P * PACK)
+HALVES = E // BANK
+CHUNK = 256
+LIST = 16
+
+
+def tile_list_overlap_track_logits_kernel(tc, tab_words, tab_scales, offs, w1, offs2, wgt, gain, w2_words, w2_scales, sil, w3, out):
+    nc = tc.nc
+    with ExitStack() as ctx:
+        keep = ctx.enter_context(tc.tile_pool(name="keep", bufs=1))
+        ring = ctx.enter_context(tc.tile_pool(name="ring", bufs=2))
+        ring3 = ctx.enter_context(tc.tile_pool(name="ring3", bufs=3))
+        shared = ctx.enter_context(tc.tile_pool(name="shared", bufs=1))
+        psum = ctx.enter_context(tc.psum_pool(name="psum", bufs=1))
+
+        frames = keep.tile([P, S // LIST], U16, name="frames")
+        picks = keep.tile([P, E // LIST], U16, name="picks")
+        table = keep.tile([P, T], U32, name="table")
+        table_sc = keep.tile([P, T], U8, name="table_sc")
+        w2_codes = keep.tile([P, PASSES, 2 * N], U8, name="w2_codes", align_bytes=64)
+        w2_sc = keep.tile([P, PASSES, N], U8, name="w2_sc", align_bytes=64)
+        wgt_sb = keep.tile([P, E], F32, name="wgt_sb")
+        gain_sb = keep.tile([P, PASSES, PACK], F32, name="gain_sb")
+        banks = [psum.tile([P, BANK], F32, name="bank%d" % k) for k in range(8)]
+
+        nc.vector.memset(table_sc[:].bitcast(I32), 0)
+        nc.vector.memset(w2_sc[:].rearrange("p a c -> p (a c)").bitcast(I32), 0)
+
+        nc.sync.dma_start(frames[:], offs)
+        nc.sync.dma_start(picks[:], offs2)
+        nc.sync.dma_start(gain_sb[:], gain.rearrange("(b p t) -> p b t", b=PASSES, t=PACK))
+        for q in range(4):
+            nc.sync.dma_start(table_sc[32 * q : 32 * q + 4, :].bitcast(I32), tab_scales[0, 4 * q : 4 * q + 4, :].bitcast(I32))
+        nc.sync.dma_start(table[:].bitcast(I32), tab_words[0].rearrange("p t i -> p (t i)").bitcast(I32))
+        w1_rows = w1.rearrange("(p j) c -> p j c", j=PACK)
+        w1_first = []
+        for u in range(2):
+            raw = keep.tile([P, PACK, 256], F32, name="w1_first%d" % u)
+            nc.sync.dma_start(raw[:], w1_rows[:, :, 256 * u : 256 * (u + 1)])
+            w1_first.append(raw)
+        w1_second = keep.tile([P, PACK, BANK], F32, name="w1_second")
+        nc.sync.dma_start(w1_second[:], w1_rows[:, :, BANK : 2 * BANK])
+        nc.sync.dma_start(wgt_sb[:], wgt)
+        w3_raw = []
+        for b in range(PASSES):
+            raw = keep.tile([P, PACK, N], F32, name="w3_raw%d" % b)
+            nc.sync.dma_start(raw[:], w3[BANK * b : BANK * (b + 1), :].rearrange("(p j) c -> p j c", j=PACK))
+            w3_raw.append(raw)
+        for q in range(4):
+            nc.sync.dma_start(w2_sc[32 * q : 32 * q + 4, :, :].bitcast(I32), w2_scales[:, 4 * q : 4 * q + 4, :].rearrange("a r c -> r a c").bitcast(I32))
+        nc.sync.dma_start(w2_codes[:].bitcast(I32), w2_words.rearrange("a p c -> p a c").bitcast(I32))
+        sil_sb = []
+        for n in range(N // P):
+            rows = keep.tile([P, E], F32, name="sil%d" % n)
+            nc.sync.dma_start(rows[:], sil[P * n : P * (n + 1), :])
+            sil_sb.append(rows)
+
+        v_sc = keep.tile([P, S], U8, name="v_sc", align_bytes=64)
+        nc.vector.tensor_copy(v_sc[:], table_sc[:].indirect(frames[:]))
+        v_codes = []
+
+        def gather_words(j):
+            if j == S // BANK - 1:
+                words = shared.tile([P, BANK], U32, name="v_last", align_bytes=64, offset=0)
+            else:
+                words = keep.tile([P, BANK], U32, name="v_codes%d" % j, align_bytes=64)
+            nc.vector.tensor_copy(words[:], table[:].indirect(frames[:, j * BANK // LIST : (j + 1) * BANK // LIST]))
+            v_codes.append(words)
+
+        def quantize(grouped, name):
+            codes = keep.tile([P, BANK], U32, name=name + "_codes", align_bytes=64)
+            scales = keep.tile([P, BANK], U8, name=name + "_sc", align_bytes=64)
+            nc.vector.quantize_mx(out=codes[:].bitcast(FP8X4), scales=scales[:], in_=grouped[:])
+            return codes, scales
+
+        w1_bf = shared.tile([P, PACK * BANK], BF16, name="w1_bf", align_bytes=64, offset=0)
+        w1_view = w1_bf[:].rearrange("p (t m j) -> p m j t", t=PACK, j=PACK)
+        for u in range(2):
+            nc.scalar.copy(w1_view[:, 64 * u : 64 * (u + 1), :, :], w1_first[u][:].rearrange("p j (m t) -> p m j t", t=PACK))
+        w1_q = [quantize(w1_bf, "w1a")]
+        for j in range(S // BANK):
+            gather_words(j)
+        w1_bf = shared.tile([P, PACK * BANK], BF16, name="w1_bf2", align_bytes=64, offset=4 * BANK)
+        nc.vector.tensor_copy(w1_bf[:].rearrange("p (t m j) -> p m j t", t=PACK, j=PACK), w1_second[:].rearrange("p j (m t) -> p m j t", t=PACK))
+        w1_q.append(quantize(w1_bf, "w1b"))
+
+        h = [[keep.tile([P, S], F32, name="h%d_%d" % (b, t), tag="h%d_%d" % (b, t)) for t in range(PACK)] for b in range(PASSES)]
+
+        def first_product(b, t):
+            codes, scales = w1_q[b]
+            for j in range(S // BANK):
+                bank = banks[(PACK * t + j) % 8]
+                nc.tensor.matmul_mx(
+                    out=bank[:],
+                    lhsT=codes[:, P * t : P * (t + 1)].bitcast(FP8X4),
+                    lhsT_scale=scales[:, P * t : P * (t + 1)],
+                    rhs=v_codes[j][:].bitcast(FP8X4),
+                    rhs_scale=v_sc[:, BANK * j : BANK * (j + 1)],
+                    start=True,
+                    stop=True,
+                )
+                nc.scalar.copy(h[b][t][:, BANK * j : BANK * (j + 1)], bank[:])
+
+        x = [[keep.tile([P, PACK, BANK], F32, name="x%d_%d" % (b, u)) for u in range(HALVES)] for b in range(PASSES)]
+
+        def pick(b, t, u):
+            nc.vector.tensor_tensor(
+                x[b][u][:, t, :],
+                h[b][t][:].indirect(picks[:, u * BANK // LIST : (u + 1) * BANK // LIST]),
+                wgt_sb[:, BANK * u : BANK * (u + 1)],
+                ALU.mult,
+            )
+
+        z_q = {}
+
+        def gate(b, u):
+            z_bf = ring.tile([P, PACK * BANK], BF16, name="z_bf", align_bytes=64)
+            sig_all = keep.tile([P, PACK * BANK], F32, name="sig%d_%d" % (b, u), tag="h0_%d" % (HALVES * b + u))
+            for c in range(BANK // CHUNK):
+                sig = sig_all[:, PACK * CHUNK * c : PACK * CHUNK * (c + 1)]
+                nc.scalar.activation(
+                    sig.rearrange("p (c i t) -> p c t i", i=4, t=PACK),
+                    x[b][u][:, :, CHUNK * c : CHUNK * (c + 1)].rearrange("p t (c i) -> p c t i", i=4),
+                    ACT.Sigmoid,
+                )
+                nc.vector.tensor_tensor(
+                    z_bf[:, PACK * CHUNK * c : PACK * CHUNK * (c + 1)].rearrange("p (m t) -> p m t", t=PACK),
+                    sig.rearrange("p (m t) -> p m t", t=PACK),
+                    gain_sb[:, b : b + 1, :].to_broadcast([P, CHUNK, PACK]),
+                    ALU.mult,
+                )
+            z_q[b, u] = quantize(z_bf, "z%d_%d" % (b, u))
+
+        w3_q = []
+
+        def cast_w3(b, copy):
+            w3_bf = ring.tile([P, PACK * BANK], BF16, name="w_bf", align_bytes=64)
+            copy(
+                w3_bf[:].rearrange("p (c i j) -> p c j i", i=4, j=PACK),
+                w3_raw[b][:].rearrange("p j (c i) -> p c j i", i=4),
+            )
+            w3_q.append(quantize(w3_bf, "w3_%d" % b))
+
+        def second_products(u):
+            steps = [(b, n) for b in range(PASSES) for n in range(N // P)]
+            if u == 1:
+                steps = [(b, n) for n in range(N // P) for b in range(PASSES)]
+            for b, n in steps:
+                codes, scales = z_q[b, u]
+                if True:
+                    nc.tensor.matmul_mx(
+                        out=banks[2 * n][:],
+                        lhsT=w2_codes[:, b, 2 * P * n : 2 * P * (n + 1)].bitcast(FP4X4),
+                        lhsT_scale=w2_sc[:, b, P * n : P * (n + 1)],
+                        rhs=codes[:].bitcast(FP8X4),
+                        rhs_scale=scales[:],
+                        start=(b == 0),
+                        stop=(b == PASSES - 1),
+                    )
+                    nc.tensor.matmul_mx(
+                        out=banks[2 * n + 1][:],
+                        lhsT=w3_q[b][0][:, P * n : P * (n + 1)].bitcast(FP8X4),
+                        lhsT_scale=w3_q[b][1][:, P * n : P * (n + 1)],
+                        rhs=codes[:].bitcast(FP8X4),
+                        rhs_scale=scales[:],
+                        start=(b == 0),
+                        stop=(b == PASSES - 1),
+                    )
+
+        def finish(u):
+            cols = slice(BANK * u, BANK * (u + 1))
+            for pair in range(2):
+                for n in (2 * pair, 2 * pair + 1):
+                    nc.vector.scalar_tensor_tensor(sil_sb[n][:, cols], sil_sb[n][:, cols], 1.0, banks[2 * n][:], ALU.subtract, ALU.mult)
+                for n in (2 * pair, 2 * pair + 1):
+                    nc.vector.tensor_tensor(sil_sb[n][:, cols], banks[2 * n + 1][:], sil_sb[n][:, cols], ALU.subtract)
+                    nc.sync.dma_start(out[P * n : P * (n + 1), cols], sil_sb[n][:, cols])
+
+        for b in range(PASSES):
+            for t in range(PACK):
+                first_product(b, t)
+                for u in range(HALVES):
+                    pick(b, t, u)
+        gate(0, 0)
+        gate(0, 1)
+        cast_w3(0, nc.scalar.copy)
+        cast_w3(1, nc.scalar.copy)
+        gate(1, 0)
+        gate(1, 1)
+        second_products(0)
+        finish(0)
+        second_products(1)
+        finish(1)

@@ -21,8 +21,9 @@ PACK = 4
 BANK = 512
 PASSES = H // (P * PACK)
 HALVES = E // BANK
-CHUNK = 256
+CHUNK = 512
 LIST = 16
+ON_GPSIMD = 4
 
 
 def tile_list_overlap_track_logits_kernel(tc, tab_words, tab_scales, offs, w1, offs2, wgt, gain, w2_words, w2_scales, sil, w3, out):
@@ -30,8 +31,7 @@ def tile_list_overlap_track_logits_kernel(tc, tab_words, tab_scales, offs, w1, o
     with ExitStack() as ctx:
         keep = ctx.enter_context(tc.tile_pool(name="keep", bufs=1))
         ring = ctx.enter_context(tc.tile_pool(name="ring", bufs=2))
-        ring3 = ctx.enter_context(tc.tile_pool(name="ring3", bufs=3))
-        shared = ctx.enter_context(tc.tile_pool(name="shared", bufs=1))
+        ring3 = ctx.enter_context(tc.tile_pool(name="ring3", bufs=4))
         psum = ctx.enter_context(tc.psum_pool(name="psum", bufs=1))
 
         frames = keep.tile([P, S // LIST], U16, name="frames")
@@ -48,17 +48,15 @@ def tile_list_overlap_track_logits_kernel(tc, tab_words, tab_scales, offs, w1, o
         nc.vector.memset(w2_sc[:].rearrange("p a c -> p (a c)").bitcast(I32), 0)
 
         nc.sync.dma_start(frames[:], offs)
-        nc.sync.dma_start(picks[:], offs2)
+        w1_rows = w1.rearrange("(p j) c -> p j c", j=PACK)
+        w1_first = [keep.tile([P, PACK, 256], F32, name="w1_first%d" % u) for u in range(2)]
+        nc.sync.dma_start(w1_first[0][:], w1_rows[:, :, 0:256])
         nc.sync.dma_start(gain_sb[:], gain.rearrange("(b p t) -> p b t", b=PASSES, t=PACK))
         for q in range(4):
             nc.sync.dma_start(table_sc[32 * q : 32 * q + 4, :].bitcast(I32), tab_scales[0, 4 * q : 4 * q + 4, :].bitcast(I32))
+        nc.sync.dma_start(w1_first[1][:], w1_rows[:, :, 256:512])
         nc.sync.dma_start(table[:].bitcast(I32), tab_words[0].rearrange("p t i -> p (t i)").bitcast(I32))
-        w1_rows = w1.rearrange("(p j) c -> p j c", j=PACK)
-        w1_first = []
-        for u in range(2):
-            raw = keep.tile([P, PACK, 256], F32, name="w1_first%d" % u)
-            nc.sync.dma_start(raw[:], w1_rows[:, :, 256 * u : 256 * (u + 1)])
-            w1_first.append(raw)
+        nc.sync.dma_start(picks[:], offs2)
         w1_second = keep.tile([P, PACK, BANK], F32, name="w1_second")
         nc.sync.dma_start(w1_second[:], w1_rows[:, :, BANK : 2 * BANK])
         nc.sync.dma_start(wgt_sb[:], wgt)
@@ -76,15 +74,14 @@ def tile_list_overlap_track_logits_kernel(tc, tab_words, tab_scales, offs, w1, o
             nc.sync.dma_start(rows[:], sil[P * n : P * (n + 1), :])
             sil_sb.append(rows)
 
+        warm = keep.tile([P, 1], F32, name="warm")
+        nc.scalar.activation(warm[:], gain_sb[:, 0, 0:1], ACT.Sigmoid)
         v_sc = keep.tile([P, S], U8, name="v_sc", align_bytes=64)
         nc.vector.tensor_copy(v_sc[:], table_sc[:].indirect(frames[:]))
         v_codes = []
 
         def gather_words(j):
-            if j == S // BANK - 1:
-                words = shared.tile([P, BANK], U32, name="v_last", align_bytes=64, offset=0)
-            else:
-                words = keep.tile([P, BANK], U32, name="v_codes%d" % j, align_bytes=64)
+            words = keep.tile([P, BANK], U32, name="v_codes%d" % j, align_bytes=64)
             nc.vector.tensor_copy(words[:], table[:].indirect(frames[:, j * BANK // LIST : (j + 1) * BANK // LIST]))
             v_codes.append(words)
 
@@ -94,23 +91,26 @@ def tile_list_overlap_track_logits_kernel(tc, tab_words, tab_scales, offs, w1, o
             nc.vector.quantize_mx(out=codes[:].bitcast(FP8X4), scales=scales[:], in_=grouped[:])
             return codes, scales
 
-        w1_bf = shared.tile([P, PACK * BANK], BF16, name="w1_bf", align_bytes=64, offset=0)
+        w1_bf = ring.tile([P, PACK * BANK], BF16, name="w_bf", align_bytes=64)
         w1_view = w1_bf[:].rearrange("p (t m j) -> p m j t", t=PACK, j=PACK)
         for u in range(2):
             nc.scalar.copy(w1_view[:, 64 * u : 64 * (u + 1), :, :], w1_first[u][:].rearrange("p j (m t) -> p m j t", t=PACK))
         w1_q = [quantize(w1_bf, "w1a")]
         for j in range(S // BANK):
             gather_words(j)
-        w1_bf = shared.tile([P, PACK * BANK], BF16, name="w1_bf2", align_bytes=64, offset=4 * BANK)
+        w1_bf = ring.tile([P, PACK * BANK], BF16, name="w_bf", align_bytes=64)
         nc.vector.tensor_copy(w1_bf[:].rearrange("p (t m j) -> p m j t", t=PACK, j=PACK), w1_second[:].rearrange("p j (m t) -> p m j t", t=PACK))
         w1_q.append(quantize(w1_bf, "w1b"))
 
         h = [[keep.tile([P, S], F32, name="h%d_%d" % (b, t), tag="h%d_%d" % (b, t)) for t in range(PACK)] for b in range(PASSES)]
 
-        def first_product(b, t):
+        turn = []
+
+        def first_product(b, t, j):
             codes, scales = w1_q[b]
-            for j in range(S // BANK):
-                bank = banks[(PACK * t + j) % 8]
+            if True:
+                bank = banks[len(turn) % 8]
+                turn.append(j)
                 nc.tensor.matmul_mx(
                     out=bank[:],
                     lhsT=codes[:, P * t : P * (t + 1)].bitcast(FP8X4),
@@ -122,26 +122,21 @@ def tile_list_overlap_track_logits_kernel(tc, tab_words, tab_scales, offs, w1, o
                 )
                 nc.scalar.copy(h[b][t][:, BANK * j : BANK * (j + 1)], bank[:])
 
-        x = [[keep.tile([P, PACK, BANK], F32, name="x%d_%d" % (b, u)) for u in range(HALVES)] for b in range(PASSES)]
+        x = [keep.tile([P, PACK, E], F32, name="x%d" % b) for b in range(PASSES)]
 
-        def pick(b, t, u):
-            nc.vector.tensor_tensor(
-                x[b][u][:, t, :],
-                h[b][t][:].indirect(picks[:, u * BANK // LIST : (u + 1) * BANK // LIST]),
-                wgt_sb[:, BANK * u : BANK * (u + 1)],
-                ALU.mult,
-            )
+        def pick(b, t):
+            nc.vector.tensor_tensor(x[b][:, t, :], h[b][t][:].indirect(picks[:]), wgt_sb[:], ALU.mult)
 
         z_q = {}
 
         def gate(b, u):
-            z_bf = ring.tile([P, PACK * BANK], BF16, name="z_bf", align_bytes=64)
+            z_bf = keep.tile([P, PACK * BANK], BF16, name="z_bf%d_%d" % (b, u), tag="z_bf%d" % (u * (1 - b)), align_bytes=64)
             sig_all = keep.tile([P, PACK * BANK], F32, name="sig%d_%d" % (b, u), tag="h0_%d" % (HALVES * b + u))
             for c in range(BANK // CHUNK):
                 sig = sig_all[:, PACK * CHUNK * c : PACK * CHUNK * (c + 1)]
                 nc.scalar.activation(
                     sig.rearrange("p (c i t) -> p c t i", i=4, t=PACK),
-                    x[b][u][:, :, CHUNK * c : CHUNK * (c + 1)].rearrange("p t (c i) -> p c t i", i=4),
+                    x[b][:, :, BANK * u + CHUNK * c : BANK * u + CHUNK * (c + 1)].rearrange("p t (c i) -> p c t i", i=4),
                     ACT.Sigmoid,
                 )
                 nc.vector.tensor_tensor(
@@ -162,15 +157,18 @@ def tile_list_overlap_track_logits_kernel(tc, tab_words, tab_scales, offs, w1, o
             )
             w3_q.append(quantize(w3_bf, "w3_%d" % b))
 
+        speech_bank = [[banks[0], banks[2], banks[4], banks[6]], [banks[1], banks[5], banks[0], banks[4]]]
+        carry_bank = [[banks[1], banks[3], banks[5], banks[7]], [banks[3], banks[7], banks[2], banks[6]]]
+
         def second_products(u):
             steps = [(b, n) for b in range(PASSES) for n in range(N // P)]
             if u == 1:
-                steps = [(b, n) for n in range(N // P) for b in range(PASSES)]
+                steps = [(0, 0), (0, 1), (1, 0), (1, 1), (0, 2), (1, 2), (0, 3), (1, 3)]
             for b, n in steps:
                 codes, scales = z_q[b, u]
                 if True:
                     nc.tensor.matmul_mx(
-                        out=banks[2 * n][:],
+                        out=speech_bank[u][n][:],
                         lhsT=w2_codes[:, b, 2 * P * n : 2 * P * (n + 1)].bitcast(FP4X4),
                         lhsT_scale=w2_sc[:, b, P * n : P * (n + 1)],
                         rhs=codes[:].bitcast(FP8X4),
@@ -179,7 +177,7 @@ def tile_list_overlap_track_logits_kernel(tc, tab_words, tab_scales, offs, w1, o
                         stop=(b == PASSES - 1),
                     )
                     nc.tensor.matmul_mx(
-                        out=banks[2 * n + 1][:],
+                        out=carry_bank[u][n][:],
                         lhsT=w3_q[b][0][:, P * n : P * (n + 1)].bitcast(FP8X4),
                         lhsT_scale=w3_q[b][1][:, P * n : P * (n + 1)],
                         rhs=codes[:].bitcast(FP8X4),
@@ -192,16 +190,25 @@ def tile_list_overlap_track_logits_kernel(tc, tab_words, tab_scales, offs, w1, o
             cols = slice(BANK * u, BANK * (u + 1))
             for pair in range(2):
                 for n in (2 * pair, 2 * pair + 1):
-                    nc.vector.scalar_tensor_tensor(sil_sb[n][:, cols], sil_sb[n][:, cols], 1.0, banks[2 * n][:], ALU.subtract, ALU.mult)
+                    nc.vector.scalar_tensor_tensor(sil_sb[n][:, cols], sil_sb[n][:, cols], 1.0, speech_bank[u][n][:], ALU.subtract, ALU.mult)
                 for n in (2 * pair, 2 * pair + 1):
-                    nc.vector.tensor_tensor(sil_sb[n][:, cols], banks[2 * n + 1][:], sil_sb[n][:, cols], ALU.subtract)
+                    if 4 * u + n < ON_GPSIMD:
+                        carry = ring3.tile([P, BANK], F32, name="carry")
+                        nc.scalar.copy(carry[:], carry_bank[u][n][:])
+                        nc.gpsimd.tensor_tensor(sil_sb[n][:, cols], carry[:], sil_sb[n][:, cols], ALU.subtract)
+                    else:
+                        nc.vector.tensor_tensor(sil_sb[n][:, cols], carry_bank[u][n][:], sil_sb[n][:, cols], ALU.subtract)
                     nc.sync.dma_start(out[P * n : P * (n + 1), cols], sil_sb[n][:, cols])
 
+        for j in range(S // BANK):
+            for t in range(2):
+                first_product(0, t, j)
         for b in range(PASSES):
             for t in range(PACK):
-                first_product(b, t)
-                for u in range(HALVES):
-                    pick(b, t, u)
+                if PACK * b + t >= 2:
+                    for j in range(S // BANK):
+                        first_product(b, t, j)
+                pick(b, t)
         gate(0, 0)
         gate(0, 1)
         cast_w3(0, nc.scalar.copy)

@@ -32,6 +32,7 @@ def tile_list_overlap_track_logits_kernel(tc, tab_words, tab_scales, offs, w1, o
         keep = ctx.enter_context(tc.tile_pool(name="keep", bufs=1))
         ring = ctx.enter_context(tc.tile_pool(name="ring", bufs=2))
         ring3 = ctx.enter_context(tc.tile_pool(name="ring3", bufs=4))
+        shared = ctx.enter_context(tc.tile_pool(name="shared", bufs=1))
         psum = ctx.enter_context(tc.psum_pool(name="psum", bufs=1))
 
         frames = keep.tile([P, S // LIST], U16, name="frames")
@@ -130,7 +131,7 @@ def tile_list_overlap_track_logits_kernel(tc, tab_words, tab_scales, offs, w1, o
         z_q = {}
 
         def gate(b, u):
-            z_bf = keep.tile([P, PACK * BANK], BF16, name="z_bf%d_%d" % (b, u), tag="z_bf%d" % (u * (1 - b)), align_bytes=64)
+            z_bf = keep.tile([P, PACK * BANK], BF16, name="z_bf%d_%d" % (b, u), tag="z_bf%d" % (1 if (b, u) == (1, 0) else 0), align_bytes=64)
             sig_all = keep.tile([P, PACK * BANK], F32, name="sig%d_%d" % (b, u), tag="h0_%d" % (HALVES * b + u))
             for c in range(BANK // CHUNK):
                 sig = sig_all[:, PACK * CHUNK * c : PACK * CHUNK * (c + 1)]
@@ -145,6 +146,20 @@ def tile_list_overlap_track_logits_kernel(tc, tab_words, tab_scales, offs, w1, o
                     gain_sb[:, b : b + 1, :].to_broadcast([P, CHUNK, PACK]),
                     ALU.mult,
                 )
+            z_q[b, u] = quantize(z_bf, "z%d_%d" % (b, u))
+
+        def gate_on_scalar(b, u):
+            sig = keep.tile([P, PACK, BANK], F32, name="sig_planes", tag="h0_%d" % (HALVES * b + u))
+            nc.scalar.activation(sig[:], x[b][:, :, BANK * u : BANK * (u + 1)], ACT.Sigmoid)
+            planes = keep.tile([P, PACK, BANK], BF16, name="z_planes")
+            for t in range(PACK):
+                nc.scalar.activation(planes[:, t, :], sig[:, t, :], ACT.Copy, scale=gain_sb[:, b, t : t + 1])
+            z_wide = shared.tile([P, 2 * PACK * BANK], BF16, name="z_last", align_bytes=64, offset=0)
+            z_bf = z_wide[:, 0 : PACK * BANK]
+            nc.vector.tensor_copy(
+                z_bf.rearrange("p (c i t) -> p c t i", i=4, t=PACK),
+                planes[:].rearrange("p t (c i) -> p c t i", i=4),
+            )
             z_q[b, u] = quantize(z_bf, "z%d_%d" % (b, u))
 
         w3_q = []
@@ -186,19 +201,22 @@ def tile_list_overlap_track_logits_kernel(tc, tab_words, tab_scales, offs, w1, o
                         stop=(b == PASSES - 1),
                     )
 
-        def finish(u):
-            cols = slice(BANK * u, BANK * (u + 1))
-            for pair in range(2):
-                for n in (2 * pair, 2 * pair + 1):
-                    nc.vector.scalar_tensor_tensor(sil_sb[n][:, cols], sil_sb[n][:, cols], 1.0, speech_bank[u][n][:], ALU.subtract, ALU.mult)
-                for n in (2 * pair, 2 * pair + 1):
-                    if 4 * u + n < ON_GPSIMD:
-                        carry = ring3.tile([P, BANK], F32, name="carry")
-                        nc.scalar.copy(carry[:], carry_bank[u][n][:])
-                        nc.gpsimd.tensor_tensor(sil_sb[n][:, cols], carry[:], sil_sb[n][:, cols], ALU.subtract)
-                    else:
-                        nc.vector.tensor_tensor(sil_sb[n][:, cols], carry_bank[u][n][:], sil_sb[n][:, cols], ALU.subtract)
-                    nc.sync.dma_start(out[P * n : P * (n + 1), cols], sil_sb[n][:, cols])
+        def dampen(u, n):
+            part = sil_sb[n][:, BANK * u : BANK * (u + 1)]
+            nc.vector.scalar_tensor_tensor(part, part, 1.0, speech_bank[u][n][:], ALU.subtract, ALU.mult)
+
+        def add_on_vector(u, n, queue):
+            part = sil_sb[n][:, BANK * u : BANK * (u + 1)]
+            nc.vector.tensor_tensor(part, carry_bank[u][n][:], part, ALU.subtract)
+            queue.dma_start(out[P * n : P * (n + 1), BANK * u : BANK * (u + 1)], part)
+
+        def add_on_gpsimd(u, n):
+            part = sil_sb[n][:, BANK * u : BANK * (u + 1)]
+            carry = ring3.tile([P, BANK], F32, name="carry")
+            nc.scalar.copy(carry[:], carry_bank[u][n][:])
+            result = shared.tile([P, BANK], F32, name="result%d" % n, align_bytes=64, offset=4 * BANK * n)
+            nc.gpsimd.tensor_tensor(result[:], carry[:], part, ALU.subtract)
+            nc.sync.dma_start(out[P * n : P * (n + 1), BANK * u : BANK * (u + 1)], result[:])
 
         for j in range(S // BANK):
             for t in range(2):
@@ -209,13 +227,22 @@ def tile_list_overlap_track_logits_kernel(tc, tab_words, tab_scales, offs, w1, o
                     for j in range(S // BANK):
                         first_product(b, t, j)
                 pick(b, t)
-        gate(0, 0)
-        gate(0, 1)
         cast_w3(0, nc.scalar.copy)
+        gate(0, 0)
         cast_w3(1, nc.scalar.copy)
         gate(1, 0)
-        gate(1, 1)
+        gate(0, 1)
+        gate_on_scalar(1, 1)
         second_products(0)
-        finish(0)
+        for n in range(4):
+            dampen(0, n)
+            add_on_gpsimd(0, n)
         second_products(1)
-        finish(1)
+        dampen(1, 0)
+        dampen(1, 1)
+        add_on_vector(1, 0, nc.scalar)
+        add_on_vector(1, 1, nc.scalar)
+        dampen(1, 2)
+        dampen(1, 3)
+        add_on_vector(1, 2, nc.scalar)
+        add_on_vector(1, 3, nc.scalar)

@@ -33,52 +33,34 @@ def tile_list_overlap_track_logits_kernel(tc, tab_words, tab_scales, offs, w1, o
         ring = ctx.enter_context(tc.tile_pool(name="ring", bufs=2))
         ring3 = ctx.enter_context(tc.tile_pool(name="ring3", bufs=4))
         shared = ctx.enter_context(tc.tile_pool(name="shared", bufs=1))
+        early = ctx.enter_context(tc.tile_pool(name="early", bufs=1))
         psum = ctx.enter_context(tc.psum_pool(name="psum", bufs=1))
 
         frames = keep.tile([P, S // LIST], U16, name="frames")
         picks = keep.tile([P, E // LIST], U16, name="picks")
-        table = keep.tile([P, T], U32, name="table")
-        table_sc = keep.tile([P, T], U8, name="table_sc")
-        w2_codes = keep.tile([P, PASSES, 2 * N], U8, name="w2_codes", align_bytes=64)
-        w2_sc = keep.tile([P, PASSES, N], U8, name="w2_sc", align_bytes=64)
-        wgt_sb = keep.tile([P, E], F32, name="wgt_sb")
+        table = early.tile([P, T], U32, name="table", offset=0)
+        table_sc = early.tile([P, T], U8, name="table_sc", offset=24 * 1024)
         gain_sb = keep.tile([P, PASSES, PACK], F32, name="gain_sb")
         banks = [psum.tile([P, BANK], F32, name="bank%d" % k) for k in range(8)]
 
         nc.vector.memset(table_sc[:].bitcast(I32), 0)
-        nc.vector.memset(w2_sc[:].rearrange("p a c -> p (a c)").bitcast(I32), 0)
 
         nc.sync.dma_start(frames[:], offs)
         w1_rows = w1.rearrange("(p j) c -> p j c", j=PACK)
         w1_first = [keep.tile([P, PACK, 256], F32, name="w1_first%d" % u) for u in range(2)]
         nc.sync.dma_start(w1_first[0][:], w1_rows[:, :, 0:256])
         nc.sync.dma_start(gain_sb[:], gain.rearrange("(b p t) -> p b t", b=PASSES, t=PACK))
-        for q in range(4):
-            nc.sync.dma_start(table_sc[32 * q : 32 * q + 4, :].bitcast(I32), tab_scales[0, 4 * q : 4 * q + 4, :].bitcast(I32))
+        nc.sync.dma_start(table_sc[0:P:8, :].bitcast(I32), tab_scales[0].bitcast(I32))
         nc.sync.dma_start(w1_first[1][:], w1_rows[:, :, 256:512])
         nc.sync.dma_start(table[:].bitcast(I32), tab_words[0].rearrange("p t i -> p (t i)").bitcast(I32))
         nc.sync.dma_start(picks[:], offs2)
-        w1_second = keep.tile([P, PACK, BANK], F32, name="w1_second")
-        nc.sync.dma_start(w1_second[:], w1_rows[:, :, BANK : 2 * BANK])
-        nc.sync.dma_start(wgt_sb[:], wgt)
-        w3_raw = []
-        for b in range(PASSES):
-            raw = keep.tile([P, PACK, N], F32, name="w3_raw%d" % b)
-            nc.sync.dma_start(raw[:], w3[BANK * b : BANK * (b + 1), :].rearrange("(p j) c -> p j c", j=PACK))
-            w3_raw.append(raw)
-        for q in range(4):
-            nc.sync.dma_start(w2_sc[32 * q : 32 * q + 4, :, :].bitcast(I32), w2_scales[:, 4 * q : 4 * q + 4, :].rearrange("a r c -> r a c").bitcast(I32))
-        nc.sync.dma_start(w2_codes[:].bitcast(I32), w2_words.rearrange("a p c -> p a c").bitcast(I32))
-        sil_sb = []
-        for n in range(N // P):
-            rows = keep.tile([P, E], F32, name="sil%d" % n)
-            nc.sync.dma_start(rows[:], sil[P * n : P * (n + 1), :])
-            sil_sb.append(rows)
 
         warm = keep.tile([P, 1], F32, name="warm")
         nc.scalar.activation(warm[:], gain_sb[:, 0, 0:1], ACT.Sigmoid)
         v_sc = keep.tile([P, S], U8, name="v_sc", align_bytes=64)
-        nc.vector.tensor_copy(v_sc[:], table_sc[:].indirect(frames[:]))
+        picked_sc = early.tile([P, S], U8, name="picked_sc", offset=30 * 1024)
+        nc.vector.memset(v_sc[:].bitcast(I32), 0)
+        nc.vector.tensor_copy(picked_sc[:], table_sc[:].indirect(frames[:]))
         v_codes = []
 
         def gather_words(j):
@@ -92,16 +74,42 @@ def tile_list_overlap_track_logits_kernel(tc, tab_words, tab_scales, offs, w1, o
             nc.vector.quantize_mx(out=codes[:].bitcast(FP8X4), scales=scales[:], in_=grouped[:])
             return codes, scales
 
-        w1_bf = ring.tile([P, PACK * BANK], BF16, name="w_bf", align_bytes=64)
+        w1_bf = early.tile([P, PACK * BANK], BF16, name="w1_bf", align_bytes=64, offset=32 * 1024)
         w1_view = w1_bf[:].rearrange("p (t m j) -> p m j t", t=PACK, j=PACK)
         for u in range(2):
             nc.scalar.copy(w1_view[:, 64 * u : 64 * (u + 1), :, :], w1_first[u][:].rearrange("p j (m t) -> p m j t", t=PACK))
+        for q in range(4):
+            nc.sync.dma_start(v_sc[32 * q : 32 * q + 4, :].bitcast(I32), picked_sc[32 * q : 32 * q + 32 : 8, :].bitcast(I32))
+        w1_second = early.tile([P, PACK, BANK], F32, name="w1_second", offset=16 * 1024 + 64)
+        nc.sync.dma_start(w1_second[:], w1_rows[:, :, BANK : 2 * BANK])
+        wgt_sb = early.tile([P, E], F32, name="wgt_sb", offset=24 * 1024 + 64)
+        nc.sync.dma_start(wgt_sb[:], wgt)
         w1_q = [quantize(w1_bf, "w1a")]
+        w2_sc = early.tile([P, PASSES, N], U8, name="w2_sc", align_bytes=64, offset=32 * 1024)
+        nc.vector.memset(w2_sc[:].rearrange("p a c -> p (a c)").bitcast(I32), 0)
+        for q in range(4):
+            nc.sync.dma_start(w2_sc[32 * q : 32 * q + 4, :, :].bitcast(I32), w2_scales[:, 4 * q : 4 * q + 4, :].rearrange("a r c -> r a c").bitcast(I32))
+        w2_codes = early.tile([P, PASSES, 2 * N], U8, name="w2_codes", align_bytes=64, offset=30 * 1024)
+        nc.sync.dma_start(w2_codes[:].bitcast(I32), w2_words.rearrange("a p c -> p a c").bitcast(I32))
         for j in range(S // BANK):
             gather_words(j)
         w1_bf = ring.tile([P, PACK * BANK], BF16, name="w_bf", align_bytes=64)
         nc.vector.tensor_copy(w1_bf[:].rearrange("p (t m j) -> p m j t", t=PACK, j=PACK), w1_second[:].rearrange("p j (m t) -> p m j t", t=PACK))
         w1_q.append(quantize(w1_bf, "w1b"))
+        w3_raw = []
+        for b in range(PASSES):
+            raw = early.tile([P, PACK, N], F32, name="w3_raw%d" % b, offset=8 * 1024 * b)
+            nc.sync.dma_start(raw[:], w3[BANK * b : BANK * (b + 1), :].rearrange("(p j) c -> p j c", j=PACK))
+            w3_raw.append(raw)
+        sil_sb = []
+
+        def load_sil(n):
+            rows = early.tile([P, E], F32, name="sil%d" % n, offset=[16 * 1024 + 64, 20 * 1024 + 64, 0, 4 * 1024][n])
+            nc.sync.dma_start(rows[:], sil[P * n : P * (n + 1), :])
+            sil_sb.append(rows)
+
+        load_sil(0)
+        load_sil(1)
 
         h = [[keep.tile([P, S], F32, name="h%d_%d" % (b, t), tag="h%d_%d" % (b, t)) for t in range(PACK)] for b in range(PASSES)]
 
@@ -131,34 +139,18 @@ def tile_list_overlap_track_logits_kernel(tc, tab_words, tab_scales, offs, w1, o
         z_q = {}
 
         def gate(b, u):
-            z_bf = keep.tile([P, PACK * BANK], BF16, name="z_bf%d_%d" % (b, u), tag="z_bf%d" % (1 if (b, u) == (1, 0) else 0), align_bytes=64)
-            sig_all = keep.tile([P, PACK * BANK], F32, name="sig%d_%d" % (b, u), tag="h0_%d" % (HALVES * b + u))
-            for c in range(BANK // CHUNK):
-                sig = sig_all[:, PACK * CHUNK * c : PACK * CHUNK * (c + 1)]
-                nc.scalar.activation(
-                    sig.rearrange("p (c i t) -> p c t i", i=4, t=PACK),
-                    x[b][:, :, BANK * u + CHUNK * c : BANK * u + CHUNK * (c + 1)].rearrange("p t (c i) -> p c t i", i=4),
-                    ACT.Sigmoid,
-                )
-                nc.vector.tensor_tensor(
-                    z_bf[:, PACK * CHUNK * c : PACK * CHUNK * (c + 1)].rearrange("p (m t) -> p m t", t=PACK),
-                    sig.rearrange("p (m t) -> p m t", t=PACK),
-                    gain_sb[:, b : b + 1, :].to_broadcast([P, CHUNK, PACK]),
-                    ALU.mult,
-                )
-            z_q[b, u] = quantize(z_bf, "z%d_%d" % (b, u))
-
-        def gate_on_scalar(b, u):
-            sig = keep.tile([P, PACK, BANK], F32, name="sig_planes", tag="h0_%d" % (HALVES * b + u))
+            sig = keep.tile([P, PACK, BANK], F32, name="sig%d_%d" % (b, u), tag="h0_%d" % (HALVES * b + u))
             nc.scalar.activation(sig[:], x[b][:, :, BANK * u : BANK * (u + 1)], ACT.Sigmoid)
-            planes = keep.tile([P, PACK, BANK], BF16, name="z_planes")
-            for t in range(PACK):
-                nc.scalar.activation(planes[:, t, :], sig[:, t, :], ACT.Copy, scale=gain_sb[:, b, t : t + 1])
-            z_wide = shared.tile([P, 2 * PACK * BANK], BF16, name="z_last", align_bytes=64, offset=0)
-            z_bf = z_wide[:, 0 : PACK * BANK]
-            nc.vector.tensor_copy(
-                z_bf.rearrange("p (c i t) -> p c t i", i=4, t=PACK),
-                planes[:].rearrange("p t (c i) -> p c t i", i=4),
+            if (b, u) == (1, 1):
+                z_wide = shared.tile([P, 2 * PACK * BANK], BF16, name="z_last", align_bytes=64, offset=0)
+                z_bf = z_wide[:, 0 : PACK * BANK]
+            else:
+                z_bf = keep.tile([P, PACK * BANK], BF16, name="z_bf%d_%d" % (b, u), tag="z_bf%d" % b, align_bytes=64)
+            nc.vector.tensor_tensor(
+                z_bf[:].rearrange("p (c i t) -> p c t i", i=4, t=PACK),
+                sig[:].rearrange("p t (c i) -> p c t i", i=4),
+                gain_sb[:, b : b + 1, :].unsqueeze(3).to_broadcast([P, BANK // 4, PACK, 4]),
+                ALU.mult,
             )
             z_q[b, u] = quantize(z_bf, "z%d_%d" % (b, u))
 
@@ -228,11 +220,13 @@ def tile_list_overlap_track_logits_kernel(tc, tab_words, tab_scales, offs, w1, o
                         first_product(b, t, j)
                 pick(b, t)
         cast_w3(0, nc.scalar.copy)
+        load_sil(2)
+        load_sil(3)
         gate(0, 0)
         cast_w3(1, nc.scalar.copy)
         gate(1, 0)
         gate(0, 1)
-        gate_on_scalar(1, 1)
+        gate(1, 1)
         second_products(0)
         for n in range(4):
             dampen(0, n)

@@ -20,104 +20,106 @@ P = 128
 PACK = 4
 BANK = 512
 PASSES = H // (P * PACK)
-HALVES = E // BANK
-CHUNK = 512
 LIST = 16
-ON_GPSIMD = 4
+KIB = 1024
+SCALE_ROWS = K // 32
+FIRST_SCALE_ROW = P - SCALE_ROWS
 
 
 def tile_list_overlap_track_logits_kernel(tc, tab_words, tab_scales, offs, w1, offs2, wgt, gain, w2_words, w2_scales, sil, w3, out):
     nc = tc.nc
     with ExitStack() as ctx:
         keep = ctx.enter_context(tc.tile_pool(name="keep", bufs=1))
-        ring = ctx.enter_context(tc.tile_pool(name="ring", bufs=2))
-        ring3 = ctx.enter_context(tc.tile_pool(name="ring3", bufs=4))
-        shared = ctx.enter_context(tc.tile_pool(name="shared", bufs=1))
         early = ctx.enter_context(tc.tile_pool(name="early", bufs=1))
+        big = ctx.enter_context(tc.tile_pool(name="big", bufs=1))
+        late = ctx.enter_context(tc.tile_pool(name="late", bufs=1))
         psum = ctx.enter_context(tc.psum_pool(name="psum", bufs=1))
 
         frames = keep.tile([P, S // LIST], U16, name="frames")
         picks = keep.tile([P, E // LIST], U16, name="picks")
         table = early.tile([P, T], U32, name="table", offset=0)
-        table_sc = early.tile([P, T], U8, name="table_sc", offset=24 * 1024)
-        gain_sb = keep.tile([P, PASSES, PACK], F32, name="gain_sb")
+        table_sc = early.tile([P, T], U8, name="table_sc", offset=24 * KIB)
         banks = [psum.tile([P, BANK], F32, name="bank%d" % k) for k in range(8)]
 
-        nc.vector.memset(table_sc[:].bitcast(I32), 0)
-
+        nc.vector.memset(table_sc[0:FIRST_SCALE_ROW, :].bitcast(I32), 0)
+        nc.sync.dma_start(table_sc[FIRST_SCALE_ROW:P, :].bitcast(I32), tab_scales[0].bitcast(I32))
         nc.sync.dma_start(frames[:], offs)
         w1_rows = w1.rearrange("(p j) c -> p j c", j=PACK)
-        w1_first = [keep.tile([P, PACK, 256], F32, name="w1_first%d" % u) for u in range(2)]
-        nc.sync.dma_start(w1_first[0][:], w1_rows[:, :, 0:256])
-        nc.sync.dma_start(gain_sb[:], gain.rearrange("(b p t) -> p b t", b=PASSES, t=PACK))
-        nc.sync.dma_start(table_sc[0:P:8, :].bitcast(I32), tab_scales[0].bitcast(I32))
-        nc.sync.dma_start(w1_first[1][:], w1_rows[:, :, 256:512])
+        w1_first = [early.tile([P, PACK, P], F32, name="w1_first%d" % u, offset=[36, 38, 40, 44][u] * KIB) for u in range(4)]
         nc.sync.dma_start(table[:].bitcast(I32), tab_words[0].rearrange("p t i -> p (t i)").bitcast(I32))
+        for u in range(4):
+            nc.sync.dma_start(w1_first[u][:], w1_rows[:, :, P * u : P * (u + 1)])
         nc.sync.dma_start(picks[:], offs2)
 
         warm = keep.tile([P, 1], F32, name="warm")
-        nc.scalar.activation(warm[:], gain_sb[:, 0, 0:1], ACT.Sigmoid)
+        nc.gpsimd.memset(warm[:], 0)
+        nc.scalar.activation(warm[:], warm[:], ACT.Sigmoid)
+
         v_sc = keep.tile([P, S], U8, name="v_sc", align_bytes=64)
-        picked_sc = early.tile([P, S], U8, name="picked_sc", offset=30 * 1024)
-        nc.vector.memset(v_sc[:].bitcast(I32), 0)
+        picked_sc = early.tile([P, S], U8, name="picked_sc", offset=30 * KIB)
+        nc.gpsimd.memset(v_sc[:].bitcast(I32), 0)
         nc.vector.tensor_copy(picked_sc[:], table_sc[:].indirect(frames[:]))
+        for q in range(4):
+            first = FIRST_SCALE_ROW + 4 * q
+            nc.sync.dma_start(v_sc[32 * q : 32 * q + 4, :].bitcast(I32), picked_sc[first : first + 4, :].bitcast(I32))
+        w1_second = early.tile([P, PACK, BANK], F32, name="w1_second", offset=16 * KIB + 32)
+        nc.sync.dma_start(w1_second[:], w1_rows[:, :, BANK : 2 * BANK])
+        wgt_sb = early.tile([P, E], F32, name="wgt_sb", offset=24 * KIB + 64)
+        nc.sync.dma_start(wgt_sb[:], wgt)
+        gain_sb = early.tile([P, PASSES, PACK], F32, name="gain_sb", offset=24 * KIB + 64 - 32)
+        nc.sync.dma_start(gain_sb[:], gain.rearrange("(b p t) -> p b t", b=PASSES, t=PACK))
+
         v_codes = []
 
-        def gather_words(j):
-            words = keep.tile([P, BANK], U32, name="v_codes%d" % j, align_bytes=64)
+        def gather_words(j, words):
             nc.vector.tensor_copy(words[:], table[:].indirect(frames[:, j * BANK // LIST : (j + 1) * BANK // LIST]))
             v_codes.append(words)
 
-        def quantize(grouped, name):
-            codes = keep.tile([P, BANK], U32, name=name + "_codes", align_bytes=64)
+        def quantize(grouped, name, codes=None):
+            if codes is None:
+                codes = keep.tile([P, BANK], U32, name=name + "_codes", align_bytes=64)
             scales = keep.tile([P, BANK], U8, name=name + "_sc", align_bytes=64)
             nc.vector.quantize_mx(out=codes[:].bitcast(FP8X4), scales=scales[:], in_=grouped[:])
             return codes, scales
 
-        w1_bf = early.tile([P, PACK * BANK], BF16, name="w1_bf", align_bytes=64, offset=32 * 1024)
+        w1_bf = early.tile([P, PACK * BANK], BF16, name="w1_bf", align_bytes=64, offset=32 * KIB)
         w1_view = w1_bf[:].rearrange("p (t m j) -> p m j t", t=PACK, j=PACK)
-        for u in range(2):
-            nc.scalar.copy(w1_view[:, 64 * u : 64 * (u + 1), :, :], w1_first[u][:].rearrange("p j (m t) -> p m j t", t=PACK))
-        for q in range(4):
-            nc.sync.dma_start(v_sc[32 * q : 32 * q + 4, :].bitcast(I32), picked_sc[32 * q : 32 * q + 32 : 8, :].bitcast(I32))
-        w1_second = early.tile([P, PACK, BANK], F32, name="w1_second", offset=16 * 1024 + 64)
-        nc.sync.dma_start(w1_second[:], w1_rows[:, :, BANK : 2 * BANK])
-        wgt_sb = early.tile([P, E], F32, name="wgt_sb", offset=24 * 1024 + 64)
-        nc.sync.dma_start(wgt_sb[:], wgt)
+        for u in range(4):
+            nc.scalar.copy(w1_view[:, 32 * u : 32 * (u + 1), :, :], w1_first[u][:].rearrange("p j (m t) -> p m j t", t=PACK))
+        for j in range(2):
+            gather_words(j, keep.tile([P, BANK], U32, name="v_codes%d" % j, align_bytes=64))
         w1_q = [quantize(w1_bf, "w1a")]
-        w2_sc = early.tile([P, PASSES, N], U8, name="w2_sc", align_bytes=64, offset=32 * 1024)
-        nc.vector.memset(w2_sc[:].rearrange("p a c -> p (a c)").bitcast(I32), 0)
+        for j in range(2, 4):
+            gather_words(j, early.tile([P, BANK], U32, name="v_codes%d" % j, align_bytes=64, offset=(28 + 2 * j) * KIB))
+
+        w2_sc = early.tile([P, PASSES, N], U8, name="w2_sc", align_bytes=64, offset=44 * KIB)
+        nc.gpsimd.memset(w2_sc[:].rearrange("p a c -> p (a c)").bitcast(I32), 0)
         for q in range(4):
             nc.sync.dma_start(w2_sc[32 * q : 32 * q + 4, :, :].bitcast(I32), w2_scales[:, 4 * q : 4 * q + 4, :].rearrange("a r c -> r a c").bitcast(I32))
-        w2_codes = early.tile([P, PASSES, 2 * N], U8, name="w2_codes", align_bytes=64, offset=30 * 1024)
+        w2_codes = early.tile([P, PASSES, 2 * N], U8, name="w2_codes", align_bytes=64, offset=30 * KIB)
         nc.sync.dma_start(w2_codes[:].bitcast(I32), w2_words.rearrange("a p c -> p a c").bitcast(I32))
-        for j in range(S // BANK):
-            gather_words(j)
-        w1_bf = ring.tile([P, PACK * BANK], BF16, name="w_bf", align_bytes=64)
+
+        w1_bf = late.tile([P, PACK * BANK], BF16, name="w1b_bf", offset=0, align_bytes=64)
         nc.vector.tensor_copy(w1_bf[:].rearrange("p (t m j) -> p m j t", t=PACK, j=PACK), w1_second[:].rearrange("p j (m t) -> p m j t", t=PACK))
-        w1_q.append(quantize(w1_bf, "w1b"))
         w3_raw = []
         for b in range(PASSES):
-            raw = early.tile([P, PACK, N], F32, name="w3_raw%d" % b, offset=8 * 1024 * b)
+            raw = early.tile([P, PACK, N], F32, name="w3_raw%d" % b, offset=8 * KIB * b)
             nc.sync.dma_start(raw[:], w3[BANK * b : BANK * (b + 1), :].rearrange("(p j) c -> p j c", j=PACK))
             w3_raw.append(raw)
         sil_sb = []
-
-        def load_sil(n):
-            rows = early.tile([P, E], F32, name="sil%d" % n, offset=[16 * 1024 + 64, 20 * 1024 + 64, 0, 4 * 1024][n])
+        for n in range(N // P):
+            rows = early.tile([P, E], F32, name="sil%d" % n, offset=[16 * KIB + 32, 20 * KIB + 32, 36 * KIB, 40 * KIB][n])
             nc.sync.dma_start(rows[:], sil[P * n : P * (n + 1), :])
             sil_sb.append(rows)
 
-        load_sil(0)
-        load_sil(1)
-
-        h = [[keep.tile([P, S], F32, name="h%d_%d" % (b, t), tag="h%d_%d" % (b, t)) for t in range(PACK)] for b in range(PASSES)]
+        h = [big.tile([P, S], F32, name="h%d" % i, offset=8 * KIB * i, align_bytes=64) for i in range(PASSES * PACK)]
 
         turn = []
 
-        def first_product(b, t, j):
+        def first_products(i, slices=range(S // BANK)):
+            b, t = divmod(i, PACK)
             codes, scales = w1_q[b]
-            if True:
+            for j in slices:
                 bank = banks[len(turn) % 8]
                 turn.append(j)
                 nc.tensor.matmul_mx(
@@ -129,114 +131,172 @@ def tile_list_overlap_track_logits_kernel(tc, tab_words, tab_scales, offs, w1, o
                     start=True,
                     stop=True,
                 )
-                nc.scalar.copy(h[b][t][:, BANK * j : BANK * (j + 1)], bank[:])
+                nc.scalar.copy(h[i][:, BANK * j : BANK * (j + 1)], bank[:])
 
-        x = [keep.tile([P, PACK, E], F32, name="x%d" % b) for b in range(PASSES)]
+        x = [late.tile([P, PACK, E], F32, name="x0", offset=0, align_bytes=64), keep.tile([P, PACK, E], F32, name="x1")]
 
-        def pick(b, t):
-            nc.vector.tensor_tensor(x[b][:, t, :], h[b][t][:].indirect(picks[:]), wgt_sb[:], ALU.mult)
+        def pick(i):
+            b, t = divmod(i, PACK)
+            nc.vector.tensor_tensor(x[b][:, t, :], h[i][:].indirect(picks[:]), wgt_sb[:], ALU.mult)
 
+        sig = {}
+        z_in = {}
         z_q = {}
 
+        def sigmoid(b, u):
+            sig[b, u] = big.tile([P, PACK, BANK], F32, name="sig%d_%d" % (b, u), offset=8 * KIB * (1 + 2 * b + u), align_bytes=64)
+            nc.scalar.activation(sig[b, u][:], x[b][:, :, BANK * u : BANK * (u + 1)], ACT.Sigmoid)
+
         def gate(b, u):
-            sig = keep.tile([P, PACK, BANK], F32, name="sig%d_%d" % (b, u), tag="h0_%d" % (HALVES * b + u))
-            nc.scalar.activation(sig[:], x[b][:, :, BANK * u : BANK * (u + 1)], ACT.Sigmoid)
             if (b, u) == (1, 1):
-                z_wide = shared.tile([P, 2 * PACK * BANK], BF16, name="z_last", align_bytes=64, offset=0)
+                z_wide = late.tile([P, 4 * PACK * BANK], BF16, name="z_last", align_bytes=64, offset=24 * KIB)
                 z_bf = z_wide[:, 0 : PACK * BANK]
             else:
                 z_bf = keep.tile([P, PACK * BANK], BF16, name="z_bf%d_%d" % (b, u), tag="z_bf%d" % b, align_bytes=64)
             nc.vector.tensor_tensor(
                 z_bf[:].rearrange("p (c i t) -> p c t i", i=4, t=PACK),
-                sig[:].rearrange("p t (c i) -> p c t i", i=4),
+                sig[b, u][:].rearrange("p t (c i) -> p c t i", i=4),
                 gain_sb[:, b : b + 1, :].unsqueeze(3).to_broadcast([P, BANK // 4, PACK, 4]),
                 ALU.mult,
             )
-            z_q[b, u] = quantize(z_bf, "z%d_%d" % (b, u))
+            z_in[b, u] = z_bf
 
+        def quantize_z(b, u, codes=None):
+            z_q[b, u] = quantize(z_in[b, u], "z%d_%d" % (b, u), codes)
+
+        HALF = N // 2
+        w3_bf = [late.tile([P, PASSES, PACK * HALF], BF16, name="w3_bf%d" % k, offset=(16 + 4 * k) * KIB, align_bytes=64) for k in range(2)]
         w3_q = []
 
-        def cast_w3(b, copy):
-            w3_bf = ring.tile([P, PACK * BANK], BF16, name="w_bf", align_bytes=64)
-            copy(
-                w3_bf[:].rearrange("p (c i j) -> p c j i", i=4, j=PACK),
-                w3_raw[b][:].rearrange("p j (c i) -> p c j i", i=4),
+        def cast_w3(b, k):
+            nc.scalar.copy(
+                w3_bf[k][:, b, :].rearrange("p (c i j) -> p c j i", i=4, j=PACK),
+                w3_raw[b][:, :, HALF * k : HALF * (k + 1)].rearrange("p j (c i) -> p c j i", i=4),
             )
-            w3_q.append(quantize(w3_bf, "w3_%d" % b))
 
-        speech_bank = [[banks[0], banks[2], banks[4], banks[6]], [banks[1], banks[5], banks[0], banks[4]]]
-        carry_bank = [[banks[1], banks[3], banks[5], banks[7]], [banks[3], banks[7], banks[2], banks[6]]]
+        def quantize_w3(k):
+            w3_q.append(quantize(w3_bf[k][:].rearrange("p b c -> p (b c)"), "w3_%d" % k))
 
-        def second_products(u):
-            steps = [(b, n) for b in range(PASSES) for n in range(N // P)]
-            if u == 1:
-                steps = [(0, 0), (0, 1), (1, 0), (1, 1), (0, 2), (1, 2), (0, 3), (1, 3)]
-            for b, n in steps:
-                codes, scales = z_q[b, u]
-                if True:
-                    nc.tensor.matmul_mx(
-                        out=speech_bank[u][n][:],
-                        lhsT=w2_codes[:, b, 2 * P * n : 2 * P * (n + 1)].bitcast(FP4X4),
-                        lhsT_scale=w2_sc[:, b, P * n : P * (n + 1)],
-                        rhs=codes[:].bitcast(FP8X4),
-                        rhs_scale=scales[:],
-                        start=(b == 0),
-                        stop=(b == PASSES - 1),
-                    )
-                    nc.tensor.matmul_mx(
-                        out=carry_bank[u][n][:],
-                        lhsT=w3_q[b][0][:, P * n : P * (n + 1)].bitcast(FP8X4),
-                        lhsT_scale=w3_q[b][1][:, P * n : P * (n + 1)],
-                        rhs=codes[:].bitcast(FP8X4),
-                        rhs_scale=scales[:],
-                        start=(b == 0),
-                        stop=(b == PASSES - 1),
-                    )
+        speech_bank = [[banks[k] for k in (0, 1, 2, 3)], [banks[k] for k in (4, 5, 2, 3)]]
+        carry_bank = [[banks[k] for k in (6, 7, 6, 7)], [banks[k] for k in (0, 1, 4, 5)]]
+
+        def speech_pass(u, b, n):
+            codes, scales = z_q[b, u]
+            nc.tensor.matmul_mx(
+                out=speech_bank[u][n][:],
+                lhsT=w2_codes[:, b, 2 * P * n : 2 * P * (n + 1)].bitcast(FP4X4),
+                lhsT_scale=w2_sc[:, b, P * n : P * (n + 1)],
+                rhs=codes[:].bitcast(FP8X4),
+                rhs_scale=scales[:],
+                start=(b == 0),
+                stop=(b == PASSES - 1),
+            )
+
+        def carry_pass(u, b, n):
+            codes, scales = z_q[b, u]
+            first = HALF * b + P * (n % 2)
+            nc.tensor.matmul_mx(
+                out=carry_bank[u][n][:],
+                lhsT=w3_q[n // 2][0][:, first : first + P].bitcast(FP8X4),
+                lhsT_scale=w3_q[n // 2][1][:, first : first + P],
+                rhs=codes[:].bitcast(FP8X4),
+                rhs_scale=scales[:],
+                start=(b == 0),
+                stop=(b == PASSES - 1),
+            )
+
+        damped = {}
 
         def dampen(u, n):
             part = sil_sb[n][:, BANK * u : BANK * (u + 1)]
-            nc.vector.scalar_tensor_tensor(part, part, 1.0, speech_bank[u][n][:], ALU.subtract, ALU.mult)
+            if u == 0:
+                damped[u, n] = late.tile([P, BANK], F32, name="damped%d" % n, offset=(32 + 2 * n) * KIB, align_bytes=64)[:]
+            else:
+                damped[u, n] = part
+            nc.vector.scalar_tensor_tensor(damped[u, n], part, 1.0, speech_bank[u][n][:], ALU.subtract, ALU.mult)
 
-        def add_on_vector(u, n, queue):
+        def add_on_vector(u, n):
             part = sil_sb[n][:, BANK * u : BANK * (u + 1)]
             nc.vector.tensor_tensor(part, carry_bank[u][n][:], part, ALU.subtract)
-            queue.dma_start(out[P * n : P * (n + 1), BANK * u : BANK * (u + 1)], part)
+            nc.scalar.dma_start(out[P * n : P * (n + 1), BANK * u : BANK * (u + 1)], part)
 
-        def add_on_gpsimd(u, n):
-            part = sil_sb[n][:, BANK * u : BANK * (u + 1)]
-            carry = ring3.tile([P, BANK], F32, name="carry")
-            nc.scalar.copy(carry[:], carry_bank[u][n][:])
-            result = shared.tile([P, BANK], F32, name="result%d" % n, align_bytes=64, offset=4 * BANK * n)
-            nc.gpsimd.tensor_tensor(result[:], carry[:], part, ALU.subtract)
+        carry = {}
+
+        def copy_carry(u, n):
+            carry[u, n] = keep.tile([P, BANK], F32, name="carry%d_%d" % (u, n))
+            nc.scalar.copy(carry[u, n][:], carry_bank[u][n][:])
+
+        def add_on_gpsimd(u, n, result):
+            nc.gpsimd.tensor_tensor(result[:], carry[u, n][:], damped[u, n], ALU.subtract)
             nc.sync.dma_start(out[P * n : P * (n + 1), BANK * u : BANK * (u + 1)], result[:])
 
-        for j in range(S // BANK):
-            for t in range(2):
-                first_product(0, t, j)
-        for b in range(PASSES):
-            for t in range(PACK):
-                if PACK * b + t >= 2:
-                    for j in range(S // BANK):
-                        first_product(b, t, j)
-                pick(b, t)
-        cast_w3(0, nc.scalar.copy)
-        load_sil(2)
-        load_sil(3)
+        w1_q.append(quantize(w1_bf, "w1b"))
+        first_products(0, [0, 1, 2])
+        first_products(1, [0])
+        first_products(0, [3])
+        first_products(1, [1, 2, 3])
+        pick(0)
+        pick(1)
+        for i in range(2, 6):
+            first_products(i)
+            pick(i)
+        sigmoid(0, 0)
         gate(0, 0)
-        cast_w3(1, nc.scalar.copy)
-        gate(1, 0)
+        first_products(6)
+        pick(6)
+        quantize_z(0, 0)
+        first_products(7)
+        pick(7)
+        for n in range(4):
+            speech_pass(0, 0, n)
+        sigmoid(0, 1)
+        cast_w3(0, 0)
         gate(0, 1)
+        quantize_z(0, 1)
+        for n in range(2):
+            speech_pass(1, 0, n)
+        sigmoid(1, 0)
+        cast_w3(1, 0)
+        sigmoid(1, 1)
+        gate(1, 0)
+        quantize_w3(0)
+        quantize_z(1, 0)
+        for b in range(PASSES):
+            for n in range(2):
+                carry_pass(0, b, n)
+        for n in range(4):
+            speech_pass(0, 1, n)
+        for b in range(PASSES):
+            cast_w3(b, 1)
+        for n in range(2):
+            copy_carry(0, n)
         gate(1, 1)
-        second_products(0)
+        quantize_w3(1)
+        quantize_z(1, 1, late.tile([P, BANK], U32, name="z_last_codes", offset=20 * KIB, align_bytes=64))
+        results = [late.tile([P, BANK], F32, name="result%d" % n, align_bytes=64, offset=(24 + 2 * n) * KIB) for n in range(4)]
+        for n in range(2, 4):
+            for b in range(PASSES):
+                carry_pass(0, b, n)
+            copy_carry(0, n)
+        for n in range(2):
+            speech_pass(1, 1, n)
         for n in range(4):
             dampen(0, n)
-            add_on_gpsimd(0, n)
-        second_products(1)
-        dampen(1, 0)
-        dampen(1, 1)
-        add_on_vector(1, 0, nc.scalar)
-        add_on_vector(1, 1, nc.scalar)
-        dampen(1, 2)
-        dampen(1, 3)
-        add_on_vector(1, 2, nc.scalar)
-        add_on_vector(1, 3, nc.scalar)
+            add_on_gpsimd(0, n, results[n])
+        for n in range(2):
+            for b in range(PASSES):
+                carry_pass(1, b, n)
+        for n in range(2, 4):
+            for b in range(PASSES):
+                speech_pass(1, b, n)
+        for n in range(2):
+            dampen(1, n)
+        for n in range(2):
+            add_on_vector(1, n)
+        for n in range(2, 4):
+            for b in range(PASSES):
+                carry_pass(1, b, n)
+        for n in range(2, 4):
+            dampen(1, n)
+        for n in range(2, 4):
+            add_on_vector(1, n)

@@ -45,10 +45,10 @@ def tile_list_overlap_track_logits_kernel(tc, tab_words, tab_scales, offs, w1, o
         nc.sync.dma_start(table_sc[FIRST_SCALE_ROW:P, :].bitcast(I32), tab_scales[0].bitcast(I32))
         nc.sync.dma_start(frames[:], offs)
         w1_rows = w1.rearrange("(p j) c -> p j c", j=PACK)
-        w1_first = [early.tile([P, PACK, P], F32, name="w1_first%d" % u, offset=[36, 38, 40, 44][u] * KIB) for u in range(4)]
+        w1_first = [early.tile([P, PACK, 256], F32, name="w1_first%d" % u, offset=(36 + 4 * u) * KIB) for u in range(2)]
+        for u in range(2):
+            nc.sync.dma_start(w1_first[u][:], w1_rows[:, :, 256 * u : 256 * (u + 1)])
         nc.sync.dma_start(table[:].bitcast(I32), tab_words[0].rearrange("p t i -> p (t i)").bitcast(I32))
-        for u in range(4):
-            nc.sync.dma_start(w1_first[u][:], w1_rows[:, :, P * u : P * (u + 1)])
         nc.sync.dma_start(picks[:], offs2)
 
         warm = keep.tile([P, 1], F32, name="warm")
@@ -84,15 +84,13 @@ def tile_list_overlap_track_logits_kernel(tc, tab_words, tab_scales, offs, w1, o
 
         w1_bf = early.tile([P, PACK * BANK], BF16, name="w1_bf", align_bytes=64, offset=32 * KIB)
         w1_view = w1_bf[:].rearrange("p (t m j) -> p m j t", t=PACK, j=PACK)
-        for u in range(4):
-            nc.scalar.copy(w1_view[:, 32 * u : 32 * (u + 1), :, :], w1_first[u][:].rearrange("p j (m t) -> p m j t", t=PACK))
-        for j in range(2):
-            gather_words(j, keep.tile([P, BANK], U32, name="v_codes%d" % j, align_bytes=64))
+        for u in range(2):
+            nc.scalar.copy(w1_view[:, 64 * u : 64 * (u + 1), :, :], w1_first[u][:].rearrange("p j (m t) -> p m j t", t=PACK))
         w1_q = [quantize(w1_bf, "w1a")]
-        for j in range(2, 4):
-            gather_words(j, early.tile([P, BANK], U32, name="v_codes%d" % j, align_bytes=64, offset=(28 + 2 * j) * KIB))
+        for j in range(4):
+            gather_words(j, keep.tile([P, BANK], U32, name="v_codes%d" % j, align_bytes=64))
 
-        w2_sc = early.tile([P, PASSES, N], U8, name="w2_sc", align_bytes=64, offset=44 * KIB)
+        w2_sc = early.tile([P, PASSES, N], U8, name="w2_sc", align_bytes=64, offset=32 * KIB)
         nc.gpsimd.memset(w2_sc[:].rearrange("p a c -> p (a c)").bitcast(I32), 0)
         for q in range(4):
             nc.sync.dma_start(w2_sc[32 * q : 32 * q + 4, :, :].bitcast(I32), w2_scales[:, 4 * q : 4 * q + 4, :].rearrange("a r c -> r a c").bitcast(I32))
@@ -231,10 +229,9 @@ def tile_list_overlap_track_logits_kernel(tc, tab_words, tab_scales, offs, w1, o
             nc.sync.dma_start(out[P * n : P * (n + 1), BANK * u : BANK * (u + 1)], result[:])
 
         w1_q.append(quantize(w1_bf, "w1b"))
-        first_products(0, [0, 1, 2])
-        first_products(1, [0])
-        first_products(0, [3])
-        first_products(1, [1, 2, 3])
+        for j in range(S // BANK):
+            first_products(0, [j])
+            first_products(1, [j])
         pick(0)
         pick(1)
         for i in range(2, 6):

@@ -46,9 +46,9 @@ def tile_list_overlap_track_logits_kernel(tc, tab_words, tab_scales, offs, w1, o
         nc.sync.dma_start(frames[:], offs)
         w1_rows = w1.rearrange("(p j) c -> p j c", j=PACK)
         w1_first = [early.tile([P, PACK, 256], F32, name="w1_first%d" % u, offset=(36 + 4 * u) * KIB) for u in range(2)]
+        nc.sync.dma_start(table[:].bitcast(I32), tab_words[0].rearrange("p t i -> p (t i)").bitcast(I32))
         for u in range(2):
             nc.sync.dma_start(w1_first[u][:], w1_rows[:, :, 256 * u : 256 * (u + 1)])
-        nc.sync.dma_start(table[:].bitcast(I32), tab_words[0].rearrange("p t i -> p (t i)").bitcast(I32))
         nc.sync.dma_start(picks[:], offs2)
 
         warm = keep.tile([P, 1], F32, name="warm")
@@ -86,11 +86,12 @@ def tile_list_overlap_track_logits_kernel(tc, tab_words, tab_scales, offs, w1, o
         w1_view = w1_bf[:].rearrange("p (t m j) -> p m j t", t=PACK, j=PACK)
         for u in range(2):
             nc.scalar.copy(w1_view[:, 64 * u : 64 * (u + 1), :, :], w1_first[u][:].rearrange("p j (m t) -> p m j t", t=PACK))
-        w1_q = [quantize(w1_bf, "w1a")]
-        for j in range(4):
+        for j in range(3):
             gather_words(j, keep.tile([P, BANK], U32, name="v_codes%d" % j, align_bytes=64))
+        w1_q = [quantize(w1_bf, "w1a")]
+        gather_words(3, early.tile([P, BANK], U32, name="v_codes3", align_bytes=64, offset=32 * KIB))
 
-        w2_sc = early.tile([P, PASSES, N], U8, name="w2_sc", align_bytes=64, offset=32 * KIB)
+        w2_sc = early.tile([P, PASSES, N], U8, name="w2_sc", align_bytes=64, offset=34 * KIB)
         nc.gpsimd.memset(w2_sc[:].rearrange("p a c -> p (a c)").bitcast(I32), 0)
         for q in range(4):
             nc.sync.dma_start(w2_sc[32 * q : 32 * q + 4, :, :].bitcast(I32), w2_scales[:, 4 * q : 4 * q + 4, :].rearrange("a r c -> r a c").bitcast(I32))
@@ -104,24 +105,18 @@ def tile_list_overlap_track_logits_kernel(tc, tab_words, tab_scales, offs, w1, o
             raw = early.tile([P, PACK, N], F32, name="w3_raw%d" % b, offset=8 * KIB * b)
             nc.sync.dma_start(raw[:], w3[BANK * b : BANK * (b + 1), :].rearrange("(p j) c -> p j c", j=PACK))
             w3_raw.append(raw)
-        sil_sb = []
-        for n in range(N // P):
-            rows = early.tile([P, E], F32, name="sil%d" % n, offset=[16 * KIB + 32, 20 * KIB + 32, 36 * KIB, 40 * KIB][n])
-            nc.sync.dma_start(rows[:], sil[P * n : P * (n + 1), :])
-            sil_sb.append(rows)
+        sil_all = early.tile([P, N // P, E], F32, name="sil_all", offset=36 * KIB)
+        nc.sync.dma_start(sil_all[:], sil.rearrange("(n p) m -> p n m", p=P))
+        sil_sb = [sil_all[:, n, :] for n in range(N // P)]
 
         h = [big.tile([P, S], F32, name="h%d" % i, offset=8 * KIB * i, align_bytes=64) for i in range(PASSES * PACK)]
 
-        turn = []
-
-        def first_products(i, slices=range(S // BANK)):
+        def first_products(i, slices):
             b, t = divmod(i, PACK)
             codes, scales = w1_q[b]
             for j in slices:
-                bank = banks[len(turn) % 8]
-                turn.append(j)
                 nc.tensor.matmul_mx(
-                    out=bank[:],
+                    out=banks[(PACK * i + j) % 8][:],
                     lhsT=codes[:, P * t : P * (t + 1)].bitcast(FP8X4),
                     lhsT_scale=scales[:, P * t : P * (t + 1)],
                     rhs=v_codes[j][:].bitcast(FP8X4),
@@ -129,7 +124,10 @@ def tile_list_overlap_track_logits_kernel(tc, tab_words, tab_scales, offs, w1, o
                     start=True,
                     stop=True,
                 )
-                nc.scalar.copy(h[i][:, BANK * j : BANK * (j + 1)], bank[:])
+
+        def copy_h(i, order):
+            for j in order:
+                nc.scalar.copy(h[i][:, BANK * j : BANK * (j + 1)], banks[(PACK * i + j) % 8][:])
 
         x = [late.tile([P, PACK, E], F32, name="x0", offset=0, align_bytes=64), keep.tile([P, PACK, E], F32, name="x1")]
 
@@ -147,10 +145,10 @@ def tile_list_overlap_track_logits_kernel(tc, tab_words, tab_scales, offs, w1, o
 
         def gate(b, u):
             if (b, u) == (1, 1):
-                z_wide = late.tile([P, 4 * PACK * BANK], BF16, name="z_last", align_bytes=64, offset=24 * KIB)
+                z_wide = late.tile([P, 4 * PACK * BANK], BF16, name="z_last", align_bytes=64, offset=16 * KIB)
                 z_bf = z_wide[:, 0 : PACK * BANK]
             else:
-                z_bf = keep.tile([P, PACK * BANK], BF16, name="z_bf%d_%d" % (b, u), tag="z_bf%d" % b, align_bytes=64)
+                z_bf = keep.tile([P, PACK * BANK], BF16, name="z_bf%d_%d" % (b, u), align_bytes=64)
             nc.vector.tensor_tensor(
                 z_bf[:].rearrange("p (c i t) -> p c t i", i=4, t=PACK),
                 sig[b, u][:].rearrange("p t (c i) -> p c t i", i=4),
@@ -163,7 +161,7 @@ def tile_list_overlap_track_logits_kernel(tc, tab_words, tab_scales, offs, w1, o
             z_q[b, u] = quantize(z_in[b, u], "z%d_%d" % (b, u), codes)
 
         HALF = N // 2
-        w3_bf = [late.tile([P, PASSES, PACK * HALF], BF16, name="w3_bf%d" % k, offset=(16 + 4 * k) * KIB, align_bytes=64) for k in range(2)]
+        w3_bf = [big.tile([P, PASSES, PACK * HALF], BF16, name="w3_bf%d" % k, offset=(48 + 4 * k) * KIB, align_bytes=64) for k in range(2)]
         w3_q = []
 
         def cast_w3(b, k):
@@ -208,7 +206,7 @@ def tile_list_overlap_track_logits_kernel(tc, tab_words, tab_scales, offs, w1, o
         def dampen(u, n):
             part = sil_sb[n][:, BANK * u : BANK * (u + 1)]
             if u == 0:
-                damped[u, n] = late.tile([P, BANK], F32, name="damped%d" % n, offset=(32 + 2 * n) * KIB, align_bytes=64)[:]
+                damped[u, n] = late.tile([P, BANK], F32, name="damped%d" % n, offset=(24 + 2 * n) * KIB, align_bytes=64)[:]
             else:
                 damped[u, n] = part
             nc.vector.scalar_tensor_tensor(damped[u, n], part, 1.0, speech_bank[u][n][:], ALU.subtract, ALU.mult)
@@ -229,27 +227,28 @@ def tile_list_overlap_track_logits_kernel(tc, tab_words, tab_scales, offs, w1, o
             nc.sync.dma_start(out[P * n : P * (n + 1), BANK * u : BANK * (u + 1)], result[:])
 
         w1_q.append(quantize(w1_bf, "w1b"))
-        for j in range(S // BANK):
-            first_products(0, [j])
-            first_products(1, [j])
-        pick(0)
-        pick(1)
+        last_first = [3, 0, 1, 2]
+        for i in range(2):
+            first_products(i, range(4))
+            copy_h(i, range(4))
+            pick(i)
         for i in range(2, 6):
-            first_products(i)
+            first_products(i, range(4))
+            copy_h(i, last_first)
             pick(i)
         sigmoid(0, 0)
         gate(0, 0)
-        first_products(6)
-        pick(6)
-        quantize_z(0, 0)
-        first_products(7)
-        pick(7)
-        for n in range(4):
-            speech_pass(0, 0, n)
+        for i in range(6, 8):
+            first_products(i, range(4))
+            copy_h(i, last_first)
+            pick(i)
         sigmoid(0, 1)
         cast_w3(0, 0)
         gate(0, 1)
+        quantize_z(0, 0, big.tile([P, BANK], U32, name="z_first_codes", offset=16 * KIB, align_bytes=64))
         quantize_z(0, 1)
+        for n in range(4):
+            speech_pass(0, 0, n)
         for n in range(2):
             speech_pass(1, 0, n)
         sigmoid(1, 0)
@@ -269,8 +268,8 @@ def tile_list_overlap_track_logits_kernel(tc, tab_words, tab_scales, offs, w1, o
             copy_carry(0, n)
         gate(1, 1)
         quantize_w3(1)
-        quantize_z(1, 1, late.tile([P, BANK], U32, name="z_last_codes", offset=20 * KIB, align_bytes=64))
-        results = [late.tile([P, BANK], F32, name="result%d" % n, align_bytes=64, offset=(24 + 2 * n) * KIB) for n in range(4)]
+        quantize_z(1, 1, big.tile([P, BANK], U32, name="z_last_codes", offset=52 * KIB, align_bytes=64))
+        results = [late.tile([P, BANK], F32, name="result%d" % n, align_bytes=64, offset=(16 + 2 * n) * KIB) for n in range(4)]
         for n in range(2, 4):
             for b in range(PASSES):
                 carry_pass(0, b, n)

@@ -24,6 +24,7 @@ LIST = 16
 KIB = 1024
 SCALE_ROWS = K // 32
 FIRST_SCALE_ROW = P - SCALE_ROWS
+SCALED = 256
 
 
 def tile_list_overlap_track_logits_kernel(tc, tab_words, tab_scales, offs, w1, offs2, wgt, gain, w2_words, w2_scales, sil, w3, out):
@@ -144,11 +145,7 @@ def tile_list_overlap_track_logits_kernel(tc, tab_words, tab_scales, offs, w1, o
             nc.scalar.activation(sig[b, u][:], x[b][:, :, BANK * u : BANK * (u + 1)], ACT.Sigmoid)
 
         def gate(b, u):
-            if (b, u) == (1, 1):
-                z_wide = late.tile([P, 4 * PACK * BANK], BF16, name="z_last", align_bytes=64, offset=16 * KIB)
-                z_bf = z_wide[:, 0 : PACK * BANK]
-            else:
-                z_bf = keep.tile([P, PACK * BANK], BF16, name="z_bf%d_%d" % (b, u), align_bytes=64)
+            z_bf = keep.tile([P, PACK * BANK], BF16, name="z_bf%d_%d" % (b, u), align_bytes=64)
             nc.vector.tensor_tensor(
                 z_bf[:].rearrange("p (c i t) -> p c t i", i=4, t=PACK),
                 sig[b, u][:].rearrange("p t (c i) -> p c t i", i=4),
@@ -157,11 +154,30 @@ def tile_list_overlap_track_logits_kernel(tc, tab_words, tab_scales, offs, w1, o
             )
             z_in[b, u] = z_bf
 
+        def last_gate():
+            z_wide = late.tile([P, 2 * PACK * BANK], BF16, name="z_last", align_bytes=64, offset=16 * KIB)
+            z_bf = z_wide[:, 0 : PACK * BANK]
+            split = BANK - SCALED
+            planes = keep.tile([P, PACK, SCALED], BF16, name="planes", align_bytes=64)
+            for t in range(PACK):
+                nc.scalar.activation(planes[:, t, :], sig[1, 1][:, t, split:BANK], ACT.Copy, scale=gain_sb[:, 1, t : t + 1])
+            nc.vector.tensor_tensor(
+                z_bf[:, 0 : PACK * split].rearrange("p (c i t) -> p c t i", i=4, t=PACK),
+                sig[1, 1][:, :, 0:split].rearrange("p t (c i) -> p c t i", i=4),
+                gain_sb[:, 1:2, :].unsqueeze(3).to_broadcast([P, split // 4, PACK, 4]),
+                ALU.mult,
+            )
+            nc.vector.tensor_copy(
+                z_bf[:, PACK * split : PACK * BANK].rearrange("p (c i t) -> p c t i", i=4, t=PACK),
+                planes[:].rearrange("p t (c i) -> p c t i", i=4),
+            )
+            z_in[1, 1] = z_bf
+
         def quantize_z(b, u, codes=None):
             z_q[b, u] = quantize(z_in[b, u], "z%d_%d" % (b, u), codes)
 
         HALF = N // 2
-        w3_bf = [big.tile([P, PASSES, PACK * HALF], BF16, name="w3_bf%d" % k, offset=(48 + 4 * k) * KIB, align_bytes=64) for k in range(2)]
+        w3_bf = [big.tile([P, PASSES * (1 + 2 * k), PACK * HALF], BF16, name="w3_bf%d" % k, offset=(48 + 4 * k) * KIB, align_bytes=64) for k in range(2)]
         w3_q = []
 
         def cast_w3(b, k):
@@ -171,7 +187,7 @@ def tile_list_overlap_track_logits_kernel(tc, tab_words, tab_scales, offs, w1, o
             )
 
         def quantize_w3(k):
-            w3_q.append(quantize(w3_bf[k][:].rearrange("p b c -> p (b c)"), "w3_%d" % k))
+            w3_q.append(quantize(w3_bf[k][:, 0:PASSES, :].rearrange("p b c -> p (b c)"), "w3_%d" % k))
 
         speech_bank = [[banks[k] for k in (0, 1, 2, 3)], [banks[k] for k in (4, 5, 2, 3)]]
         carry_bank = [[banks[k] for k in (6, 7, 6, 7)], [banks[k] for k in (0, 1, 4, 5)]]
@@ -206,7 +222,8 @@ def tile_list_overlap_track_logits_kernel(tc, tab_words, tab_scales, offs, w1, o
         def dampen(u, n):
             part = sil_sb[n][:, BANK * u : BANK * (u + 1)]
             if u == 0:
-                damped[u, n] = late.tile([P, BANK], F32, name="damped%d" % n, offset=(24 + 2 * n) * KIB, align_bytes=64)[:]
+                pool, offset = (late, 16 + 2 * n) if n < 2 else (big, 48 + 2 * n)
+                damped[u, n] = pool.tile([P, BANK], F32, name="damped%d" % n, offset=offset * KIB, align_bytes=64)[:]
             else:
                 damped[u, n] = part
             nc.vector.scalar_tensor_tensor(damped[u, n], part, 1.0, speech_bank[u][n][:], ALU.subtract, ALU.mult)
@@ -219,12 +236,13 @@ def tile_list_overlap_track_logits_kernel(tc, tab_words, tab_scales, offs, w1, o
         carry = {}
 
         def copy_carry(u, n):
-            carry[u, n] = keep.tile([P, BANK], F32, name="carry%d_%d" % (u, n))
-            nc.scalar.copy(carry[u, n][:], carry_bank[u][n][:])
+            width = BANK if n < 3 else HALF
+            carry[u, n] = keep.tile([P, width], F32, name="carry%d_%d" % (u, n))
+            nc.scalar.copy(carry[u, n][:], carry_bank[u][n][:, 0:width])
 
-        def add_on_gpsimd(u, n, result):
-            nc.gpsimd.tensor_tensor(result[:], carry[u, n][:], damped[u, n], ALU.subtract)
-            nc.sync.dma_start(out[P * n : P * (n + 1), BANK * u : BANK * (u + 1)], result[:])
+        def add_on_gpsimd(n, width, result):
+            nc.gpsimd.tensor_tensor(result[:, 0:width], carry[0, n][:, 0:width], damped[0, n][:, 0:width], ALU.subtract)
+            nc.sync.dma_start(out[P * n : P * (n + 1), 0:width], result[:, 0:width])
 
         w1_q.append(quantize(w1_bf, "w1b"))
         last_first = [3, 0, 1, 2]
@@ -262,26 +280,27 @@ def tile_list_overlap_track_logits_kernel(tc, tab_words, tab_scales, offs, w1, o
                 carry_pass(0, b, n)
         for n in range(4):
             speech_pass(0, 1, n)
+        last_gate()
         for b in range(PASSES):
             cast_w3(b, 1)
         for n in range(2):
             copy_carry(0, n)
-        gate(1, 1)
+        quantize_z(1, 1)
+        for n in range(2):
+            speech_pass(1, 1, n)
+        for n in range(2):
+            dampen(0, n)
+            for b in range(PASSES):
+                carry_pass(1, b, n)
         quantize_w3(1)
-        quantize_z(1, 1, big.tile([P, BANK], U32, name="z_last_codes", offset=52 * KIB, align_bytes=64))
-        results = [late.tile([P, BANK], F32, name="result%d" % n, align_bytes=64, offset=(16 + 2 * n) * KIB) for n in range(4)]
+        results = [big.tile([P, BANK], F32, name="result%d" % n, align_bytes=64, offset=(56 + 2 * n) * KIB) for n in range(4)]
         for n in range(2, 4):
             for b in range(PASSES):
                 carry_pass(0, b, n)
             copy_carry(0, n)
-        for n in range(2):
-            speech_pass(1, 1, n)
-        for n in range(4):
             dampen(0, n)
-            add_on_gpsimd(0, n, results[n])
-        for n in range(2):
-            for b in range(PASSES):
-                carry_pass(1, b, n)
+        for n in range(4):
+            add_on_gpsimd(n, BANK if n < 3 else HALF, results[n])
         for n in range(2, 4):
             for b in range(PASSES):
                 speech_pass(1, b, n)
@@ -296,3 +315,6 @@ def tile_list_overlap_track_logits_kernel(tc, tab_words, tab_scales, offs, w1, o
             dampen(1, n)
         for n in range(2, 4):
             add_on_vector(1, n)
+        rest = results[3][:, HALF:BANK]
+        nc.vector.tensor_tensor(rest, carry_bank[0][3][:, HALF:BANK], damped[0, 3][:, HALF:BANK], ALU.subtract)
+        nc.sync.dma_start(out[3 * P : 4 * P, HALF:BANK], rest)

@@ -24,7 +24,6 @@ LIST = 16
 KIB = 1024
 SCALE_ROWS = K // 32
 FIRST_SCALE_ROW = P - SCALE_ROWS
-SCALED = 256
 
 
 def tile_list_overlap_track_logits_kernel(tc, tab_words, tab_scales, offs, w1, offs2, wgt, gain, w2_words, w2_scales, sil, w3, out):
@@ -62,7 +61,7 @@ def tile_list_overlap_track_logits_kernel(tc, tab_words, tab_scales, offs, w1, o
         nc.vector.tensor_copy(picked_sc[:], table_sc[:].indirect(frames[:]))
         for q in range(4):
             first = FIRST_SCALE_ROW + 4 * q
-            nc.sync.dma_start(v_sc[32 * q : 32 * q + 4, :].bitcast(I32), picked_sc[first : first + 4, :].bitcast(I32))
+            nc.scalar.dma_start(v_sc[32 * q : 32 * q + 4, :].bitcast(I32), picked_sc[first : first + 4, :].bitcast(I32))
         w1_second = early.tile([P, PACK, BANK], F32, name="w1_second", offset=16 * KIB + 32)
         nc.sync.dma_start(w1_second[:], w1_rows[:, :, BANK : 2 * BANK])
         wgt_sb = early.tile([P, E], F32, name="wgt_sb", offset=24 * KIB + 64)
@@ -144,34 +143,27 @@ def tile_list_overlap_track_logits_kernel(tc, tab_words, tab_scales, offs, w1, o
             sig[b, u] = big.tile([P, PACK, BANK], F32, name="sig%d_%d" % (b, u), offset=8 * KIB * (1 + 2 * b + u), align_bytes=64)
             nc.scalar.activation(sig[b, u][:], x[b][:, :, BANK * u : BANK * (u + 1)], ACT.Sigmoid)
 
-        def gate(b, u):
-            z_bf = keep.tile([P, PACK * BANK], BF16, name="z_bf%d_%d" % (b, u), align_bytes=64)
-            nc.vector.tensor_tensor(
-                z_bf[:].rearrange("p (c i t) -> p c t i", i=4, t=PACK),
-                sig[b, u][:].rearrange("p t (c i) -> p c t i", i=4),
-                gain_sb[:, b : b + 1, :].unsqueeze(3).to_broadcast([P, BANK // 4, PACK, 4]),
-                ALU.mult,
-            )
-            z_in[b, u] = z_bf
-
-        def last_gate():
-            z_wide = late.tile([P, 2 * PACK * BANK], BF16, name="z_last", align_bytes=64, offset=16 * KIB)
-            z_bf = z_wide[:, 0 : PACK * BANK]
-            split = BANK - SCALED
-            planes = keep.tile([P, PACK, SCALED], BF16, name="planes", align_bytes=64)
-            for t in range(PACK):
-                nc.scalar.activation(planes[:, t, :], sig[1, 1][:, t, split:BANK], ACT.Copy, scale=gain_sb[:, 1, t : t + 1])
+        def gate(b, u, z_bf, scaled=0):
+            split = BANK - scaled
+            if scaled:
+                planes = keep.tile([P, PACK, scaled], BF16, name="planes%d" % b, align_bytes=64)
+                for t in range(PACK):
+                    nc.scalar.activation(planes[:, t, :], sig[b, u][:, t, split:BANK], ACT.Copy, scale=gain_sb[:, b, t : t + 1])
             nc.vector.tensor_tensor(
                 z_bf[:, 0 : PACK * split].rearrange("p (c i t) -> p c t i", i=4, t=PACK),
-                sig[1, 1][:, :, 0:split].rearrange("p t (c i) -> p c t i", i=4),
-                gain_sb[:, 1:2, :].unsqueeze(3).to_broadcast([P, split // 4, PACK, 4]),
+                sig[b, u][:, :, 0:split].rearrange("p t (c i) -> p c t i", i=4),
+                gain_sb[:, b : b + 1, :].unsqueeze(3).to_broadcast([P, split // 4, PACK, 4]),
                 ALU.mult,
             )
-            nc.vector.tensor_copy(
-                z_bf[:, PACK * split : PACK * BANK].rearrange("p (c i t) -> p c t i", i=4, t=PACK),
-                planes[:].rearrange("p t (c i) -> p c t i", i=4),
-            )
-            z_in[1, 1] = z_bf
+            if scaled:
+                nc.vector.tensor_copy(
+                    z_bf[:, PACK * split : PACK * BANK].rearrange("p (c i t) -> p c t i", i=4, t=PACK),
+                    planes[:].rearrange("p t (c i) -> p c t i", i=4),
+                )
+            z_in[b, u] = z_bf[:, 0 : PACK * BANK]
+
+        def z_tile(b, u):
+            return keep.tile([P, PACK * BANK], BF16, name="z_bf%d_%d" % (b, u), align_bytes=64)
 
         def quantize_z(b, u, codes=None):
             z_q[b, u] = quantize(z_in[b, u], "z%d_%d" % (b, u), codes)
@@ -255,14 +247,14 @@ def tile_list_overlap_track_logits_kernel(tc, tab_words, tab_scales, offs, w1, o
             copy_h(i, last_first)
             pick(i)
         sigmoid(0, 0)
-        gate(0, 0)
+        gate(0, 0, z_tile(0, 0))
         for i in range(6, 8):
             first_products(i, range(4))
             copy_h(i, last_first)
             pick(i)
         sigmoid(0, 1)
+        gate(0, 1, z_tile(0, 1), 0)
         cast_w3(0, 0)
-        gate(0, 1)
         quantize_z(0, 0, big.tile([P, BANK], U32, name="z_first_codes", offset=16 * KIB, align_bytes=64))
         quantize_z(0, 1)
         for n in range(4):
@@ -272,7 +264,7 @@ def tile_list_overlap_track_logits_kernel(tc, tab_words, tab_scales, offs, w1, o
         sigmoid(1, 0)
         cast_w3(1, 0)
         sigmoid(1, 1)
-        gate(1, 0)
+        gate(1, 0, z_tile(1, 0))
         quantize_w3(0)
         quantize_z(1, 0)
         for b in range(PASSES):
@@ -280,7 +272,7 @@ def tile_list_overlap_track_logits_kernel(tc, tab_words, tab_scales, offs, w1, o
                 carry_pass(0, b, n)
         for n in range(4):
             speech_pass(0, 1, n)
-        last_gate()
+        gate(1, 1, late.tile([P, 2 * PACK * BANK], BF16, name="z_last", align_bytes=64, offset=16 * KIB), 256)
         for b in range(PASSES):
             cast_w3(b, 1)
         for n in range(2):

@@ -49,6 +49,8 @@ def tile_list_overlap_track_logits_kernel(tc, tab_words, tab_scales, offs, w1, o
         nc.sync.dma_start(table[:].bitcast(I32), tab_words[0].rearrange("p t i -> p (t i)").bitcast(I32))
         for u in range(2):
             nc.sync.dma_start(w1_first[u][:], w1_rows[:, :, 256 * u : 256 * (u + 1)])
+        w1_second = early.tile([P, PACK, BANK], F32, name="w1_second", offset=16 * KIB)
+        nc.sync.dma_start(w1_second[:], w1_rows[:, :, BANK : 2 * BANK])
         nc.sync.dma_start(picks[:], offs2)
 
         warm = keep.tile([P, 1], F32, name="warm")
@@ -62,8 +64,6 @@ def tile_list_overlap_track_logits_kernel(tc, tab_words, tab_scales, offs, w1, o
         for q in range(4):
             first = FIRST_SCALE_ROW + 4 * q
             nc.scalar.dma_start(v_sc[32 * q : 32 * q + 4, :].bitcast(I32), picked_sc[first : first + 4, :].bitcast(I32))
-        w1_second = early.tile([P, PACK, BANK], F32, name="w1_second", offset=16 * KIB + 32)
-        nc.sync.dma_start(w1_second[:], w1_rows[:, :, BANK : 2 * BANK])
         wgt_sb = early.tile([P, E], F32, name="wgt_sb", offset=24 * KIB + 64)
         nc.sync.dma_start(wgt_sb[:], wgt)
         gain_sb = early.tile([P, PASSES, PACK], F32, name="gain_sb", offset=24 * KIB + 64 - 32)
@@ -172,10 +172,10 @@ def tile_list_overlap_track_logits_kernel(tc, tab_words, tab_scales, offs, w1, o
         w3_bf = [big.tile([P, PASSES * (1 + 2 * k), PACK * HALF], BF16, name="w3_bf%d" % k, offset=(48 + 4 * k) * KIB, align_bytes=64) for k in range(2)]
         w3_q = []
 
-        def cast_w3(b, k):
+        def cast_w3(b, k, first=0, last=HALF):
             nc.scalar.copy(
-                w3_bf[k][:, b, :].rearrange("p (c i j) -> p c j i", i=4, j=PACK),
-                w3_raw[b][:, :, HALF * k : HALF * (k + 1)].rearrange("p j (c i) -> p c j i", i=4),
+                w3_bf[k][:, b, PACK * first : PACK * last].rearrange("p (c i j) -> p c j i", i=4, j=PACK),
+                w3_raw[b][:, :, HALF * k + first : HALF * k + last].rearrange("p j (c i) -> p c j i", i=4),
             )
 
         def quantize_w3(k):
@@ -236,12 +236,15 @@ def tile_list_overlap_track_logits_kernel(tc, tab_words, tab_scales, offs, w1, o
             nc.gpsimd.tensor_tensor(result[:, 0:width], carry[0, n][:, 0:width], damped[0, n][:, 0:width], ALU.subtract)
             nc.sync.dma_start(out[P * n : P * (n + 1), 0:width], result[:, 0:width])
 
-        w1_q.append(quantize(w1_bf, "w1b"))
         last_first = [3, 0, 1, 2]
-        for i in range(2):
-            first_products(i, range(4))
-            copy_h(i, range(4))
-            pick(i)
+        first_products(0, range(4))
+        copy_h(0, [0, 1, 3])
+        nc.vector.tensor_copy(h[0][:, 2 * BANK : 3 * BANK], banks[2][:])
+        w1_q.append(quantize(w1_bf, "w1b"))
+        pick(0)
+        first_products(1, range(4))
+        copy_h(1, range(4))
+        pick(1)
         for i in range(2, 6):
             first_products(i, range(4))
             copy_h(i, last_first)
@@ -255,6 +258,7 @@ def tile_list_overlap_track_logits_kernel(tc, tab_words, tab_scales, offs, w1, o
         sigmoid(0, 1)
         gate(0, 1, z_tile(0, 1), 0)
         cast_w3(0, 0)
+        cast_w3(1, 0, 0, P)
         quantize_z(0, 0, big.tile([P, BANK], U32, name="z_first_codes", offset=16 * KIB, align_bytes=64))
         quantize_z(0, 1)
         for n in range(4):
@@ -262,7 +266,7 @@ def tile_list_overlap_track_logits_kernel(tc, tab_words, tab_scales, offs, w1, o
         for n in range(2):
             speech_pass(1, 0, n)
         sigmoid(1, 0)
-        cast_w3(1, 0)
+        cast_w3(1, 0, P, HALF)
         sigmoid(1, 1)
         gate(1, 0, z_tile(1, 0))
         quantize_w3(0)
@@ -280,7 +284,7 @@ def tile_list_overlap_track_logits_kernel(tc, tab_words, tab_scales, offs, w1, o
         quantize_z(1, 1)
         for n in range(2):
             speech_pass(1, 1, n)
-        for n in range(2):
+        for n in (1, 0):
             dampen(0, n)
             for b in range(PASSES):
                 carry_pass(1, b, n)
@@ -290,17 +294,18 @@ def tile_list_overlap_track_logits_kernel(tc, tab_words, tab_scales, offs, w1, o
             for b in range(PASSES):
                 carry_pass(0, b, n)
             copy_carry(0, n)
+        for n in (3, 2):
             dampen(0, n)
         for n in range(4):
             add_on_gpsimd(n, BANK if n < 3 else HALF, results[n])
-        for n in range(2, 4):
+        for n in (3, 2):
             for b in range(PASSES):
                 speech_pass(1, b, n)
-        for n in range(2):
+        for n in (1, 0):
             dampen(1, n)
         for n in range(2):
             add_on_vector(1, n)
-        for n in range(2, 4):
+        for n in (3, 2):
             for b in range(PASSES):
                 carry_pass(1, b, n)
         for n in range(2, 4):

@@ -1,6 +1,7 @@
 from contextlib import ExitStack
 
 import concourse.mybir as mybir
+from concourse.masks import make_identity
 
 T, S, E, K, H, N = 4096, 2048, 1024, 512, 1024, 512
 FLOPS = 2 * K * H * S + 2 * 2 * H * N * E
@@ -24,50 +25,64 @@ LIST = 16
 KIB = 1024
 SCALE_ROWS = K // 32
 FIRST_SCALE_ROW = P - SCALE_ROWS
+FIRST_GAIN_ROW = P - PASSES
+PIECE = 256
+HALF = N // 2
+RING = 7
+SCALAR_CAST = 64
 
 
 def tile_list_overlap_track_logits_kernel(tc, tab_words, tab_scales, offs, w1, offs2, wgt, gain, w2_words, w2_scales, sil, w3, out):
     nc = tc.nc
     with ExitStack() as ctx:
         keep = ctx.enter_context(tc.tile_pool(name="keep", bufs=1))
-        early = ctx.enter_context(tc.tile_pool(name="early", bufs=1))
-        big = ctx.enter_context(tc.tile_pool(name="big", bufs=1))
-        late = ctx.enter_context(tc.tile_pool(name="late", bufs=1))
+        arena = ctx.enter_context(tc.tile_pool(name="arena", bufs=1))
         psum = ctx.enter_context(tc.psum_pool(name="psum", bufs=1))
+
+        def place(shape, dtype, name, kib):
+            return arena.tile(shape, dtype, name=name, offset=kib * KIB, align_bytes=64)
+
+        def own(shape, dtype, name):
+            return keep.tile(shape, dtype, name=name, align_bytes=64)
 
         frames = keep.tile([P, S // LIST], U16, name="frames")
         picks = keep.tile([P, E // LIST], U16, name="picks")
-        table = early.tile([P, T], U32, name="table", offset=0)
-        table_sc = early.tile([P, T], U8, name="table_sc", offset=24 * KIB)
+        table = place([P, T], U32, "table", 96)
+        table_sc = place([P, T], U8, "table_sc", 112)
         banks = [psum.tile([P, BANK], F32, name="bank%d" % k) for k in range(8)]
 
         nc.vector.memset(table_sc[0:FIRST_SCALE_ROW, :].bitcast(I32), 0)
         nc.sync.dma_start(table_sc[FIRST_SCALE_ROW:P, :].bitcast(I32), tab_scales[0].bitcast(I32))
+        gain_rows = own([P, BANK], F32, "gain_rows")
+        nc.scalar.dma_start(gain_rows[FIRST_GAIN_ROW:P, :], gain.rearrange("(b c) -> b c", b=PASSES))
         nc.sync.dma_start(frames[:], offs)
-        w1_rows = w1.rearrange("(p j) c -> p j c", j=PACK)
-        w1_first = [early.tile([P, PACK, 256], F32, name="w1_first%d" % u, offset=(36 + 4 * u) * KIB) for u in range(2)]
         nc.sync.dma_start(table[:].bitcast(I32), tab_words[0].rearrange("p t i -> p (t i)").bitcast(I32))
-        for u in range(2):
-            nc.sync.dma_start(w1_first[u][:], w1_rows[:, :, 256 * u : 256 * (u + 1)])
-        w1_second = early.tile([P, PACK, BANK], F32, name="w1_second", offset=16 * KIB)
-        nc.sync.dma_start(w1_second[:], w1_rows[:, :, BANK : 2 * BANK])
         nc.sync.dma_start(picks[:], offs2)
+        w1_rows = w1.rearrange("(p j) c -> p j c", j=PACK)
+        w1_raw = [place([P, PACK, PIECE], F32, "w1_raw%d" % u, kib) for u, kib in enumerate((152, 122, 126, 154))]
+        for u in range(3):
+            nc.sync.dma_start(w1_raw[u][:], w1_rows[:, :, PIECE * u : PIECE * (u + 1)])
 
         warm = keep.tile([P, 1], F32, name="warm")
         nc.gpsimd.memset(warm[:], 0)
         nc.scalar.activation(warm[:], warm[:], ACT.Sigmoid)
 
-        v_sc = keep.tile([P, S], U8, name="v_sc", align_bytes=64)
-        picked_sc = early.tile([P, S], U8, name="picked_sc", offset=30 * KIB)
+        ident = own([P, P], F32, "ident")
+        make_identity(nc, ident[:])
+        nc.gpsimd.memset(gain_rows[0:FIRST_GAIN_ROW, :], 0)
+        gain_bank = banks[RING][:].rearrange("p (t q) -> p t q", t=PACK)
+        for t in range(PACK):
+            nc.tensor.transpose(gain_bank[:, t, :], gain_rows[:, t:BANK:PACK], ident[:])
+        gain_sb = own([P, PACK, PASSES], F32, "gain_sb")
+        nc.scalar.copy(gain_sb[:], gain_bank[:, :, FIRST_GAIN_ROW:P])
+
+        v_sc = own([P, S], U8, "v_sc")
+        picked_sc = place([P, S], U8, "picked_sc", 116)
         nc.gpsimd.memset(v_sc[:].bitcast(I32), 0)
         nc.vector.tensor_copy(picked_sc[:], table_sc[:].indirect(frames[:]))
         for q in range(4):
             first = FIRST_SCALE_ROW + 4 * q
             nc.scalar.dma_start(v_sc[32 * q : 32 * q + 4, :].bitcast(I32), picked_sc[first : first + 4, :].bitcast(I32))
-        wgt_sb = early.tile([P, E], F32, name="wgt_sb", offset=24 * KIB + 64)
-        nc.sync.dma_start(wgt_sb[:], wgt)
-        gain_sb = early.tile([P, PASSES, PACK], F32, name="gain_sb", offset=24 * KIB + 64 - 32)
-        nc.sync.dma_start(gain_sb[:], gain.rearrange("(b p t) -> p b t", b=PASSES, t=PACK))
 
         v_codes = []
 
@@ -75,50 +90,50 @@ def tile_list_overlap_track_logits_kernel(tc, tab_words, tab_scales, offs, w1, o
             nc.vector.tensor_copy(words[:], table[:].indirect(frames[:, j * BANK // LIST : (j + 1) * BANK // LIST]))
             v_codes.append(words)
 
-        def quantize(grouped, name, codes=None):
-            if codes is None:
-                codes = keep.tile([P, BANK], U32, name=name + "_codes", align_bytes=64)
-            scales = keep.tile([P, BANK], U8, name=name + "_sc", align_bytes=64)
-            nc.vector.quantize_mx(out=codes[:].bitcast(FP8X4), scales=scales[:], in_=grouped[:])
-            return codes, scales
+        def quantize(grouped, codes, scales):
+            nc.vector.quantize_mx(out=codes.bitcast(FP8X4), scales=scales, in_=grouped)
 
-        w1_bf = early.tile([P, PACK * BANK], BF16, name="w1_bf", align_bytes=64, offset=32 * KIB)
-        w1_view = w1_bf[:].rearrange("p (t m j) -> p m j t", t=PACK, j=PACK)
-        for u in range(2):
-            nc.scalar.copy(w1_view[:, 64 * u : 64 * (u + 1), :, :], w1_first[u][:].rearrange("p j (m t) -> p m j t", t=PACK))
+        w1_bf = [place([P, PACK * BANK], BF16, "w1_bf%d" % b, 134 + 4 * b) for b in range(PASSES)]
+        w1_codes = [own([P, BANK], U32, "w1_codes%d" % b) for b in range(PASSES)]
+        w1_sc = [own([P, BANK], U8, "w1_sc%d" % b) for b in range(PASSES)]
+        for u in range(3):
+            b, half = divmod(u, 2)
+            view = w1_bf[b][:].rearrange("p (t m j) -> p m j t", t=PACK, j=PACK)
+            nc.scalar.copy(view[:, 64 * half : 64 * (half + 1), :, :], w1_raw[u][:].rearrange("p j (m t) -> p m j t", t=PACK))
+        nc.sync.dma_start(w1_raw[3][:], w1_rows[:, :, 3 * PIECE : 4 * PIECE])
+        wgt_sb = place([P, E], F32, "wgt_sb", 150)
+        nc.sync.dma_start(wgt_sb[:], wgt)
+        nc.gpsimd.tensor_scalar(
+            w1_bf[1][:].rearrange("p (t m j) -> p t m j", t=PACK, j=PACK)[:, :, 64:P, :],
+            w1_raw[3][:].rearrange("p j (m t) -> p t m j", t=PACK),
+            1.0, 0.0, ALU.mult, ALU.add,
+        )
         for j in range(3):
-            gather_words(j, keep.tile([P, BANK], U32, name="v_codes%d" % j, align_bytes=64))
-        w1_q = [quantize(w1_bf, "w1a")]
-        gather_words(3, early.tile([P, BANK], U32, name="v_codes3", align_bytes=64, offset=32 * KIB))
+            gather_words(j, own([P, BANK], U32, "v_codes%d" % j))
+        quantize(w1_bf[0][:, 0 : 2 * BANK], w1_codes[0][:, 0 : 2 * P], w1_sc[0][:, 0 : 2 * P])
+        gather_words(3, place([P, BANK], U32, "v_codes3", 122))
+        quantize(w1_bf[0][:, 2 * BANK : 4 * BANK], w1_codes[0][:, 2 * P : 4 * P], w1_sc[0][:, 2 * P : 4 * P])
 
-        w2_sc = early.tile([P, PASSES, N], U8, name="w2_sc", align_bytes=64, offset=34 * KIB)
+        w3_raw = place([P, PASSES, PACK, N], F32, "w3_raw", 96)
+        nc.sync.dma_start(w3_raw[:].rearrange("p b j c -> p b (j c)"), w3.rearrange("(b p j) c -> p b (j c)", b=PASSES, j=PACK))
+        w2_codes = place([P, PASSES, 2 * N], U8, "w2_codes", 126)
+        nc.sync.dma_start(w2_codes[:].bitcast(I32), w2_words.rearrange("a p c -> p a c").bitcast(I32))
+        w2_sc = place([P, PASSES, N], U8, "w2_sc", 154)
         nc.gpsimd.memset(w2_sc[:].rearrange("p a c -> p (a c)").bitcast(I32), 0)
         for q in range(4):
             nc.sync.dma_start(w2_sc[32 * q : 32 * q + 4, :, :].bitcast(I32), w2_scales[:, 4 * q : 4 * q + 4, :].rearrange("a r c -> r a c").bitcast(I32))
-        w2_codes = early.tile([P, PASSES, 2 * N], U8, name="w2_codes", align_bytes=64, offset=30 * KIB)
-        nc.sync.dma_start(w2_codes[:].bitcast(I32), w2_words.rearrange("a p c -> p a c").bitcast(I32))
-
-        w1_bf = late.tile([P, PACK * BANK], BF16, name="w1b_bf", offset=0, align_bytes=64)
-        nc.vector.tensor_copy(w1_bf[:].rearrange("p (t m j) -> p m j t", t=PACK, j=PACK), w1_second[:].rearrange("p j (m t) -> p m j t", t=PACK))
-        w3_raw = []
-        for b in range(PASSES):
-            raw = early.tile([P, PACK, N], F32, name="w3_raw%d" % b, offset=8 * KIB * b)
-            nc.sync.dma_start(raw[:], w3[BANK * b : BANK * (b + 1), :].rearrange("(p j) c -> p j c", j=PACK))
-            w3_raw.append(raw)
-        sil_all = early.tile([P, N // P, E], F32, name="sil_all", offset=36 * KIB)
+        sil_all = place([P, N // P, E], F32, "sil_all", 134)
         nc.sync.dma_start(sil_all[:], sil.rearrange("(n p) m -> p n m", p=P))
-        sil_sb = [sil_all[:, n, :] for n in range(N // P)]
 
-        h = [big.tile([P, S], F32, name="h%d" % i, offset=8 * KIB * i, align_bytes=64) for i in range(PASSES * PACK)]
+        h = [place([P, S], F32, "h%d" % i, 8 * i) for i in range(PASSES * PACK)]
 
-        def first_products(i, slices):
+        def first_products(i):
             b, t = divmod(i, PACK)
-            codes, scales = w1_q[b]
-            for j in slices:
+            for j in range(4):
                 nc.tensor.matmul_mx(
-                    out=banks[(PACK * i + j) % 8][:],
-                    lhsT=codes[:, P * t : P * (t + 1)].bitcast(FP8X4),
-                    lhsT_scale=scales[:, P * t : P * (t + 1)],
+                    out=banks[(PACK * i + j) % RING][:],
+                    lhsT=w1_codes[b][:, P * t : P * (t + 1)].bitcast(FP8X4),
+                    lhsT_scale=w1_sc[b][:, P * t : P * (t + 1)],
                     rhs=v_codes[j][:].bitcast(FP8X4),
                     rhs_scale=v_sc[:, BANK * j : BANK * (j + 1)],
                     start=True,
@@ -127,62 +142,46 @@ def tile_list_overlap_track_logits_kernel(tc, tab_words, tab_scales, offs, w1, o
 
         def copy_h(i, order):
             for j in order:
-                nc.scalar.copy(h[i][:, BANK * j : BANK * (j + 1)], banks[(PACK * i + j) % 8][:])
+                nc.scalar.copy(h[i][:, BANK * j : BANK * (j + 1)], banks[(PACK * i + j) % RING][:])
 
-        x = [late.tile([P, PACK, E], F32, name="x0", offset=0, align_bytes=64), keep.tile([P, PACK, E], F32, name="x1")]
+        x = [place([P, PACK, E], F32, "x%d" % b, 64 + 16 * b) for b in range(PASSES)]
 
         def pick(i):
             b, t = divmod(i, PACK)
             nc.vector.tensor_tensor(x[b][:, t, :], h[i][:].indirect(picks[:]), wgt_sb[:], ALU.mult)
 
         sig = {}
-        z_in = {}
+        z_bf = {}
         z_q = {}
 
         def sigmoid(b, u):
-            sig[b, u] = big.tile([P, PACK, BANK], F32, name="sig%d_%d" % (b, u), offset=8 * KIB * (1 + 2 * b + u), align_bytes=64)
+            sig[b, u] = place([P, PACK, BANK], F32, "sig%d_%d" % (b, u), 8 * (5 - 2 * b - u))
             nc.scalar.activation(sig[b, u][:], x[b][:, :, BANK * u : BANK * (u + 1)], ACT.Sigmoid)
 
-        def gate(b, u, z_bf, scaled=0):
-            split = BANK - scaled
-            if scaled:
-                planes = keep.tile([P, PACK, scaled], BF16, name="planes%d" % b, align_bytes=64)
-                for t in range(PACK):
-                    nc.scalar.activation(planes[:, t, :], sig[b, u][:, t, split:BANK], ACT.Copy, scale=gain_sb[:, b, t : t + 1])
+        def grouped_view(b, u):
+            z_bf[b, u] = place([P, PACK * BANK], BF16, "z_bf%d_%d" % (b, u), 4 * (2 * b + u))
+            return z_bf[b, u][:].rearrange("p (c i t) -> p c t i", i=4, t=PACK)
+
+        def gate(b, u):
+            row = FIRST_GAIN_ROW + b
             nc.vector.tensor_tensor(
-                z_bf[:, 0 : PACK * split].rearrange("p (c i t) -> p c t i", i=4, t=PACK),
-                sig[b, u][:, :, 0:split].rearrange("p t (c i) -> p c t i", i=4),
-                gain_sb[:, b : b + 1, :].unsqueeze(3).to_broadcast([P, split // 4, PACK, 4]),
+                grouped_view(b, u),
+                sig[b, u][:].rearrange("p t (c i) -> p c t i", i=4),
+                gain_bank[:, :, row : row + 1].rearrange("p t o -> p o t").unsqueeze(3).to_broadcast([P, BANK // 4, PACK, 4]),
                 ALU.mult,
             )
-            if scaled:
-                nc.vector.tensor_copy(
-                    z_bf[:, PACK * split : PACK * BANK].rearrange("p (c i t) -> p c t i", i=4, t=PACK),
-                    planes[:].rearrange("p t (c i) -> p c t i", i=4),
-                )
-            z_in[b, u] = z_bf[:, 0 : PACK * BANK]
 
-        def z_tile(b, u):
-            return keep.tile([P, PACK * BANK], BF16, name="z_bf%d_%d" % (b, u), align_bytes=64)
+        def quantize_z(b, u, codes):
+            scales = own([P, BANK], U8, "z_sc%d_%d" % (b, u))
+            quantize(z_bf[b, u][:], codes[:], scales[:])
+            z_q[b, u] = (codes, scales)
 
-        def quantize_z(b, u, codes=None):
-            z_q[b, u] = quantize(z_in[b, u], "z%d_%d" % (b, u), codes)
+        def cast_on_gpsimd(dst, src):
+            nc.gpsimd.tensor_scalar(dst, src, 1.0, 0.0, ALU.mult, ALU.add)
 
-        HALF = N // 2
-        w3_bf = [big.tile([P, PASSES * (1 + 2 * k), PACK * HALF], BF16, name="w3_bf%d" % k, offset=(48 + 4 * k) * KIB, align_bytes=64) for k in range(2)]
-        w3_q = []
-
-        def cast_w3(b, k, first=0, last=HALF):
-            nc.scalar.copy(
-                w3_bf[k][:, b, PACK * first : PACK * last].rearrange("p (c i j) -> p c j i", i=4, j=PACK),
-                w3_raw[b][:, :, HALF * k + first : HALF * k + last].rearrange("p j (c i) -> p c j i", i=4),
-            )
-
-        def quantize_w3(k):
-            w3_q.append(quantize(w3_bf[k][:, 0:PASSES, :].rearrange("p b c -> p (b c)"), "w3_%d" % k))
-
-        speech_bank = [[banks[k] for k in (0, 1, 2, 3)], [banks[k] for k in (4, 5, 2, 3)]]
-        carry_bank = [[banks[k] for k in (6, 7, 6, 7)], [banks[k] for k in (0, 1, 4, 5)]]
+        speech_bank = [[banks[k] for k in (0, 1, 2, 3)], [banks[k] for k in (4, 5, 6, 2)]]
+        carry_bank = [[banks[RING]] * 4, [banks[k] for k in (0, 1, 3, 4)]]
+        w3_q = {}
 
         def speech_pass(u, b, n):
             codes, scales = z_q[b, u]
@@ -198,120 +197,116 @@ def tile_list_overlap_track_logits_kernel(tc, tab_words, tab_scales, offs, w1, o
 
         def carry_pass(u, b, n):
             codes, scales = z_q[b, u]
-            first = HALF * b + P * (n % 2)
+            w_codes, w_scales = w3_q[b, n // 2]
+            first = P * (n % 2)
             nc.tensor.matmul_mx(
                 out=carry_bank[u][n][:],
-                lhsT=w3_q[n // 2][0][:, first : first + P].bitcast(FP8X4),
-                lhsT_scale=w3_q[n // 2][1][:, first : first + P],
+                lhsT=w_codes[:, first : first + P].bitcast(FP8X4),
+                lhsT_scale=w_scales[:, first : first + P],
                 rhs=codes[:].bitcast(FP8X4),
                 rhs_scale=scales[:],
                 start=(b == 0),
                 stop=(b == PASSES - 1),
             )
 
-        damped = {}
-
-        def dampen(u, n):
-            part = sil_sb[n][:, BANK * u : BANK * (u + 1)]
-            if u == 0:
-                pool, offset = (late, 16 + 2 * n) if n < 2 else (big, 48 + 2 * n)
-                damped[u, n] = pool.tile([P, BANK], F32, name="damped%d" % n, offset=offset * KIB, align_bytes=64)[:]
-            else:
-                damped[u, n] = part
-            nc.vector.scalar_tensor_tensor(damped[u, n], part, 1.0, speech_bank[u][n][:], ALU.subtract, ALU.mult)
-
-        def add_on_vector(u, n):
-            part = sil_sb[n][:, BANK * u : BANK * (u + 1)]
-            nc.vector.tensor_tensor(part, carry_bank[u][n][:], part, ALU.subtract)
-            nc.scalar.dma_start(out[P * n : P * (n + 1), BANK * u : BANK * (u + 1)], part)
-
-        carry = {}
-
-        def copy_carry(u, n):
-            width = BANK if n < 3 else HALF
-            carry[u, n] = keep.tile([P, width], F32, name="carry%d_%d" % (u, n))
-            nc.scalar.copy(carry[u, n][:], carry_bank[u][n][:, 0:width])
-
-        def add_on_gpsimd(n, width, result):
-            nc.gpsimd.tensor_tensor(result[:, 0:width], carry[0, n][:, 0:width], damped[0, n][:, 0:width], ALU.subtract)
-            nc.sync.dma_start(out[P * n : P * (n + 1), 0:width], result[:, 0:width])
+        def dampen(dst, u, n):
+            nc.vector.scalar_tensor_tensor(dst, sil_all[:, n, BANK * u : BANK * (u + 1)], 1.0, speech_bank[u][n][:], ALU.subtract, ALU.mult)
 
         last_first = [3, 0, 1, 2]
-        first_products(0, range(4))
+        first_products(0)
         copy_h(0, [0, 1, 3])
         nc.vector.tensor_copy(h[0][:, 2 * BANK : 3 * BANK], banks[2][:])
-        w1_q.append(quantize(w1_bf, "w1b"))
+        quantize(w1_bf[1][:], w1_codes[1][:], w1_sc[1][:])
         pick(0)
-        first_products(1, range(4))
+        first_products(1)
         copy_h(1, range(4))
         pick(1)
-        for i in range(2, 6):
-            first_products(i, range(4))
+        for i in range(2, 8):
+            first_products(i)
             copy_h(i, last_first)
             pick(i)
-        sigmoid(0, 0)
-        gate(0, 0, z_tile(0, 0))
-        for i in range(6, 8):
-            first_products(i, range(4))
-            copy_h(i, last_first)
-            pick(i)
-        sigmoid(0, 1)
-        gate(0, 1, z_tile(0, 1), 0)
-        cast_w3(0, 0)
-        cast_w3(1, 0, 0, P)
-        quantize_z(0, 0, big.tile([P, BANK], U32, name="z_first_codes", offset=16 * KIB, align_bytes=64))
-        quantize_z(0, 1)
+
+        w3_low = place([P, PASSES, HALF, PACK], BF16, "w3_low", 56)
+        w3_high = [place([P, HALF, PACK], BF16, "w3_high0", 60)]
+        cast_on_gpsimd(w3_low[:], w3_raw[:, :, :, 0:HALF].rearrange("p b j c -> p b c j"))
+        cast_on_gpsimd(w3_high[0][:, 0 : HALF - SCALAR_CAST, :], w3_raw[:, 0, :, HALF : N - SCALAR_CAST].rearrange("p j c -> p c j"))
+        for u in range(2):
+            sigmoid(0, u)
+            gate(0, u)
+        quantize_z(0, 0, place([P, BANK], U32, "z_codes0_0", 64))
+        quantize_z(0, 1, own([P, BANK], U32, "z_codes0_1"))
         for n in range(4):
             speech_pass(0, 0, n)
-        for n in range(2):
+        for n in range(3):
             speech_pass(1, 0, n)
+        w3_high.append(place([P, HALF, PACK], BF16, "w3_high1", 4))
+        cast_on_gpsimd(w3_high[1][:], w3_raw[:, 1, :, HALF:N].rearrange("p j c -> p c j"))
         sigmoid(1, 0)
-        cast_w3(1, 0, P, HALF)
-        sigmoid(1, 1)
-        gate(1, 0, z_tile(1, 0))
-        quantize_w3(0)
-        quantize_z(1, 0)
+        gate(1, 0)
+        nc.scalar.copy(
+            w3_high[0][:, HALF - SCALAR_CAST : HALF, :].rearrange("p (c i) j -> p c j i", i=4),
+            w3_raw[:, 0, :, N - SCALAR_CAST : N].rearrange("p j (c i) -> p c j i", i=4),
+        )
+        low_codes = place([P, PASSES * HALF], U32, "w3_low_codes", 66)
+        low_sc = own([P, PASSES * HALF], U8, "w3_low_sc")
+        quantize(w3_low[:].rearrange("p b c j -> p (b c j)"), low_codes[:], low_sc[:])
         for b in range(PASSES):
-            for n in range(2):
-                carry_pass(0, b, n)
+            w3_q[b, 0] = (low_codes[:, HALF * b : HALF * (b + 1)], low_sc[:, HALF * b : HALF * (b + 1)])
+        carry_pass(0, 0, 0)
+        quantize_z(1, 0, own([P, BANK], U32, "z_codes1_0"))
+        carry_pass(0, 1, 0)
         for n in range(4):
             speech_pass(0, 1, n)
-        gate(1, 1, late.tile([P, 2 * PACK * BANK], BF16, name="z_last", align_bytes=64, offset=16 * KIB), 256)
-        for b in range(PASSES):
-            cast_w3(b, 1)
-        for n in range(2):
-            copy_carry(0, n)
-        quantize_z(1, 1)
-        for n in range(2):
+
+        def quantize_high(b, kib):
+            codes = place([P, HALF], U32, "w3_high_codes%d" % b, kib)
+            scales = own([P, HALF], U8, "w3_high_sc%d" % b)
+            quantize(w3_high[b][:].rearrange("p c j -> p (c j)"), codes[:], scales[:])
+            w3_q[b, 1] = (codes[:], scales[:])
+
+        quantize_high(0, 68)
+        sigmoid(1, 1)
+        planes = place([P, PACK, BANK], BF16, "planes", 48)
+        for t in range(PACK):
+            nc.scalar.activation(planes[:, t, :], sig[1, 1][:, t, :], ACT.Copy, scale=gain_sb[:, t, 1:2])
+        nc.vector.tensor_copy(grouped_view(1, 1), planes[:].rearrange("p t (c i) -> p c t i", i=4))
+        quantize_high(1, 16)
+        quantize_z(1, 1, own([P, BANK], U32, "z_codes1_1"))
+
+        carry = [place([P, BANK], F32, "carry%d" % n, 70 + 2 * n) for n in range(4)]
+        damped = place([P, N // P, BANK], F32, "damped", 48)
+
+        def carry_out(n):
+            nc.scalar.copy(carry[n][:], banks[RING][:])
+
+        def both_passes(one_pass, u, n):
+            for b in range(PASSES):
+                one_pass(u, b, n)
+
+        carry_out(0)
+        both_passes(carry_pass, 0, 1)
+        carry_out(1)
+        both_passes(carry_pass, 0, 2)
+        carry_out(2)
+        for n in range(3):
             speech_pass(1, 1, n)
-        for n in (1, 0):
-            dampen(0, n)
-            for b in range(PASSES):
-                carry_pass(1, b, n)
-        quantize_w3(1)
-        results = [big.tile([P, BANK], F32, name="result%d" % n, align_bytes=64, offset=(56 + 2 * n) * KIB) for n in range(4)]
-        for n in range(2, 4):
-            for b in range(PASSES):
-                carry_pass(0, b, n)
-            copy_carry(0, n)
-        for n in (3, 2):
-            dampen(0, n)
         for n in range(4):
-            add_on_gpsimd(n, BANK if n < 3 else HALF, results[n])
-        for n in (3, 2):
-            for b in range(PASSES):
-                speech_pass(1, b, n)
-        for n in (1, 0):
-            dampen(1, n)
+            dampen(damped[:, n, :], 0, n)
         for n in range(2):
-            add_on_vector(1, n)
-        for n in (3, 2):
-            for b in range(PASSES):
-                carry_pass(1, b, n)
-        for n in range(2, 4):
-            dampen(1, n)
-        for n in range(2, 4):
-            add_on_vector(1, n)
-        rest = results[3][:, HALF:BANK]
-        nc.vector.tensor_tensor(rest, carry_bank[0][3][:, HALF:BANK], damped[0, 3][:, HALF:BANK], ALU.subtract)
-        nc.sync.dma_start(out[3 * P : 4 * P, HALF:BANK], rest)
+            both_passes(carry_pass, 1, n)
+        both_passes(carry_pass, 0, 3)
+        carry_out(3)
+        for n in range(4):
+            nc.gpsimd.tensor_tensor(carry[n][:], carry[n][:], damped[:, n, :], ALU.subtract)
+            nc.sync.dma_start(out[P * n : P * (n + 1), 0:BANK], carry[n][:])
+        both_passes(speech_pass, 1, 3)
+        for pair in ((0, 1), (2, 3)):
+            for n in pair:
+                dampen(sil_all[:, n, BANK:E], 1, n)
+            if pair[0] == 0:
+                for n in (2, 3):
+                    both_passes(carry_pass, 1, n)
+            for n in pair:
+                part = sil_all[:, n, BANK:E]
+                nc.vector.tensor_tensor(part, carry_bank[1][n][:], part, ALU.subtract)
+                nc.scalar.dma_start(out[P * n : P * (n + 1), BANK:E], part)

@@ -103,16 +103,16 @@ def tile_list_overlap_track_logits_kernel(tc, tab_words, tab_scales, offs, w1, o
         nc.sync.dma_start(w1_raw[3][:], w1_rows[:, :, 3 * PIECE : 4 * PIECE])
         wgt_sb = place([P, E], F32, "wgt_sb", 150)
         nc.sync.dma_start(wgt_sb[:], wgt)
-        nc.gpsimd.tensor_scalar(
-            w1_bf[1][:].rearrange("p (t m j) -> p t m j", t=PACK, j=PACK)[:, :, 64:P, :],
-            w1_raw[3][:].rearrange("p j (m t) -> p t m j", t=PACK),
-            1.0, 0.0, ALU.mult, ALU.add,
-        )
         for j in range(3):
             gather_words(j, own([P, BANK], U32, "v_codes%d" % j))
         quantize(w1_bf[0][:, 0 : 2 * BANK], w1_codes[0][:, 0 : 2 * P], w1_sc[0][:, 0 : 2 * P])
         gather_words(3, place([P, BANK], U32, "v_codes3", 122))
         quantize(w1_bf[0][:, 2 * BANK : 4 * BANK], w1_codes[0][:, 2 * P : 4 * P], w1_sc[0][:, 2 * P : 4 * P])
+
+        nc.vector.tensor_copy(
+            w1_bf[1][:].rearrange("p (t m j) -> p m j t", t=PACK, j=PACK)[:, 64:P, :, :],
+            w1_raw[3][:].rearrange("p j (m t) -> p m j t", t=PACK),
+        )
 
         w3_raw = place([P, PASSES, PACK, N], F32, "w3_raw", 96)
         nc.sync.dma_start(w3_raw[:].rearrange("p b j c -> p b (j c)"), w3.rearrange("(b p j) c -> p b (j c)", b=PASSES, j=PACK))

@@ -214,8 +214,7 @@ def tile_list_overlap_track_logits_kernel(tc, tab_words, tab_scales, offs, w1, o
 
         last_first = [3, 0, 1, 2]
         first_products(0)
-        copy_h(0, [0, 1, 3])
-        nc.vector.tensor_copy(h[0][:, 2 * BANK : 3 * BANK], banks[2][:])
+        copy_h(0, range(4))
         quantize(w1_bf[1][:], w1_codes[1][:], w1_sc[1][:])
         pick(0)
         first_products(1)
@@ -243,10 +242,6 @@ def tile_list_overlap_track_logits_kernel(tc, tab_words, tab_scales, offs, w1, o
         cast_on_gpsimd(w3_high[1][:], w3_raw[:, 1, :, HALF:N].rearrange("p j c -> p c j"))
         sigmoid(1, 0)
         gate(1, 0)
-        nc.scalar.copy(
-            w3_high[0][:, HALF - SCALAR_CAST : HALF, :].rearrange("p (c i) j -> p c j i", i=4),
-            w3_raw[:, 0, :, N - SCALAR_CAST : N].rearrange("p j (c i) -> p c j i", i=4),
-        )
         low_codes = place([P, PASSES * HALF], U32, "w3_low_codes", 66)
         low_sc = own([P, PASSES * HALF], U8, "w3_low_sc")
         quantize(w3_low[:].rearrange("p b c j -> p (b c j)"), low_codes[:], low_sc[:])
@@ -264,20 +259,30 @@ def tile_list_overlap_track_logits_kernel(tc, tab_words, tab_scales, offs, w1, o
             quantize(w3_high[b][:].rearrange("p c j -> p (c j)"), codes[:], scales[:])
             w3_q[b, 1] = (codes[:], scales[:])
 
-        quantize_high(0, 68)
+        quantize_high(1, 68)
         sigmoid(1, 1)
-        planes = place([P, PACK, BANK], BF16, "planes", 48)
+        pairs = place([P, 2, BANK, 2], BF16, "pairs", 48)
         for t in range(PACK):
-            nc.scalar.activation(planes[:, t, :], sig[1, 1][:, t, :], ACT.Copy, scale=gain_sb[:, t, 1:2])
-        nc.vector.tensor_copy(grouped_view(1, 1), planes[:].rearrange("p t (c i) -> p c t i", i=4))
-        quantize_high(1, 16)
+            nc.scalar.activation(pairs[:, t // 2, :, t % 2], sig[1, 1][:, t, :], ACT.Copy, scale=gain_sb[:, t, 1:2])
+        nc.scalar.copy(
+            w3_high[0][:, HALF - SCALAR_CAST : HALF, :].rearrange("p (c i) j -> p c j i", i=4),
+            w3_raw[:, 0, :, N - SCALAR_CAST : N].rearrange("p j (c i) -> p c j i", i=4),
+        )
+        z_bf[1, 1] = place([P, PACK * BANK], BF16, "z_bf1_1", 12)
+        nc.vector.tensor_copy(
+            z_bf[1, 1][:].bitcast(I32).rearrange("p (c i u) -> p c u i", i=4, u=2),
+            pairs[:].rearrange("p u c e -> p (u c e)").bitcast(I32).rearrange("p (u c i) -> p c u i", i=4, u=2),
+        )
+        quantize_high(0, 69)
         quantize_z(1, 1, own([P, BANK], U32, "z_codes1_1"))
 
         carry = [place([P, BANK], F32, "carry%d" % n, 70 + 2 * n) for n in range(4)]
         damped = place([P, N // P, BANK], F32, "damped", 48)
 
+        shared = [BANK, BANK, BANK, HALF]
+
         def carry_out(n):
-            nc.scalar.copy(carry[n][:], banks[RING][:])
+            nc.scalar.copy(carry[n][:, 0 : shared[n]], banks[RING][:, 0 : shared[n]])
 
         def both_passes(one_pass, u, n):
             for b in range(PASSES):
@@ -297,8 +302,9 @@ def tile_list_overlap_track_logits_kernel(tc, tab_words, tab_scales, offs, w1, o
         both_passes(carry_pass, 0, 3)
         carry_out(3)
         for n in range(4):
-            nc.gpsimd.tensor_tensor(carry[n][:], carry[n][:], damped[:, n, :], ALU.subtract)
-            nc.sync.dma_start(out[P * n : P * (n + 1), 0:BANK], carry[n][:])
+            part = carry[n][:, 0 : shared[n]]
+            nc.gpsimd.tensor_tensor(part, part, damped[:, n, 0 : shared[n]], ALU.subtract)
+            nc.sync.dma_start(out[P * n : P * (n + 1), 0 : shared[n]], part)
         both_passes(speech_pass, 1, 3)
         for pair in ((0, 1), (2, 3)):
             for n in pair:
@@ -310,3 +316,6 @@ def tile_list_overlap_track_logits_kernel(tc, tab_words, tab_scales, offs, w1, o
                 part = sil_all[:, n, BANK:E]
                 nc.vector.tensor_tensor(part, carry_bank[1][n][:], part, ALU.subtract)
                 nc.scalar.dma_start(out[P * n : P * (n + 1), BANK:E], part)
+        rest = carry[3][:, HALF:BANK]
+        nc.vector.tensor_tensor(rest, banks[RING][:, HALF:BANK], damped[:, 3, HALF:BANK], ALU.subtract)
+        nc.sync.dma_start(out[3 * P : 4 * P, HALF:BANK], rest)

@@ -105,9 +105,9 @@ def tile_list_overlap_track_logits_kernel(tc, tab_words, tab_scales, offs, w1, o
         nc.sync.dma_start(wgt_sb[:], wgt)
         for j in range(3):
             gather_words(j, own([P, BANK], U32, "v_codes%d" % j))
-        quantize(w1_bf[0][:, 0 : 2 * BANK], w1_codes[0][:, 0 : 2 * P], w1_sc[0][:, 0 : 2 * P])
+        quantize(w1_bf[0][:, 0:BANK], w1_codes[0][:, 0:P], w1_sc[0][:, 0:P])
         gather_words(3, place([P, BANK], U32, "v_codes3", 122))
-        quantize(w1_bf[0][:, 2 * BANK : 4 * BANK], w1_codes[0][:, 2 * P : 4 * P], w1_sc[0][:, 2 * P : 4 * P])
+        quantize(w1_bf[0][:, BANK : 4 * BANK], w1_codes[0][:, P : 4 * P], w1_sc[0][:, P : 4 * P])
 
         nc.vector.tensor_copy(
             w1_bf[1][:].rearrange("p (t m j) -> p m j t", t=PACK, j=PACK)[:, 64:P, :, :],
@@ -262,7 +262,7 @@ def tile_list_overlap_track_logits_kernel(tc, tab_words, tab_scales, offs, w1, o
         quantize_high(1, 68)
         sigmoid(1, 1)
         pairs = place([P, 2, BANK, 2], BF16, "pairs", 48)
-        for t in range(PACK):
+        for t in (0, 2, 1, 3):
             nc.scalar.activation(pairs[:, t // 2, :, t % 2], sig[1, 1][:, t, :], ACT.Copy, scale=gain_sb[:, t, 1:2])
         nc.scalar.copy(
             w3_high[0][:, HALF - SCALAR_CAST : HALF, :].rearrange("p (c i) j -> p c j i", i=4),

@@ -29,7 +29,7 @@ FIRST_GAIN_ROW = P - PASSES
 PIECE = 256
 HALF = N // 2
 RING = 7
-SCALAR_CAST = 64
+SCALAR_CAST = 112
 
 
 def tile_list_overlap_track_logits_kernel(tc, tab_words, tab_scales, offs, w1, offs2, wgt, gain, w2_words, w2_scales, sil, w3, out):

@@ -29,7 +29,6 @@ FIRST_GAIN_ROW = P - PASSES
 PIECE = 256
 HALF = N // 2
 RING = 7
-SCALAR_CAST = 112
 
 
 def tile_list_overlap_track_logits_kernel(tc, tab_words, tab_scales, offs, w1, offs2, wgt, gain, w2_words, w2_scales, sil, w3, out):
@@ -226,9 +225,8 @@ def tile_list_overlap_track_logits_kernel(tc, tab_words, tab_scales, offs, w1, o
             pick(i)
 
         w3_low = place([P, PASSES, HALF, PACK], BF16, "w3_low", 56)
-        w3_high = [place([P, HALF, PACK], BF16, "w3_high0", 60)]
+        w3_high = {}
         cast_on_gpsimd(w3_low[:], w3_raw[:, :, :, 0:HALF].rearrange("p b j c -> p b c j"))
-        cast_on_gpsimd(w3_high[0][:, 0 : HALF - SCALAR_CAST, :], w3_raw[:, 0, :, HALF : N - SCALAR_CAST].rearrange("p j c -> p c j"))
         for u in range(2):
             sigmoid(0, u)
             gate(0, u)
@@ -238,7 +236,7 @@ def tile_list_overlap_track_logits_kernel(tc, tab_words, tab_scales, offs, w1, o
             speech_pass(0, 0, n)
         for n in range(3):
             speech_pass(1, 0, n)
-        w3_high.append(place([P, HALF, PACK], BF16, "w3_high1", 4))
+        w3_high[1] = place([P, HALF, PACK], BF16, "w3_high1", 0)
         cast_on_gpsimd(w3_high[1][:], w3_raw[:, 1, :, HALF:N].rearrange("p j c -> p c j"))
         sigmoid(1, 0)
         gate(1, 0)
@@ -259,27 +257,29 @@ def tile_list_overlap_track_logits_kernel(tc, tab_words, tab_scales, offs, w1, o
             quantize(w3_high[b][:].rearrange("p c j -> p (c j)"), codes[:], scales[:])
             w3_q[b, 1] = (codes[:], scales[:])
 
-        quantize_high(1, 68)
         sigmoid(1, 1)
         pairs = place([P, 2, BANK, 2], BF16, "pairs", 48)
         for t in (0, 2, 1, 3):
             nc.scalar.activation(pairs[:, t // 2, :, t % 2], sig[1, 1][:, t, :], ACT.Copy, scale=gain_sb[:, t, 1:2])
+        w3_high[0] = place([P, HALF, PACK], BF16, "w3_high0", 18)
         nc.scalar.copy(
-            w3_high[0][:, HALF - SCALAR_CAST : HALF, :].rearrange("p (c i) j -> p c j i", i=4),
-            w3_raw[:, 0, :, N - SCALAR_CAST : N].rearrange("p j (c i) -> p c j i", i=4),
+            w3_high[0][:].rearrange("p (c i) j -> p c j i", i=4),
+            w3_raw[:, 0, :, HALF:N].rearrange("p j (c i) -> p c j i", i=4),
         )
         z_bf[1, 1] = place([P, PACK * BANK], BF16, "z_bf1_1", 12)
         nc.vector.tensor_copy(
             z_bf[1, 1][:].bitcast(I32).rearrange("p (c i u) -> p c u i", i=4, u=2),
             pairs[:].rearrange("p u c e -> p (u c e)").bitcast(I32).rearrange("p (u c i) -> p c u i", i=4, u=2),
         )
-        quantize_high(0, 69)
+        quantize_high(1, 16)
         quantize_z(1, 1, own([P, BANK], U32, "z_codes1_1"))
-
-        carry = [place([P, BANK], F32, "carry%d" % n, 70 + 2 * n) for n in range(4)]
-        damped = place([P, N // P, BANK], F32, "damped", 48)
+        quantize_high(0, 69)
 
         shared = [BANK, BANK, BANK, HALF]
+        carry = [place([P, shared[n]], F32, "carry%d" % n, 70 + 2 * n) for n in range(4)]
+        damped = place([P, N // P, BANK], F32, "damped", 48)
+
+        result = place([P, N // P, BANK], F32, "result", 18)
 
         def carry_out(n):
             nc.scalar.copy(carry[n][:, 0 : shared[n]], banks[RING][:, 0 : shared[n]])
@@ -302,8 +302,8 @@ def tile_list_overlap_track_logits_kernel(tc, tab_words, tab_scales, offs, w1, o
         both_passes(carry_pass, 0, 3)
         carry_out(3)
         for n in range(4):
-            part = carry[n][:, 0 : shared[n]]
-            nc.gpsimd.tensor_tensor(part, part, damped[:, n, 0 : shared[n]], ALU.subtract)
+            part = result[:, n, 0 : shared[n]]
+            nc.gpsimd.tensor_tensor(part, carry[n][:, 0 : shared[n]], damped[:, n, 0 : shared[n]], ALU.subtract)
             nc.sync.dma_start(out[P * n : P * (n + 1), 0 : shared[n]], part)
         both_passes(speech_pass, 1, 3)
         for pair in ((0, 1), (2, 3)):
@@ -316,6 +316,6 @@ def tile_list_overlap_track_logits_kernel(tc, tab_words, tab_scales, offs, w1, o
                 part = sil_all[:, n, BANK:E]
                 nc.vector.tensor_tensor(part, carry_bank[1][n][:], part, ALU.subtract)
                 nc.scalar.dma_start(out[P * n : P * (n + 1), BANK:E], part)
-        rest = carry[3][:, HALF:BANK]
+        rest = result[:, 3, HALF:BANK]
         nc.vector.tensor_tensor(rest, banks[RING][:, HALF:BANK], damped[:, 3, HALF:BANK], ALU.subtract)
         nc.sync.dma_start(out[3 * P : 4 * P, HALF:BANK], rest)

@@ -92,7 +92,7 @@ def tile_list_overlap_track_logits_kernel(tc, tab_words, tab_scales, offs, w1, o
         def quantize(grouped, codes, scales):
             nc.vector.quantize_mx(out=codes.bitcast(FP8X4), scales=scales, in_=grouped)
 
-        w1_bf = [place([P, PACK * BANK], BF16, "w1_bf%d" % b, 134 + 4 * b) for b in range(PASSES)]
+        w1_bf = [place([P, PACK * BANK], BF16, "w1_bf%d" % b, 134 + 24 * b) for b in range(PASSES)]
         w1_codes = [own([P, BANK], U32, "w1_codes%d" % b) for b in range(PASSES)]
         w1_sc = [own([P, BANK], U8, "w1_sc%d" % b) for b in range(PASSES)]
         for u in range(3):
@@ -117,11 +117,11 @@ def tile_list_overlap_track_logits_kernel(tc, tab_words, tab_scales, offs, w1, o
         nc.sync.dma_start(w3_raw[:].rearrange("p b j c -> p b (j c)"), w3.rearrange("(b p j) c -> p b (j c)", b=PASSES, j=PACK))
         w2_codes = place([P, PASSES, 2 * N], U8, "w2_codes", 126)
         nc.sync.dma_start(w2_codes[:].bitcast(I32), w2_words.rearrange("a p c -> p a c").bitcast(I32))
-        w2_sc = place([P, PASSES, N], U8, "w2_sc", 154)
+        w2_sc = place([P, PASSES, N], U8, "w2_sc", 158)
         nc.gpsimd.memset(w2_sc[:].rearrange("p a c -> p (a c)").bitcast(I32), 0)
         for q in range(4):
             nc.sync.dma_start(w2_sc[32 * q : 32 * q + 4, :, :].bitcast(I32), w2_scales[:, 4 * q : 4 * q + 4, :].rearrange("a r c -> r a c").bitcast(I32))
-        sil_all = place([P, N // P, E], F32, "sil_all", 134)
+        sil_all = place([P, N // P, E], F32, "sil_all", 160)
         nc.sync.dma_start(sil_all[:], sil.rearrange("(n p) m -> p n m", p=P))
 
         h = [place([P, S], F32, "h%d" % i, 8 * i) for i in range(PASSES * PACK)]

@@ -72,8 +72,8 @@ def tile_list_overlap_track_logits_kernel(tc, tab_words, tab_scales, offs, w1, o
         gain_bank = banks[RING][:].rearrange("p (t q) -> p t q", t=PACK)
         for t in range(PACK):
             nc.tensor.transpose(gain_bank[:, t, :], gain_rows[:, t:BANK:PACK], ident[:])
-        gain_sb = own([P, PACK, PASSES], F32, "gain_sb")
-        nc.scalar.copy(gain_sb[:], gain_bank[:, :, FIRST_GAIN_ROW:P])
+        gain_last = own([P, PACK, 1], F32, "gain_last")
+        nc.scalar.copy(gain_last[:], gain_bank[:, :, P - 1 : P])
 
         v_sc = own([P, S], U8, "v_sc")
         picked_sc = place([P, S], U8, "picked_sc", 116)
@@ -260,7 +260,7 @@ def tile_list_overlap_track_logits_kernel(tc, tab_words, tab_scales, offs, w1, o
         sigmoid(1, 1)
         pairs = place([P, 2, BANK, 2], BF16, "pairs", 48)
         for t in (0, 2, 1, 3):
-            nc.scalar.activation(pairs[:, t // 2, :, t % 2], sig[1, 1][:, t, :], ACT.Copy, scale=gain_sb[:, t, 1:2])
+            nc.scalar.activation(pairs[:, t // 2, :, t % 2], sig[1, 1][:, t, :], ACT.Copy, scale=gain_last[:, t, :])
         w3_high[0] = place([P, HALF, PACK], BF16, "w3_high0", 18)
         nc.scalar.copy(
             w3_high[0][:].rearrange("p (c i) j -> p c j i", i=4),

@@ -27,7 +27,6 @@ SCALE_ROWS = K // 32
 FIRST_SCALE_ROW = P - SCALE_ROWS
 FIRST_GAIN_ROW = P - PASSES
 PIECE = 256
-HALF = N // 2
 RING = 7
 
 
@@ -149,6 +148,19 @@ def tile_list_overlap_track_logits_kernel(tc, tab_words, tab_scales, offs, w1, o
             b, t = divmod(i, PACK)
             nc.vector.tensor_tensor(x[b][:, t, :], h[i][:].indirect(picks[:]), wgt_sb[:], ALU.mult)
 
+        last_first = [3, 0, 1, 2]
+        first_products(0)
+        copy_h(0, range(4))
+        quantize(w1_bf[1][:], w1_codes[1][:], w1_sc[1][:])
+        pick(0)
+        first_products(1)
+        copy_h(1, range(4))
+        pick(1)
+        for i in range(2, 8):
+            first_products(i)
+            copy_h(i, last_first)
+            pick(i)
+
         sig = {}
         z_bf = {}
         z_q = {}
@@ -157,14 +169,11 @@ def tile_list_overlap_track_logits_kernel(tc, tab_words, tab_scales, offs, w1, o
             sig[b, u] = place([P, PACK, BANK], F32, "sig%d_%d" % (b, u), 8 * (5 - 2 * b - u))
             nc.scalar.activation(sig[b, u][:], x[b][:, :, BANK * u : BANK * (u + 1)], ACT.Sigmoid)
 
-        def grouped_view(b, u):
-            z_bf[b, u] = place([P, PACK * BANK], BF16, "z_bf%d_%d" % (b, u), 4 * (2 * b + u))
-            return z_bf[b, u][:].rearrange("p (c i t) -> p c t i", i=4, t=PACK)
-
         def gate(b, u):
             row = FIRST_GAIN_ROW + b
+            z_bf[b, u] = place([P, PACK * BANK], BF16, "z_bf%d_%d" % (b, u), 4 * (2 * b + u))
             nc.vector.tensor_tensor(
-                grouped_view(b, u),
+                z_bf[b, u][:].rearrange("p (c i t) -> p c t i", i=4, t=PACK),
                 sig[b, u][:].rearrange("p t (c i) -> p c t i", i=4),
                 gain_bank[:, :, row : row + 1].rearrange("p t o -> p o t").unsqueeze(3).to_broadcast([P, BANK // 4, PACK, 4]),
                 ALU.mult,
@@ -175,12 +184,15 @@ def tile_list_overlap_track_logits_kernel(tc, tab_words, tab_scales, offs, w1, o
             quantize(z_bf[b, u][:], codes[:], scales[:])
             z_q[b, u] = (codes, scales)
 
-        def cast_on_gpsimd(dst, src):
-            nc.gpsimd.tensor_scalar(dst, src, 1.0, 0.0, ALU.mult, ALU.add)
+        def round_w3(b, first, last, kib):
+            grouped = place([P, last - first, PACK], BF16, "w3_bf%d_%d" % (b, first), kib)
+            nc.gpsimd.tensor_scalar(grouped[:], w3_raw[:, b, :, first:last].rearrange("p j c -> p c j"), 1.0, 0.0, ALU.mult, ALU.add)
+            return grouped[:].rearrange("p c j -> p (c j)")
 
-        speech_bank = [[banks[k] for k in (0, 1, 2, 3)], [banks[k] for k in (4, 5, 6, 2)]]
-        carry_bank = [[banks[RING]] * 4, [banks[k] for k in (0, 1, 3, 4)]]
-        w3_q = {}
+        w3_codes = [place([P, N], U32, "w3_codes%d" % b, 32 - 8 * b) for b in range(PASSES)]
+        w3_sc = [own([P, N], U8, "w3_sc%d" % b) for b in range(PASSES)]
+        speech_bank = [[banks[k] for k in (0, 1, 2, 3)], [banks[k] for k in (4, 5, 6, 3)]]
+        carry_bank = [[banks[k] for k in (RING, 0, 1, 2)], [banks[k] for k in (RING, 0, 1, 2)]]
 
         def speech_pass(u, b, n):
             codes, scales = z_q[b, u]
@@ -196,37 +208,26 @@ def tile_list_overlap_track_logits_kernel(tc, tab_words, tab_scales, offs, w1, o
 
         def carry_pass(u, b, n):
             codes, scales = z_q[b, u]
-            w_codes, w_scales = w3_q[b, n // 2]
-            first = P * (n % 2)
             nc.tensor.matmul_mx(
                 out=carry_bank[u][n][:],
-                lhsT=w_codes[:, first : first + P].bitcast(FP8X4),
-                lhsT_scale=w_scales[:, first : first + P],
+                lhsT=w3_codes[b][:, P * n : P * (n + 1)].bitcast(FP8X4),
+                lhsT_scale=w3_sc[b][:, P * n : P * (n + 1)],
                 rhs=codes[:].bitcast(FP8X4),
                 rhs_scale=scales[:],
                 start=(b == 0),
                 stop=(b == PASSES - 1),
             )
 
-        def dampen(dst, u, n):
-            nc.vector.scalar_tensor_tensor(dst, sil_all[:, n, BANK * u : BANK * (u + 1)], 1.0, speech_bank[u][n][:], ALU.subtract, ALU.mult)
+        def both_passes(one_pass, u, n):
+            for b in range(PASSES):
+                one_pass(u, b, n)
 
-        last_first = [3, 0, 1, 2]
-        first_products(0)
-        copy_h(0, range(4))
-        quantize(w1_bf[1][:], w1_codes[1][:], w1_sc[1][:])
-        pick(0)
-        first_products(1)
-        copy_h(1, range(4))
-        pick(1)
-        for i in range(2, 8):
-            first_products(i)
-            copy_h(i, last_first)
-            pick(i)
+        def dampen(dst, u, n, first=0, last=BANK):
+            silence = sil_all[:, n, BANK * u + first : BANK * u + last]
+            nc.vector.scalar_tensor_tensor(dst, silence, 1.0, speech_bank[u][n][:, first:last], ALU.subtract, ALU.mult)
 
-        w3_low = place([P, PASSES, HALF, PACK], BF16, "w3_low", 56)
-        w3_high = {}
-        cast_on_gpsimd(w3_low[:], w3_raw[:, :, :, 0:HALF].rearrange("p b j c -> p b c j"))
+        w3_first = round_w3(0, 0, N, 56)
+        w3_second = round_w3(1, 0, P, 60)
         for u in range(2):
             sigmoid(0, u)
             gate(0, u)
@@ -236,86 +237,75 @@ def tile_list_overlap_track_logits_kernel(tc, tab_words, tab_scales, offs, w1, o
             speech_pass(0, 0, n)
         for n in range(3):
             speech_pass(1, 0, n)
-        w3_high[1] = place([P, HALF, PACK], BF16, "w3_high1", 0)
-        cast_on_gpsimd(w3_high[1][:], w3_raw[:, 1, :, HALF:N].rearrange("p j c -> p c j"))
+        w3_third = round_w3(1, P, N, 0)
         sigmoid(1, 0)
         gate(1, 0)
-        low_codes = place([P, PASSES * HALF], U32, "w3_low_codes", 66)
-        low_sc = own([P, PASSES * HALF], U8, "w3_low_sc")
-        quantize(w3_low[:].rearrange("p b c j -> p (b c j)"), low_codes[:], low_sc[:])
-        for b in range(PASSES):
-            w3_q[b, 0] = (low_codes[:, HALF * b : HALF * (b + 1)], low_sc[:, HALF * b : HALF * (b + 1)])
+        quantize(w3_first, w3_codes[0][:], w3_sc[0][:])
         carry_pass(0, 0, 0)
         quantize_z(1, 0, own([P, BANK], U32, "z_codes1_0"))
-        carry_pass(0, 1, 0)
         for n in range(4):
             speech_pass(0, 1, n)
+        quantize(w3_second, w3_codes[1][:, 0:P], w3_sc[1][:, 0:P])
+        quantize(w3_third, w3_codes[1][:, P:N], w3_sc[1][:, P:N])
+        carry_pass(0, 1, 0)
 
-        def quantize_high(b, kib):
-            codes = place([P, HALF], U32, "w3_high_codes%d" % b, kib)
-            scales = own([P, HALF], U8, "w3_high_sc%d" % b)
-            quantize(w3_high[b][:].rearrange("p c j -> p (c j)"), codes[:], scales[:])
-            w3_q[b, 1] = (codes[:], scales[:])
-
-        sigmoid(1, 1)
+        planes = [place([P, 2, BANK], F32, "sig1_1_%d" % e, 16 + 4 * e) for e in range(2)]
+        for e in range(2):
+            nc.scalar.activation(planes[e][:], x[1][:, e:PACK:2, BANK:E], ACT.Sigmoid)
         pairs = place([P, 2, BANK, 2], BF16, "pairs", 48)
         for t in (0, 2, 1, 3):
-            nc.scalar.activation(pairs[:, t // 2, :, t % 2], sig[1, 1][:, t, :], ACT.Copy, scale=gain_last[:, t, :])
-        w3_high[0] = place([P, HALF, PACK], BF16, "w3_high0", 18)
-        nc.scalar.copy(
-            w3_high[0][:].rearrange("p (c i) j -> p c j i", i=4),
-            w3_raw[:, 0, :, HALF:N].rearrange("p j (c i) -> p c j i", i=4),
-        )
+            nc.scalar.activation(pairs[:, t // 2, :, t % 2], planes[t % 2][:, t // 2, :], ACT.Copy, scale=gain_last[:, t, :])
         z_bf[1, 1] = place([P, PACK * BANK], BF16, "z_bf1_1", 12)
-        nc.vector.tensor_copy(
-            z_bf[1, 1][:].bitcast(I32).rearrange("p (c i u) -> p c u i", i=4, u=2),
-            pairs[:].rearrange("p u c e -> p (u c e)").bitcast(I32).rearrange("p (u c i) -> p c u i", i=4, u=2),
+        nc.scalar.copy(
+            z_bf[1, 1][:].bitcast(U32).rearrange("p (c i u) -> p c u i", i=4, u=2),
+            pairs[:].rearrange("p u c e -> p (u c e)").bitcast(U32).rearrange("p (u c i) -> p c u i", i=4, u=2),
         )
-        quantize_high(1, 16)
-        quantize_z(1, 1, own([P, BANK], U32, "z_codes1_1"))
-        quantize_high(0, 69)
 
-        shared = [BANK, BANK, BANK, HALF]
-        carry = [place([P, shared[n]], F32, "carry%d" % n, 70 + 2 * n) for n in range(4)]
-        damped = place([P, N // P, BANK], F32, "damped", 48)
+        damped = [place([P, BANK], F32, "damped%d" % n, kib) for n, kib in enumerate((66, 68, 48, 50))]
+        result = place([P, N // P, BANK], F32, "result", 8)
 
-        result = place([P, N // P, BANK], F32, "result", 18)
+        def second_half(n, first=0, last=BANK):
+            return sil_all[:, n, BANK + first : BANK + last]
 
-        def carry_out(n):
-            nc.scalar.copy(carry[n][:, 0 : shared[n]], banks[RING][:, 0 : shared[n]])
+        def sum_on_gpsimd(u, n, source, kib):
+            carry = place([P, BANK], F32, "carry%d_%d" % (u, n), kib)
+            nc.scalar.copy(carry[:], carry_bank[u][n][:])
+            part = result[:, 2 * u + n, :]
+            nc.gpsimd.tensor_tensor(part, carry[:], source, ALU.subtract)
+            nc.sync.dma_start(out[P * n : P * (n + 1), BANK * u : BANK * (u + 1)], part)
 
-        def both_passes(one_pass, u, n):
-            for b in range(PASSES):
-                one_pass(u, b, n)
+        def sum_on_vector(u, n, part, first=0, last=BANK):
+            nc.vector.tensor_tensor(part, carry_bank[u][n][:, first:last], part, ALU.subtract)
+            queue = nc.scalar if u == 1 else nc.sync
+            queue.dma_start(out[P * n : P * (n + 1), BANK * u + first : BANK * u + last], part)
 
-        carry_out(0)
-        both_passes(carry_pass, 0, 1)
-        carry_out(1)
-        both_passes(carry_pass, 0, 2)
-        carry_out(2)
-        for n in range(3):
-            speech_pass(1, 1, n)
-        for n in range(4):
-            dampen(damped[:, n, :], 0, n)
         for n in range(2):
-            both_passes(carry_pass, 1, n)
+            dampen(damped[n][:], 0, n)
+            both_passes(carry_pass, 0, n + 1)
+        quantize_z(1, 1, own([P, BANK], U32, "z_codes1_1"))
+        for n in range(2):
+            sum_on_gpsimd(0, n, damped[n][:], 20 + 2 * n)
+        dampen(damped[2][:], 0, 2)
         both_passes(carry_pass, 0, 3)
-        carry_out(3)
-        for n in range(4):
-            part = result[:, n, 0 : shared[n]]
-            nc.gpsimd.tensor_tensor(part, carry[n][:, 0 : shared[n]], damped[:, n, 0 : shared[n]], ALU.subtract)
-            nc.sync.dma_start(out[P * n : P * (n + 1), 0 : shared[n]], part)
+        dampen(damped[3][:], 0, 3)
+        speech_pass(1, 1, 0)
+        both_passes(carry_pass, 1, 0)
+        sum_on_vector(0, 2, damped[2][:])
+        dampen(second_half(0), 1, 0)
+        sum_on_vector(0, 3, damped[3][:])
+        for n in (2, 1):
+            speech_pass(1, 1, n)
+        both_passes(carry_pass, 1, 1)
+        both_passes(carry_pass, 1, 2)
         both_passes(speech_pass, 1, 3)
-        for pair in ((0, 1), (2, 3)):
-            for n in pair:
-                dampen(sil_all[:, n, BANK:E], 1, n)
-            if pair[0] == 0:
-                for n in (2, 3):
-                    both_passes(carry_pass, 1, n)
-            for n in pair:
-                part = sil_all[:, n, BANK:E]
-                nc.vector.tensor_tensor(part, carry_bank[1][n][:], part, ALU.subtract)
-                nc.scalar.dma_start(out[P * n : P * (n + 1), BANK:E], part)
-        rest = result[:, 3, HALF:BANK]
-        nc.vector.tensor_tensor(rest, banks[RING][:, HALF:BANK], damped[:, 3, HALF:BANK], ALU.subtract)
-        nc.sync.dma_start(out[3 * P : 4 * P, HALF:BANK], rest)
+        both_passes(carry_pass, 1, 3)
+        for n in (2, 1):
+            dampen(second_half(n), 1, n)
+        for n in range(2):
+            sum_on_gpsimd(1, n, second_half(n), 80 + 2 * n)
+        sum_on_vector(1, 2, second_half(2))
+        halves = ((0, BANK // 2), (BANK // 2, BANK))
+        for first, last in halves:
+            dampen(second_half(3, first, last), 1, 3, first, last)
+        for first, last in halves:
+            sum_on_vector(1, 3, second_half(3, first, last), first, last)

@@ -184,10 +184,13 @@ def tile_list_overlap_track_logits_kernel(tc, tab_words, tab_scales, offs, w1, o
             quantize(z_bf[b, u][:], codes[:], scales[:])
             z_q[b, u] = (codes, scales)
 
-        def round_w3(b, first, last, kib):
-            grouped = place([P, last - first, PACK], BF16, "w3_bf%d_%d" % (b, first), kib)
-            nc.gpsimd.tensor_scalar(grouped[:], w3_raw[:, b, :, first:last].rearrange("p j c -> p c j"), 1.0, 0.0, ALU.mult, ALU.add)
-            return grouped[:].rearrange("p c j -> p (c j)")
+        def round_w3(first, last, kib):
+            grouped = place([P, PASSES, last - first, PACK], BF16, "w3_bf%d" % first, kib)
+            nc.gpsimd.tensor_scalar(grouped[:], w3_raw[:, :, :, first:last].rearrange("p b j c -> p b c j"), 1.0, 0.0, ALU.mult, ALU.add)
+            return grouped
+
+        def quantize_w3(grouped, b, first, last):
+            quantize(grouped[:, b, :, :].rearrange("p c j -> p (c j)"), w3_codes[b][:, first:last], w3_sc[b][:, first:last])
 
         w3_codes = [place([P, N], U32, "w3_codes%d" % b, 32 - 8 * b) for b in range(PASSES)]
         w3_sc = [own([P, N], U8, "w3_sc%d" % b) for b in range(PASSES)]
@@ -226,8 +229,7 @@ def tile_list_overlap_track_logits_kernel(tc, tab_words, tab_scales, offs, w1, o
             silence = sil_all[:, n, BANK * u + first : BANK * u + last]
             nc.vector.scalar_tensor_tensor(dst, silence, 1.0, speech_bank[u][n][:, first:last], ALU.subtract, ALU.mult)
 
-        w3_first = round_w3(0, 0, N, 56)
-        w3_second = round_w3(1, 0, P, 60)
+        w3_wide = round_w3(0, 3 * P, 50)
         for u in range(2):
             sigmoid(0, u)
             gate(0, u)
@@ -237,22 +239,23 @@ def tile_list_overlap_track_logits_kernel(tc, tab_words, tab_scales, offs, w1, o
             speech_pass(0, 0, n)
         for n in range(3):
             speech_pass(1, 0, n)
-        w3_third = round_w3(1, P, N, 0)
+        w3_last = round_w3(3 * P, N, 0)
         sigmoid(1, 0)
         gate(1, 0)
-        quantize(w3_first, w3_codes[0][:], w3_sc[0][:])
+        quantize_w3(w3_wide, 0, 0, 3 * P)
         carry_pass(0, 0, 0)
         quantize_z(1, 0, own([P, BANK], U32, "z_codes1_0"))
         for n in range(4):
             speech_pass(0, 1, n)
-        quantize(w3_second, w3_codes[1][:, 0:P], w3_sc[1][:, 0:P])
-        quantize(w3_third, w3_codes[1][:, P:N], w3_sc[1][:, P:N])
+        quantize_w3(w3_wide, 1, 0, 3 * P)
+        for b in range(PASSES):
+            quantize_w3(w3_last, b, 3 * P, N)
         carry_pass(0, 1, 0)
 
         planes = [place([P, 2, BANK], F32, "sig1_1_%d" % e, 16 + 4 * e) for e in range(2)]
         for e in range(2):
             nc.scalar.activation(planes[e][:], x[1][:, e:PACK:2, BANK:E], ACT.Sigmoid)
-        pairs = place([P, 2, BANK, 2], BF16, "pairs", 48)
+        pairs = place([P, 2, BANK, 2], BF16, "pairs", 56)
         for t in (0, 2, 1, 3):
             nc.scalar.activation(pairs[:, t // 2, :, t % 2], planes[t % 2][:, t // 2, :], ACT.Copy, scale=gain_last[:, t, :])
         z_bf[1, 1] = place([P, PACK * BANK], BF16, "z_bf1_1", 12)
@@ -261,7 +264,7 @@ def tile_list_overlap_track_logits_kernel(tc, tab_words, tab_scales, offs, w1, o
             pairs[:].rearrange("p u c e -> p (u c e)").bitcast(U32).rearrange("p (u c i) -> p c u i", i=4, u=2),
         )
 
-        damped = [place([P, BANK], F32, "damped%d" % n, kib) for n, kib in enumerate((66, 68, 48, 50))]
+        damped = [place([P, BANK], F32, "damped%d" % n, kib) for n, kib in enumerate((66, 68, 56, 58))]
         result = place([P, N // P, BANK], F32, "result", 8)
 
         def second_half(n, first=0, last=BANK):

@@ -28,6 +28,7 @@ FIRST_SCALE_ROW = P - SCALE_ROWS
 FIRST_GAIN_ROW = P - PASSES
 PIECE = 256
 RING = 7
+SHARE = 256
 
 
 def tile_list_overlap_track_logits_kernel(tc, tab_words, tab_scales, offs, w1, offs2, wgt, gain, w2_words, w2_scales, sil, w3, out):
@@ -270,12 +271,12 @@ def tile_list_overlap_track_logits_kernel(tc, tab_words, tab_scales, offs, w1, o
         def second_half(n, first=0, last=BANK):
             return sil_all[:, n, BANK + first : BANK + last]
 
-        def sum_on_gpsimd(u, n, source, kib):
-            carry = place([P, BANK], F32, "carry%d_%d" % (u, n), kib)
-            nc.scalar.copy(carry[:], carry_bank[u][n][:])
-            part = result[:, 2 * u + n, :]
+        def sum_on_gpsimd(u, n, source, kib, last=BANK):
+            carry = place([P, last], F32, "carry%d_%d" % (u, n), kib)
+            nc.scalar.copy(carry[:], carry_bank[u][n][:, 0:last])
+            part = result[:, 2 * u + n, 0:last]
             nc.gpsimd.tensor_tensor(part, carry[:], source, ALU.subtract)
-            nc.sync.dma_start(out[P * n : P * (n + 1), BANK * u : BANK * (u + 1)], part)
+            nc.sync.dma_start(out[P * n : P * (n + 1), BANK * u : BANK * u + last], part)
 
         def sum_on_vector(u, n, part, first=0, last=BANK):
             nc.vector.tensor_tensor(part, carry_bank[u][n][:, first:last], part, ALU.subtract)
@@ -304,11 +305,12 @@ def tile_list_overlap_track_logits_kernel(tc, tab_words, tab_scales, offs, w1, o
         both_passes(carry_pass, 1, 3)
         for n in (2, 1):
             dampen(second_half(n), 1, n)
-        for n in range(2):
-            sum_on_gpsimd(1, n, second_half(n), 80 + 2 * n)
+        sum_on_gpsimd(1, 0, second_half(0), 80)
+        sum_on_gpsimd(1, 1, second_half(1, 0, SHARE), 82, SHARE)
         sum_on_vector(1, 2, second_half(2))
         halves = ((0, BANK // 2), (BANK // 2, BANK))
         for first, last in halves:
             dampen(second_half(3, first, last), 1, 3, first, last)
+        sum_on_vector(1, 1, second_half(1, SHARE, BANK), SHARE, BANK)
         for first, last in halves:
             sum_on_vector(1, 3, second_half(3, first, last), first, last)

@@ -196,7 +196,7 @@ def tile_list_overlap_track_logits_kernel(tc, tab_words, tab_scales, offs, w1, o
         w3_codes = [place([P, N], U32, "w3_codes%d" % b, 32 - 8 * b) for b in range(PASSES)]
         w3_sc = [own([P, N], U8, "w3_sc%d" % b) for b in range(PASSES)]
         speech_bank = [[banks[k] for k in (0, 1, 2, 3)], [banks[k] for k in (4, 5, 6, 3)]]
-        carry_bank = [[banks[k] for k in (RING, 0, 1, 2)], [banks[k] for k in (RING, 0, 1, 2)]]
+        carry_bank = [[banks[k] for k in (RING, 1, 2, 0)]] * 2
 
         def speech_pass(u, b, n):
             codes, scales = z_q[b, u]
@@ -246,7 +246,7 @@ def tile_list_overlap_track_logits_kernel(tc, tab_words, tab_scales, offs, w1, o
         quantize_w3(w3_wide, 0, 0, 3 * P)
         carry_pass(0, 0, 0)
         quantize_z(1, 0, own([P, BANK], U32, "z_codes1_0"))
-        for n in range(4):
+        for n in (1, 2, 0, 3):
             speech_pass(0, 1, n)
         quantize_w3(w3_wide, 1, 0, 3 * P)
         for b in range(PASSES):
@@ -261,12 +261,12 @@ def tile_list_overlap_track_logits_kernel(tc, tab_words, tab_scales, offs, w1, o
             nc.scalar.activation(pairs[:, t // 2, :, t % 2], planes[t % 2][:, t // 2, :], ACT.Copy, scale=gain_last[:, t, :])
         z_bf[1, 1] = place([P, PACK * BANK], BF16, "z_bf1_1", 12)
         nc.scalar.copy(
-            z_bf[1, 1][:].bitcast(U32).rearrange("p (c i u) -> p c u i", i=4, u=2),
-            pairs[:].rearrange("p u c e -> p (u c e)").bitcast(U32).rearrange("p (u c i) -> p c u i", i=4, u=2),
+            z_bf[1, 1][:].bitcast(U32).rearrange("p (c i u) -> p c u i", i=2, u=2),
+            pairs[:].rearrange("p u c e -> p (u c e)").bitcast(U32).rearrange("p (u c i) -> p c u i", i=2, u=2),
         )
 
-        damped = [place([P, BANK], F32, "damped%d" % n, kib) for n, kib in enumerate((66, 68, 56, 58))]
-        result = place([P, N // P, BANK], F32, "result", 8)
+        damped = [place([P, BANK], F32, "damped%d" % n, kib) for n, kib in enumerate((66, 68, 70, 56))]
+        result = place([P, N // P, BANK], F32, "result", 72)
 
         def second_half(n, first=0, last=BANK):
             return sil_all[:, n, BANK + first : BANK + last]
@@ -280,17 +280,15 @@ def tile_list_overlap_track_logits_kernel(tc, tab_words, tab_scales, offs, w1, o
 
         def sum_on_vector(u, n, part, first=0, last=BANK):
             nc.vector.tensor_tensor(part, carry_bank[u][n][:, first:last], part, ALU.subtract)
-            queue = nc.scalar if u == 1 else nc.sync
+            queue = nc.sync if (u, n) == (0, 3) else nc.scalar
             queue.dma_start(out[P * n : P * (n + 1), BANK * u + first : BANK * u + last], part)
 
-        for n in range(2):
+        for n, freed_for in ((1, 1), (2, 2), (0, 3)):
             dampen(damped[n][:], 0, n)
-            both_passes(carry_pass, 0, n + 1)
+            both_passes(carry_pass, 0, freed_for)
         quantize_z(1, 1, own([P, BANK], U32, "z_codes1_1"))
         for n in range(2):
             sum_on_gpsimd(0, n, damped[n][:], 20 + 2 * n)
-        dampen(damped[2][:], 0, 2)
-        both_passes(carry_pass, 0, 3)
         dampen(damped[3][:], 0, 3)
         speech_pass(1, 1, 0)
         both_passes(carry_pass, 1, 0)

@@ -29,6 +29,7 @@ FIRST_GAIN_ROW = P - PASSES
 PIECE = 256
 RING = 7
 SHARE = 256
+GATED = 448
 
 
 def tile_list_overlap_track_logits_kernel(tc, tab_words, tab_scales, offs, w1, offs2, wgt, gain, w2_words, w2_scales, sil, w3, out):
@@ -170,14 +171,28 @@ def tile_list_overlap_track_logits_kernel(tc, tab_words, tab_scales, offs, w1, o
             sig[b, u] = place([P, PACK, BANK], F32, "sig%d_%d" % (b, u), 8 * (5 - 2 * b - u))
             nc.scalar.activation(sig[b, u][:], x[b][:, :, BANK * u : BANK * (u + 1)], ACT.Sigmoid)
 
-        def gate(b, u):
+        def gate(b, u, last=BANK):
             row = FIRST_GAIN_ROW + b
-            z_bf[b, u] = place([P, PACK * BANK], BF16, "z_bf%d_%d" % (b, u), 4 * (2 * b + u))
             nc.vector.tensor_tensor(
-                z_bf[b, u][:].rearrange("p (c i t) -> p c t i", i=4, t=PACK),
-                sig[b, u][:].rearrange("p t (c i) -> p c t i", i=4),
-                gain_bank[:, :, row : row + 1].rearrange("p t o -> p o t").unsqueeze(3).to_broadcast([P, BANK // 4, PACK, 4]),
+                z_bf[b, u][:, 0 : PACK * last].rearrange("p (c i t) -> p c t i", i=4, t=PACK),
+                sig[b, u][:, :, 0:last].rearrange("p t (c i) -> p c t i", i=4),
+                gain_bank[:, :, row : row + 1].rearrange("p t o -> p o t").unsqueeze(3).to_broadcast([P, last // 4, PACK, 4]),
                 ALU.mult,
+            )
+
+        def grouped_tile(b, u):
+            z_bf[b, u] = place([P, PACK * BANK], BF16, "z_bf%d_%d" % (b, u), 4 * (2 * b + u))
+
+        def gate_on_scalar(plane, width, name, kib):
+            pairs = place([P, 2, width, 2], BF16, name, kib)
+            for t in (0, 2, 1, 3):
+                nc.scalar.activation(pairs[:, t // 2, :, t % 2], plane(t), ACT.Copy, scale=gain_last[:, t, :])
+            return pairs
+
+        def join(grouped, pairs):
+            nc.scalar.copy(
+                grouped.bitcast(U32).rearrange("p (c i u) -> p c u i", i=2, u=2),
+                pairs[:].rearrange("p u c e -> p (u c e)").bitcast(U32).rearrange("p (u c i) -> p c u i", i=2, u=2),
             )
 
         def quantize_z(b, u, codes):
@@ -233,6 +248,7 @@ def tile_list_overlap_track_logits_kernel(tc, tab_words, tab_scales, offs, w1, o
         w3_wide = round_w3(0, 3 * P, 50)
         for u in range(2):
             sigmoid(0, u)
+            grouped_tile(0, u)
             gate(0, u)
         quantize_z(0, 0, place([P, BANK], U32, "z_codes0_0", 64))
         quantize_z(0, 1, own([P, BANK], U32, "z_codes0_1"))
@@ -242,28 +258,27 @@ def tile_list_overlap_track_logits_kernel(tc, tab_words, tab_scales, offs, w1, o
             speech_pass(1, 0, n)
         w3_last = round_w3(3 * P, N, 0)
         sigmoid(1, 0)
-        gate(1, 0)
+        grouped_tile(1, 0)
+        gate(1, 0, GATED)
+        few_pairs = gate_on_scalar(lambda t: sig[1, 0][:, t, GATED:BANK], BANK - GATED, "few_pairs", 60)
+        planes = [place([P, 2, BANK], F32, "sig1_1_%d" % e, 16 + 4 * e) for e in range(2)]
+        nc.scalar.activation(planes[0][:], x[1][:, 0:PACK:2, BANK:E], ACT.Sigmoid)
+        join(z_bf[1, 0][:, PACK * GATED : PACK * BANK], few_pairs)
+        nc.scalar.activation(planes[1][:], x[1][:, 1:PACK:2, BANK:E], ACT.Sigmoid)
         quantize_w3(w3_wide, 0, 0, 3 * P)
         carry_pass(0, 0, 0)
         quantize_z(1, 0, own([P, BANK], U32, "z_codes1_0"))
-        for n in (1, 2, 0, 3):
+        for n in (1, 2, 0):
             speech_pass(0, 1, n)
         quantize_w3(w3_wide, 1, 0, 3 * P)
+        carry_pass(0, 1, 0)
+        speech_pass(0, 1, 3)
         for b in range(PASSES):
             quantize_w3(w3_last, b, 3 * P, N)
-        carry_pass(0, 1, 0)
 
-        planes = [place([P, 2, BANK], F32, "sig1_1_%d" % e, 16 + 4 * e) for e in range(2)]
-        for e in range(2):
-            nc.scalar.activation(planes[e][:], x[1][:, e:PACK:2, BANK:E], ACT.Sigmoid)
-        pairs = place([P, 2, BANK, 2], BF16, "pairs", 56)
-        for t in (0, 2, 1, 3):
-            nc.scalar.activation(pairs[:, t // 2, :, t % 2], planes[t % 2][:, t // 2, :], ACT.Copy, scale=gain_last[:, t, :])
-        z_bf[1, 1] = place([P, PACK * BANK], BF16, "z_bf1_1", 12)
-        nc.scalar.copy(
-            z_bf[1, 1][:].bitcast(U32).rearrange("p (c i u) -> p c u i", i=2, u=2),
-            pairs[:].rearrange("p u c e -> p (u c e)").bitcast(U32).rearrange("p (u c i) -> p c u i", i=2, u=2),
-        )
+        pairs = gate_on_scalar(lambda t: planes[t % 2][:, t // 2, :], BANK, "pairs", 56)
+        grouped_tile(1, 1)
+        join(z_bf[1, 1][:], pairs)
 
         damped = [place([P, BANK], F32, "damped%d" % n, kib) for n, kib in enumerate((66, 68, 70, 56))]
         result = place([P, N // P, BANK], F32, "result", 72)
@@ -283,15 +298,17 @@ def tile_list_overlap_track_logits_kernel(tc, tab_words, tab_scales, offs, w1, o
             queue = nc.sync if (u, n) == (0, 3) else nc.scalar
             queue.dma_start(out[P * n : P * (n + 1), BANK * u + first : BANK * u + last], part)
 
-        for n, freed_for in ((1, 1), (2, 2), (0, 3)):
+        for n in (1, 2):
             dampen(damped[n][:], 0, n)
-            both_passes(carry_pass, 0, freed_for)
+            both_passes(carry_pass, 0, n)
+        dampen(damped[0][:], 0, 0)
         quantize_z(1, 1, own([P, BANK], U32, "z_codes1_1"))
         for n in range(2):
             sum_on_gpsimd(0, n, damped[n][:], 20 + 2 * n)
         dampen(damped[3][:], 0, 3)
         speech_pass(1, 1, 0)
         both_passes(carry_pass, 1, 0)
+        both_passes(carry_pass, 0, 3)
         sum_on_vector(0, 2, damped[2][:])
         dampen(second_half(0), 1, 0)
         sum_on_vector(0, 3, damped[3][:])

@@ -80,9 +80,8 @@ def tile_list_overlap_track_logits_kernel(tc, tab_words, tab_scales, offs, w1, o
         picked_sc = place([P, S], U8, "picked_sc", 116)
         nc.gpsimd.memset(v_sc[:].bitcast(I32), 0)
         nc.vector.tensor_copy(picked_sc[:], table_sc[:].indirect(frames[:]))
-        for q in range(4):
-            first = FIRST_SCALE_ROW + 4 * q
-            nc.scalar.dma_start(v_sc[32 * q : 32 * q + 4, :].bitcast(I32), picked_sc[first : first + 4, :].bitcast(I32))
+        for r in range(4):
+            nc.scalar.dma_start(v_sc[r:P:32, :].bitcast(I32), picked_sc[FIRST_SCALE_ROW + r : P : 4, :].bitcast(I32))
 
         v_codes = []
 

@@ -204,11 +204,18 @@ def tile_list_overlap_track_logits_kernel(tc, tab_words, tab_scales, offs, w1, o
             nc.gpsimd.tensor_scalar(grouped[:], w3_raw[:, :, :, first:last].rearrange("p b j c -> p b c j"), 1.0, 0.0, ALU.mult, ALU.add)
             return grouped
 
-        def quantize_w3(grouped, b, first, last):
-            quantize(grouped[:, b, :, :].rearrange("p c j -> p (c j)"), w3_codes[b][:, first:last], w3_sc[b][:, first:last])
+        def quantize_w3(grouped, operands, kib):
+            name = "%d_%d" % operands[0]
+            codes = place([P, P * len(operands)], U32, "w3_codes" + name, kib)
+            scales = own([P, P * len(operands)], U8, "w3_sc" + name)
+            quantize(grouped, codes[:], scales[:])
+            for k, operand in enumerate(operands):
+                w3_q[operand] = (codes[:, P * k : P * (k + 1)], scales[:, P * k : P * (k + 1)])
 
-        w3_codes = [place([P, N], U32, "w3_codes%d" % b, 32 - 8 * b) for b in range(PASSES)]
-        w3_sc = [own([P, N], U8, "w3_sc%d" % b) for b in range(PASSES)]
+        def quantize_wide(b, kib):
+            quantize_w3(w3_wide[:, b, :, :].rearrange("p c j -> p (c j)"), [(b, n) for n in range(3)], kib)
+
+        w3_q = {}
         speech_bank = [[banks[k] for k in (0, 1, 2, 3)], [banks[k] for k in (4, 5, 6, 3)]]
         carry_bank = [[banks[k] for k in (RING, 1, 2, 0)]] * 2
 
@@ -226,10 +233,11 @@ def tile_list_overlap_track_logits_kernel(tc, tab_words, tab_scales, offs, w1, o
 
         def carry_pass(u, b, n):
             codes, scales = z_q[b, u]
+            w_codes, w_scales = w3_q[b, n]
             nc.tensor.matmul_mx(
                 out=carry_bank[u][n][:],
-                lhsT=w3_codes[b][:, P * n : P * (n + 1)].bitcast(FP8X4),
-                lhsT_scale=w3_sc[b][:, P * n : P * (n + 1)],
+                lhsT=w_codes.bitcast(FP8X4),
+                lhsT_scale=w_scales,
                 rhs=codes[:].bitcast(FP8X4),
                 rhs_scale=scales[:],
                 start=(b == 0),
@@ -264,16 +272,15 @@ def tile_list_overlap_track_logits_kernel(tc, tab_words, tab_scales, offs, w1, o
         nc.scalar.activation(planes[0][:], x[1][:, 0:PACK:2, BANK:E], ACT.Sigmoid)
         join(z_bf[1, 0][:, PACK * GATED : PACK * BANK], few_pairs)
         nc.scalar.activation(planes[1][:], x[1][:, 1:PACK:2, BANK:E], ACT.Sigmoid)
-        quantize_w3(w3_wide, 0, 0, 3 * P)
+        quantize_wide(0, 32)
         carry_pass(0, 0, 0)
         quantize_z(1, 0, own([P, BANK], U32, "z_codes1_0"))
         for n in (1, 2, 0):
             speech_pass(0, 1, n)
-        quantize_w3(w3_wide, 1, 0, 3 * P)
+        quantize_wide(1, 24)
         carry_pass(0, 1, 0)
         speech_pass(0, 1, 3)
-        for b in range(PASSES):
-            quantize_w3(w3_last, b, 3 * P, N)
+        quantize_w3(w3_last[:].rearrange("p b c j -> p (b c j)"), [(b, 3) for b in range(PASSES)], 26)
 
         pairs = gate_on_scalar(lambda t: planes[t % 2][:, t // 2, :], BANK, "pairs", 56)
         grouped_tile(1, 1)
@@ -293,7 +300,7 @@ def tile_list_overlap_track_logits_kernel(tc, tab_words, tab_scales, offs, w1, o
             nc.sync.dma_start(out[P * n : P * (n + 1), BANK * u : BANK * u + last], part)
 
         def sum_on_vector(u, n, part, first=0, last=BANK):
-            nc.vector.tensor_tensor(part, carry_bank[u][n][:, first:last], part, ALU.subtract)
+            nc.vector.scalar_tensor_tensor(part, part, -1.0, carry_bank[u][n][:, first:last], ALU.mult, ALU.add)
             queue = nc.sync if (u, n) == (0, 3) else nc.scalar
             queue.dma_start(out[P * n : P * (n + 1), BANK * u + first : BANK * u + last], part)
 
@@ -323,8 +330,7 @@ def tile_list_overlap_track_logits_kernel(tc, tab_words, tab_scales, offs, w1, o
         sum_on_gpsimd(1, 1, second_half(1, 0, SHARE), 82, SHARE)
         sum_on_vector(1, 2, second_half(2))
         halves = ((0, BANK // 2), (BANK // 2, BANK))
-        for first, last in halves:
-            dampen(second_half(3, first, last), 1, 3, first, last)
+        dampen(second_half(3), 1, 3)
         sum_on_vector(1, 1, second_half(1, SHARE, BANK), SHARE, BANK)
         for first, last in halves:
             sum_on_vector(1, 3, second_half(3, first, last), first, last)

@@ -29,7 +29,8 @@ FIRST_GAIN_ROW = P - PASSES
 PIECE = 256
 RING = 7
 SHARE = 256
-GATED = 448
+GATED = 480
+LEFT = 32
 
 
 def tile_list_overlap_track_logits_kernel(tc, tab_words, tab_scales, offs, w1, offs2, wgt, gain, w2_words, w2_scales, sil, w3, out):
@@ -199,9 +200,10 @@ def tile_list_overlap_track_logits_kernel(tc, tab_words, tab_scales, offs, w1, o
             quantize(z_bf[b, u][:], codes[:], scales[:])
             z_q[b, u] = (codes, scales)
 
-        def round_w3(first, last, kib):
+        def round_w3(first, last, kib, left=0):
             grouped = place([P, PASSES, last - first, PACK], BF16, "w3_bf%d" % first, kib)
-            nc.gpsimd.tensor_scalar(grouped[:], w3_raw[:, :, :, first:last].rearrange("p b j c -> p b c j"), 1.0, 0.0, ALU.mult, ALU.add)
+            rows = w3_raw[:, :, :, first : last - left].rearrange("p b j c -> p b c j")
+            nc.gpsimd.tensor_scalar(grouped[:, :, 0 : last - left - first, :], rows, 1.0, 0.0, ALU.mult, ALU.add)
             return grouped
 
         def quantize_w3(grouped, operands, kib):
@@ -252,7 +254,7 @@ def tile_list_overlap_track_logits_kernel(tc, tab_words, tab_scales, offs, w1, o
             silence = sil_all[:, n, BANK * u + first : BANK * u + last]
             nc.vector.scalar_tensor_tensor(dst, silence, 1.0, speech_bank[u][n][:, first:last], ALU.subtract, ALU.mult)
 
-        w3_wide = round_w3(0, 3 * P, 50)
+        w3_wide = round_w3(0, 3 * P, 50, LEFT)
         for u in range(2):
             sigmoid(0, u)
             grouped_tile(0, u)
@@ -271,6 +273,10 @@ def tile_list_overlap_track_logits_kernel(tc, tab_words, tab_scales, offs, w1, o
         planes = [place([P, 2, BANK], F32, "sig1_1_%d" % e, 16 + 4 * e) for e in range(2)]
         nc.scalar.activation(planes[0][:], x[1][:, 0:PACK:2, BANK:E], ACT.Sigmoid)
         join(z_bf[1, 0][:, PACK * GATED : PACK * BANK], few_pairs)
+        nc.scalar.copy(
+            w3_wide[:, :, 3 * P - LEFT : 3 * P, :].rearrange("p b (c i) j -> p b c j i", i=4),
+            w3_raw[:, :, :, 3 * P - LEFT : 3 * P].rearrange("p b j (c i) -> p b c j i", i=4),
+        )
         nc.scalar.activation(planes[1][:], x[1][:, 1:PACK:2, BANK:E], ACT.Sigmoid)
         quantize_wide(0, 32)
         carry_pass(0, 0, 0)

@@ -30,7 +30,7 @@ PIECE = 256
 RING = 7
 SHARE = 256
 GATED = 480
-LEFT = 32
+LEFT = 48
 
 
 def tile_list_overlap_track_logits_kernel(tc, tab_words, tab_scales, offs, w1, offs2, wgt, gain, w2_words, w2_scales, sil, w3, out):

@@ -110,8 +110,8 @@ def tile_list_overlap_track_logits_kernel(tc, tab_words, tab_scales, offs, w1, o
         quantize(w1_bf[0][:, BANK : 4 * BANK], w1_codes[0][:, P : 4 * P], w1_sc[0][:, P : 4 * P])
 
         nc.vector.tensor_copy(
-            w1_bf[1][:].rearrange("p (t m j) -> p m j t", t=PACK, j=PACK)[:, 64:P, :, :],
-            w1_raw[3][:].rearrange("p j (m t) -> p m j t", t=PACK),
+            w1_bf[1][:].rearrange("p (t m j) -> p m t j", t=PACK, j=PACK)[:, 64:P, :, :],
+            w1_raw[3][:].rearrange("p j (m t) -> p m t j", t=PACK),
         )
 
         w3_raw = place([P, PASSES, PACK, N], F32, "w3_raw", 96)

@@ -25,7 +25,7 @@ LIST = 16
 KIB = 1024
 SCALE_ROWS = K // 32
 FIRST_SCALE_ROW = P - SCALE_ROWS
-FIRST_GAIN_ROW = P - PASSES
+FIRST_GAIN_ROW = P // 2 - PASSES
 PIECE = 256
 RING = 7
 SHARE = 256
@@ -55,7 +55,7 @@ def tile_list_overlap_track_logits_kernel(tc, tab_words, tab_scales, offs, w1, o
         nc.vector.memset(table_sc[0:FIRST_SCALE_ROW, :].bitcast(I32), 0)
         nc.sync.dma_start(table_sc[FIRST_SCALE_ROW:P, :].bitcast(I32), tab_scales[0].bitcast(I32))
         gain_rows = own([P, BANK], F32, "gain_rows")
-        nc.scalar.dma_start(gain_rows[FIRST_GAIN_ROW:P, :], gain.rearrange("(b c) -> b c", b=PASSES))
+        nc.scalar.dma_start(gain_rows[FIRST_GAIN_ROW : P // 2, :], gain.rearrange("(b c) -> b c", b=PASSES))
         nc.sync.dma_start(frames[:], offs)
         nc.sync.dma_start(table[:].bitcast(I32), tab_words[0].rearrange("p t i -> p (t i)").bitcast(I32))
         nc.sync.dma_start(picks[:], offs2)
@@ -71,11 +71,12 @@ def tile_list_overlap_track_logits_kernel(tc, tab_words, tab_scales, offs, w1, o
         ident = own([P, P], F32, "ident")
         make_identity(nc, ident[:])
         nc.gpsimd.memset(gain_rows[0:FIRST_GAIN_ROW, :], 0)
+        nc.gpsimd.memset(gain_rows[P // 2 : P, :], 0)
         gain_bank = banks[RING][:].rearrange("p (t q) -> p t q", t=PACK)
         for t in range(PACK):
             nc.tensor.transpose(gain_bank[:, t, :], gain_rows[:, t:BANK:PACK], ident[:])
         gain_last = own([P, PACK, 1], F32, "gain_last")
-        nc.scalar.copy(gain_last[:], gain_bank[:, :, P - 1 : P])
+        nc.scalar.copy(gain_last[:], gain_bank[:, :, FIRST_GAIN_ROW + 1 : FIRST_GAIN_ROW + 2])
 
         v_sc = own([P, S], U8, "v_sc")
         picked_sc = place([P, S], U8, "picked_sc", 116)

from contextlib import ExitStack

import concourse.mybir as mybir
from concourse.masks import make_identity

T, S, E, K, H, N = 4096, 2048, 1024, 512, 1024, 512
FLOPS = 2 * K * H * S + 2 * 2 * H * N * E

F32 = mybir.dt.float32
BF16 = mybir.dt.bfloat16
I32 = mybir.dt.int32
U32 = mybir.dt.uint32
U16 = mybir.dt.uint16
U8 = mybir.dt.uint8
FP8X4 = mybir.dt.float8_e4m3fn_x4
FP4X4 = mybir.dt.float4_e2m1fn_x4
ALU = mybir.AluOpType
ACT = mybir.ActivationFunctionType

P = 128
PACK = 4
BANK = 512
PASSES = H // (P * PACK)
LIST = 16
KIB = 1024
SCALE_ROWS = K // 32
FIRST_SCALE_ROW = P - SCALE_ROWS
FIRST_GAIN_ROW = P // 2 - PASSES
PIECE = 256
RING = 7
SHARE = 256
GATED = 480
LEFT = 48


def tile_list_overlap_track_logits_kernel(tc, tab_words, tab_scales, offs, w1, offs2, wgt, gain, w2_words, w2_scales, sil, w3, out):
    nc = tc.nc
    with ExitStack() as ctx:
        keep = ctx.enter_context(tc.tile_pool(name="keep", bufs=1))
        arena = ctx.enter_context(tc.tile_pool(name="arena", bufs=1))
        psum = ctx.enter_context(tc.psum_pool(name="psum", bufs=1))

        def place(shape, dtype, name, kib):
            return arena.tile(shape, dtype, name=name, offset=kib * KIB, align_bytes=64)

        def own(shape, dtype, name):
            return keep.tile(shape, dtype, name=name, align_bytes=64)

        frames = keep.tile([P, S // LIST], U16, name="frames")
        picks = keep.tile([P, E // LIST], U16, name="picks")
        table = place([P, T], U32, "table", 96)
        table_sc = place([P, T], U8, "table_sc", 112)
        banks = [psum.tile([P, BANK], F32, name="bank%d" % k) for k in range(8)]

        nc.vector.memset(table_sc[0:FIRST_SCALE_ROW, :].bitcast(I32), 0)
        nc.sync.dma_start(table_sc[FIRST_SCALE_ROW:P, :].bitcast(I32), tab_scales[0].bitcast(I32))
        gain_rows = own([P, BANK], F32, "gain_rows")
        nc.scalar.dma_start(gain_rows[FIRST_GAIN_ROW : P // 2, :], gain.rearrange("(b c) -> b c", b=PASSES))
        nc.sync.dma_start(frames[:], offs)
        nc.sync.dma_start(table[:].bitcast(I32), tab_words[0].rearrange("p t i -> p (t i)").bitcast(I32))
        nc.sync.dma_start(picks[:], offs2)
        w1_rows = w1.rearrange("(p j) c -> p j c", j=PACK)
        w1_raw = [place([P, PACK, PIECE], F32, "w1_raw%d" % u, kib) for u, kib in enumerate((152, 122, 126, 154))]
        for u in range(3):
            nc.sync.dma_start(w1_raw[u][:], w1_rows[:, :, PIECE * u : PIECE * (u + 1)])

        warm = keep.tile([P, 1], F32, name="warm")
        nc.gpsimd.memset(warm[:], 0)
        nc.scalar.activation(warm[:], warm[:], ACT.Sigmoid)

        ident = own([P, P], F32, "ident")
        make_identity(nc, ident[:])
        nc.gpsimd.memset(gain_rows[0:FIRST_GAIN_ROW, :], 0)
        nc.gpsimd.memset(gain_rows[P // 2 : P, :], 0)
        gain_bank = banks[RING][:].rearrange("p (t q) -> p t q", t=PACK)
        for t in range(PACK):
            nc.tensor.transpose(gain_bank[:, t, :], gain_rows[:, t:BANK:PACK], ident[:])
        gain_last = own([P, PACK, 1], F32, "gain_last")
        nc.scalar.copy(gain_last[:], gain_bank[:, :, FIRST_GAIN_ROW + 1 : FIRST_GAIN_ROW + 2])

        v_sc = own([P, S], U8, "v_sc")
        picked_sc = place([P, S], U8, "picked_sc", 116)
        nc.gpsimd.memset(v_sc[:].bitcast(I32), 0)
        nc.vector.tensor_copy(picked_sc[:], table_sc[:].indirect(frames[:]))
        for r in range(4):
            nc.scalar.dma_start(v_sc[r:P:32, :].bitcast(I32), picked_sc[FIRST_SCALE_ROW + r : P : 4, :].bitcast(I32))

        v_codes = []

        def gather_words(j, words):
            nc.vector.tensor_copy(words[:], table[:].indirect(frames[:, j * BANK // LIST : (j + 1) * BANK // LIST]))
            v_codes.append(words)

        def quantize(grouped, codes, scales):
            nc.vector.quantize_mx(out=codes.bitcast(FP8X4), scales=scales, in_=grouped)

        w1_bf = [place([P, PACK * BANK], BF16, "w1_bf%d" % b, 134 + 24 * b) for b in range(PASSES)]
        w1_codes = [own([P, BANK], U32, "w1_codes%d" % b) for b in range(PASSES)]
        w1_sc = [own([P, BANK], U8, "w1_sc%d" % b) for b in range(PASSES)]
        for u in range(3):
            b, half = divmod(u, 2)
            view = w1_bf[b][:].rearrange("p (t m j) -> p m j t", t=PACK, j=PACK)
            nc.scalar.copy(view[:, 64 * half : 64 * (half + 1), :, :], w1_raw[u][:].rearrange("p j (m t) -> p m j t", t=PACK))
        nc.sync.dma_start(w1_raw[3][:], w1_rows[:, :, 3 * PIECE : 4 * PIECE])
        wgt_sb = place([P, E], F32, "wgt_sb", 150)
        nc.sync.dma_start(wgt_sb[:], wgt)
        for j in range(3):
            gather_words(j, own([P, BANK], U32, "v_codes%d" % j))
        quantize(w1_bf[0][:, 0:BANK], w1_codes[0][:, 0:P], w1_sc[0][:, 0:P])
        gather_words(3, place([P, BANK], U32, "v_codes3", 122))
        quantize(w1_bf[0][:, BANK : 4 * BANK], w1_codes[0][:, P : 4 * P], w1_sc[0][:, P : 4 * P])

        nc.vector.tensor_copy(
            w1_bf[1][:].rearrange("p (t m j) -> p m t j", t=PACK, j=PACK)[:, 64:P, :, :],
            w1_raw[3][:].rearrange("p j (m t) -> p m t j", t=PACK),
        )

        w3_raw = place([P, PASSES, PACK, N], F32, "w3_raw", 96)
        nc.sync.dma_start(w3_raw[:].rearrange("p b j c -> p b (j c)"), w3.rearrange("(b p j) c -> p b (j c)", b=PASSES, j=PACK))
        w2_codes = place([P, PASSES, 2 * N], U8, "w2_codes", 126)
        nc.sync.dma_start(w2_codes[:].bitcast(I32), w2_words.rearrange("a p c -> p a c").bitcast(I32))
        w2_sc = place([P, PASSES, N], U8, "w2_sc", 158)
        nc.gpsimd.memset(w2_sc[:].rearrange("p a c -> p (a c)").bitcast(I32), 0)
        for q in range(4):
            nc.sync.dma_start(w2_sc[32 * q : 32 * q + 4, :, :].bitcast(I32), w2_scales[:, 4 * q : 4 * q + 4, :].rearrange("a r c -> r a c").bitcast(I32))
        sil_all = place([P, N // P, E], F32, "sil_all", 160)
        nc.sync.dma_start(sil_all[:], sil.rearrange("(n p) m -> p n m", p=P))

        h = [place([P, S], F32, "h%d" % i, 8 * i) for i in range(PASSES * PACK)]

        def first_products(i):
            b, t = divmod(i, PACK)
            for j in range(4):
                nc.tensor.matmul_mx(
                    out=banks[(PACK * i + j) % RING][:],
                    lhsT=w1_codes[b][:, P * t : P * (t + 1)].bitcast(FP8X4),
                    lhsT_scale=w1_sc[b][:, P * t : P * (t + 1)],
                    rhs=v_codes[j][:].bitcast(FP8X4),
                    rhs_scale=v_sc[:, BANK * j : BANK * (j + 1)],
                    start=True,
                    stop=True,
                )

        def copy_h(i, order):
            for j in order:
                nc.scalar.copy(h[i][:, BANK * j : BANK * (j + 1)], banks[(PACK * i + j) % RING][:])

        x = [place([P, PACK, E], F32, "x%d" % b, 64 + 16 * b) for b in range(PASSES)]

        def pick(i):
            b, t = divmod(i, PACK)
            nc.vector.tensor_tensor(x[b][:, t, :], h[i][:].indirect(picks[:]), wgt_sb[:], ALU.mult)

        last_first = [3, 0, 1, 2]
        first_products(0)
        copy_h(0, range(4))
        quantize(w1_bf[1][:], w1_codes[1][:], w1_sc[1][:])
        pick(0)
        first_products(1)
        copy_h(1, range(4))
        pick(1)
        for i in range(2, 8):
            first_products(i)
            copy_h(i, last_first)
            pick(i)

        sig = {}
        z_bf = {}
        z_q = {}

        def sigmoid(b, u):
            sig[b, u] = place([P, PACK, BANK], F32, "sig%d_%d" % (b, u), 8 * (5 - 2 * b - u))
            nc.scalar.activation(sig[b, u][:], x[b][:, :, BANK * u : BANK * (u + 1)], ACT.Sigmoid)

        def gate(b, u, last=BANK):
            row = FIRST_GAIN_ROW + b
            nc.vector.tensor_tensor(
                z_bf[b, u][:, 0 : PACK * last].rearrange("p (c i t) -> p c t i", i=4, t=PACK),
                sig[b, u][:, :, 0:last].rearrange("p t (c i) -> p c t i", i=4),
                gain_bank[:, :, row : row + 1].rearrange("p t o -> p o t").unsqueeze(3).to_broadcast([P, last // 4, PACK, 4]),
                ALU.mult,
            )

        def grouped_tile(b, u):
            z_bf[b, u] = place([P, PACK * BANK], BF16, "z_bf%d_%d" % (b, u), 4 * (2 * b + u))

        def gate_on_scalar(plane, width, name, kib):
            pairs = place([P, 2, width, 2], BF16, name, kib)
            for t in (0, 2, 1, 3):
                nc.scalar.activation(pairs[:, t // 2, :, t % 2], plane(t), ACT.Copy, scale=gain_last[:, t, :])
            return pairs

        def join(grouped, pairs):
            nc.scalar.copy(
                grouped.bitcast(U32).rearrange("p (c i u) -> p c u i", i=2, u=2),
                pairs[:].rearrange("p u c e -> p (u c e)").bitcast(U32).rearrange("p (u c i) -> p c u i", i=2, u=2),
            )

        def quantize_z(b, u, codes):
            scales = own([P, BANK], U8, "z_sc%d_%d" % (b, u))
            quantize(z_bf[b, u][:], codes[:], scales[:])
            z_q[b, u] = (codes, scales)

        def round_w3(first, last, kib, left=0):
            grouped = place([P, PASSES, last - first, PACK], BF16, "w3_bf%d" % first, kib)
            rows = w3_raw[:, :, :, first : last - left].rearrange("p b j c -> p b c j")
            nc.gpsimd.tensor_scalar(grouped[:, :, 0 : last - left - first, :], rows, 1.0, 0.0, ALU.mult, ALU.add)
            return grouped

        def quantize_w3(grouped, operands, kib):
            name = "%d_%d" % operands[0]
            codes = place([P, P * len(operands)], U32, "w3_codes" + name, kib)
            scales = own([P, P * len(operands)], U8, "w3_sc" + name)
            quantize(grouped, codes[:], scales[:])
            for k, operand in enumerate(operands):
                w3_q[operand] = (codes[:, P * k : P * (k + 1)], scales[:, P * k : P * (k + 1)])

        def quantize_wide(b, kib):
            quantize_w3(w3_wide[:, b, :, :].rearrange("p c j -> p (c j)"), [(b, n) for n in range(3)], kib)

        w3_q = {}
        speech_bank = [[banks[k] for k in (0, 1, 2, 3)], [banks[k] for k in (4, 5, 6, 3)]]
        carry_bank = [[banks[k] for k in (RING, 1, 2, 0)]] * 2

        def speech_pass(u, b, n):
            codes, scales = z_q[b, u]
            nc.tensor.matmul_mx(
                out=speech_bank[u][n][:],
                lhsT=w2_codes[:, b, 2 * P * n : 2 * P * (n + 1)].bitcast(FP4X4),
                lhsT_scale=w2_sc[:, b, P * n : P * (n + 1)],
                rhs=codes[:].bitcast(FP8X4),
                rhs_scale=scales[:],
                start=(b == 0),
                stop=(b == PASSES - 1),
            )

        def carry_pass(u, b, n):
            codes, scales = z_q[b, u]
            w_codes, w_scales = w3_q[b, n]
            nc.tensor.matmul_mx(
                out=carry_bank[u][n][:],
                lhsT=w_codes.bitcast(FP8X4),
                lhsT_scale=w_scales,
                rhs=codes[:].bitcast(FP8X4),
                rhs_scale=scales[:],
                start=(b == 0),
                stop=(b == PASSES - 1),
            )

        def both_passes(one_pass, u, n):
            for b in range(PASSES):
                one_pass(u, b, n)

        def dampen(dst, u, n, first=0, last=BANK):
            silence = sil_all[:, n, BANK * u + first : BANK * u + last]
            nc.vector.scalar_tensor_tensor(dst, silence, 1.0, speech_bank[u][n][:, first:last], ALU.subtract, ALU.mult)

        w3_wide = round_w3(0, 3 * P, 50, LEFT)
        for u in range(2):
            sigmoid(0, u)
            grouped_tile(0, u)
            gate(0, u)
        quantize_z(0, 0, place([P, BANK], U32, "z_codes0_0", 64))
        quantize_z(0, 1, own([P, BANK], U32, "z_codes0_1"))
        for n in range(4):
            speech_pass(0, 0, n)
        for n in range(3):
            speech_pass(1, 0, n)
        w3_last = round_w3(3 * P, N, 0)
        sigmoid(1, 0)
        grouped_tile(1, 0)
        gate(1, 0, GATED)
        few_pairs = gate_on_scalar(lambda t: sig[1, 0][:, t, GATED:BANK], BANK - GATED, "few_pairs", 60)
        planes = [place([P, 2, BANK], F32, "sig1_1_%d" % e, 16 + 4 * e) for e in range(2)]
        nc.scalar.activation(planes[0][:], x[1][:, 0:PACK:2, BANK:E], ACT.Sigmoid)
        join(z_bf[1, 0][:, PACK * GATED : PACK * BANK], few_pairs)
        nc.scalar.copy(
            w3_wide[:, :, 3 * P - LEFT : 3 * P, :].rearrange("p b (c i) j -> p b c j i", i=4),
            w3_raw[:, :, :, 3 * P - LEFT : 3 * P].rearrange("p b j (c i) -> p b c j i", i=4),
        )
        nc.scalar.activation(planes[1][:], x[1][:, 1:PACK:2, BANK:E], ACT.Sigmoid)
        quantize_wide(0, 32)
        carry_pass(0, 0, 0)
        quantize_z(1, 0, own([P, BANK], U32, "z_codes1_0"))
        for n in (1, 2, 0):
            speech_pass(0, 1, n)
        quantize_wide(1, 24)
        carry_pass(0, 1, 0)
        speech_pass(0, 1, 3)
        quantize_w3(w3_last[:].rearrange("p b c j -> p (b c j)"), [(b, 3) for b in range(PASSES)], 26)

        pairs = gate_on_scalar(lambda t: planes[t % 2][:, t // 2, :], BANK, "pairs", 56)
        grouped_tile(1, 1)
        join(z_bf[1, 1][:], pairs)

        damped = [place([P, BANK], F32, "damped%d" % n, kib) for n, kib in enumerate((66, 68, 70, 56))]
        result = place([P, N // P, BANK], F32, "result", 72)

        def second_half(n, first=0, last=BANK):
            return sil_all[:, n, BANK + first : BANK + last]

        def sum_on_gpsimd(u, n, source, kib, last=BANK):
            carry = place([P, last], F32, "carry%d_%d" % (u, n), kib)
            nc.scalar.copy(carry[:], carry_bank[u][n][:, 0:last])
            part = result[:, 2 * u + n, 0:last]
            nc.gpsimd.tensor_tensor(part, carry[:], source, ALU.subtract)
            nc.sync.dma_start(out[P * n : P * (n + 1), BANK * u : BANK * u + last], part)

        def sum_on_vector(u, n, part, first=0, last=BANK):
            nc.vector.scalar_tensor_tensor(part, part, -1.0, carry_bank[u][n][:, first:last], ALU.mult, ALU.add)
            queue = nc.sync if (u, n) == (0, 3) else nc.scalar
            queue.dma_start(out[P * n : P * (n + 1), BANK * u + first : BANK * u + last], part)

        for n in (1, 2):
            dampen(damped[n][:], 0, n)
            both_passes(carry_pass, 0, n)
        dampen(damped[0][:], 0, 0)
        quantize_z(1, 1, own([P, BANK], U32, "z_codes1_1"))
        for n in range(2):
            sum_on_gpsimd(0, n, damped[n][:], 20 + 2 * n)
        dampen(damped[3][:], 0, 3)
        speech_pass(1, 1, 0)
        both_passes(carry_pass, 1, 0)
        both_passes(carry_pass, 0, 3)
        sum_on_vector(0, 2, damped[2][:])
        dampen(second_half(0), 1, 0)
        sum_on_vector(0, 3, damped[3][:])
        for n in (2, 1):
            speech_pass(1, 1, n)
        both_passes(carry_pass, 1, 1)
        both_passes(carry_pass, 1, 2)
        both_passes(speech_pass, 1, 3)
        both_passes(carry_pass, 1, 3)
        for n in (2, 1):
            dampen(second_half(n), 1, n)
        sum_on_gpsimd(1, 0, second_half(0), 80)
        sum_on_gpsimd(1, 1, second_half(1, 0, SHARE), 82, SHARE)
        sum_on_vector(1, 2, second_half(2))
        halves = ((0, BANK // 2), (BANK // 2, BANK))
        dampen(second_half(3), 1, 3)
        sum_on_vector(1, 1, second_half(1, SHARE, BANK), SHARE, BANK)
        for first, last in halves:
            sum_on_vector(1, 3, second_half(3, first, last), first, last)
